import numpy as np
import ml_dtypes


def mxq(x, axis, fmt="e4m3"):
    dtype, down = {"e4m3": (ml_dtypes.float8_e4m3fn, 7), "e5m2": (ml_dtypes.float8_e5m2, 14)}[fmt]
    v = np.moveaxis(np.asarray(x, np.float32).astype(ml_dtypes.bfloat16).astype(np.float64), axis, -1)
    blocks = v.reshape(v.shape[:-1] + (-1, 32))
    amax = np.abs(blocks).max(-1, keepdims=True)
    byte = np.maximum(np.where(amax > 0, np.frexp(amax)[1] - 1 + 127, 0) - down, 1)
    scale = np.exp2(byte - 127.0)
    codes = (blocks / scale).astype(np.float32).astype(dtype).astype(np.float64)
    return np.moveaxis((codes * scale).reshape(v.shape), -1, axis)


WIDE = False


def mx_kscale(k):
    if not WIDE:
        return np.ones(k)
    levels = np.array([24, -24, 12, -12, 0])
    if k % 512:
        return np.exp2(np.random.permutation(np.resize(levels, k // 32))).repeat(32)
    a = np.empty((k // 512, 16))
    for p in range(k // 512):
        a[p, :8] = np.random.permutation(np.resize(levels, 8))
        for g in range(8):
            far = levels[np.abs(levels - a[p, g]) >= 10]
            a[p, g + 8] = far[np.random.randint(len(far))]
    return np.exp2(a.ravel()).repeat(32)


def f64(x):
    return np.asarray(x).astype(np.float64)


def striped(idx):
    return np.tile(idx.reshape(-1, 16).T, (8, 1)).astype(np.uint16)


def unstriped(offs):
    return offs[:16].T.reshape(-1).astype(np.int64)


E2M1 = np.array([0.0, 0.5, 1.0, 1.5, 2.0, 3.0, 4.0, 6.0, -0.0, -0.5, -1.0, -1.5, -2.0, -3.0, -4.0, -6.0])


def pack_weight(w, fmt):
    k, n = w.shape
    w = f64(np.asarray(w, np.float32).astype(ml_dtypes.bfloat16)).reshape(k // 32, 32, n)
    amax = np.abs(w).max(1)
    if fmt == "e4m3":
        byte = np.frexp(amax)[1] - 1 + 127 - 7
    else:
        mant, ex = np.frexp(amax / 6.0)
        byte = np.where(mant > 0.5, ex, ex - 1) + 127
    byte = np.clip(np.where(amax > 0, byte, 1), 1, 254)
    scaled = (w * np.exp2(127.0 - byte)[:, None, :]).reshape(k, n).astype(np.float32)
    by_word = np.ascontiguousarray(scaled.reshape(k // 512, 128, 4, n).transpose(0, 1, 3, 2))
    if fmt == "e4m3":
        words = by_word.astype(ml_dtypes.float8_e4m3fn).view(np.uint8)
    else:
        c = by_word.astype(ml_dtypes.float4_e2m1fn).view(np.uint8) & 0xF
        words = (c[..., 0::2] | (c[..., 1::2] << 4)).reshape(k // 512, 128, 2 * n)
    return np.ascontiguousarray(words), np.ascontiguousarray(byte.astype(np.uint8).reshape(k // 512, 16, n))


def unpack_weight(words, scales, fmt):
    g, _, n = scales.shape
    words = np.ascontiguousarray(words).reshape(g, 128, n, -1)
    if fmt == "e4m3":
        vals = words.view(ml_dtypes.float8_e4m3fn).astype(np.float64)
    else:
        nib = np.empty((g, 128, n, 4), np.uint8)
        nib[..., 0::2] = words & 0xF
        nib[..., 1::2] = words >> 4
        vals = E2M1[nib]
    vals = vals * np.repeat(np.exp2(scales.astype(np.float64) - 127.0), 8, axis=1)[..., None]
    return vals.transpose(0, 1, 3, 2).reshape(g * 512, n)


def pack_table4(v):
    words, scales = pack_weight(v, "e2m1")
    g, t = words.shape[0] // 2, v.shape[1]
    return np.ascontiguousarray(words.reshape(g, 2, 128, t, 2).transpose(0, 2, 3, 1, 4).reshape(g, 128, t, 4)), scales


def unpack_table4(words, scales):
    g, _, t, _ = words.shape
    return unpack_weight(words.reshape(g, 128, t, 2, 2).transpose(0, 3, 1, 2, 4).reshape(2 * g, 128, 2 * t), scales, "e2m1")


def gelu(f):
    return 0.5 * f * (1.0 + np.tanh(np.sqrt(2.0 / np.pi) * (f + 0.044715 * f**3)))


K, L, N, T, J = 1024, 1024, 512, 4096, 1024


def setup_inputs():
    n = np.random.standard_normal
    s = mx_kscale(K)[:, None]
    s2 = mx_kscale(L)[:, None]
    p_tab = pack_table4(n((K, T)) * s)
    p_wx = pack_weight(n((L, N)) / np.sqrt(L) / s2, "e2m1")
    return {
        "tab_words": p_tab[0],
        "tab_scales": p_tab[1],
        "wt": (n((K, N)) / np.sqrt(K) / s).astype(np.float32),
        "x": (n((L, J)) * s2).astype(np.float32),
        "wx_words": p_wx[0],
        "wx_scales": p_wx[1],
        "b": (0.3 * n(N)).astype(np.float32),
        "offs": striped(np.random.permutation(T)[:J]),
    }


def reference(tab_words, tab_scales, wt, x, wx_words, wx_scales, b, offs):
    idx = unstriped(offs)
    tab_ = unpack_table4(tab_words, tab_scales)[:, idx]
    wt_q_ = mxq(f64(wt), 0, "e4m3")
    wt_r_ = mxq(f64(wt) - wt_q_, 0, "e4m3")
    x_ = mxq(f64(x), 0, "e4m3")
    wx_ = unpack_weight(wx_words, wx_scales, "e2m1")
    y = wt_q_.T @ tab_ + wt_r_.T @ tab_ + wx_.T @ x_
    return gelu(y + f64(b)[:, None])

@@ -1,0 +1,249 @@
+from contextlib import ExitStack
+
+import concourse.mybir as mybir
+
+K, L, N, T, J = 1024, 1024, 512, 4096, 1024
+FLOPS = 2 * N * J * (2 * K + L) + 2 * 512 * K * N
+
+F32 = mybir.dt.float32
+BF16 = mybir.dt.bfloat16
+I32 = mybir.dt.int32
+U32 = mybir.dt.uint32
+U16 = mybir.dt.uint16
+U8 = mybir.dt.uint8
+FP8X4 = mybir.dt.float8_e4m3fn_x4
+FP4X4 = mybir.dt.float4_e2m1fn_x4
+ACT = mybir.ActivationFunctionType
+ALU = mybir.AluOpType
+
+P = 128
+PACK = 4
+K_PASS = P * PACK
+HALF = 512
+PIECE = 256
+CLEAR_SPLIT = 2048
+
+
+def tile_list_tiert_gelu_kernel(
+    tc, tab_words, tab_scales, wt, x, wx_words, wx_scales, b, offs, out
+):
+    nc = tc.nc
+    with ExitStack() as ctx:
+        lists = ctx.enter_context(tc.tile_pool(name="lists", bufs=1))
+        keep = ctx.enter_context(tc.tile_pool(name="keep", bufs=1))
+        psum = ctx.enter_context(tc.psum_pool(name="psum", bufs=1))
+
+        def sb(shape, dtype, name, tag=None):
+            return keep.tile(shape, dtype, name=name, tag=tag or name, align_bytes=64)
+
+        def bank(index, shape, name):
+            return psum.tile(shape, F32, name=name, tag="bank%d" % index)
+
+        def walk_out(ap):
+            return ap.rearrange("p (c i) t -> p c t i", i=4)
+
+        def walk_in(ap):
+            return ap.rearrange("p t (c i) -> p c t i", i=4)
+
+        def round_and_weave(engine, woven, rows):
+            if engine == "scalar":
+                nc.scalar.activation(out=walk_out(woven[:]), in_=walk_in(rows), func=ACT.Copy)
+            else:
+                nc.vector.tensor_copy(out=walk_out(woven[:]), in_=walk_in(rows))
+
+        def quantize(codes, scales, woven):
+            nc.vector.quantize_mx(
+                out=codes.bitcast(FP8X4), scales=scales, in_=woven[:].rearrange("p c t -> p (c t)")
+            )
+
+        scale_window = sb([P, T], U8, "scale_window")
+        nc.gpsimd.memset(scale_window[:, :CLEAR_SPLIT].bitcast(I32), 0)
+        nc.vector.memset(scale_window[:, CLEAR_SPLIT:].bitcast(I32), 0)
+        eye_woven = sb([P, PACK, P, PACK], BF16, "eye_woven")
+        eye_flat = eye_woven[:].rearrange("p t m i -> p (t m i)")
+        nc.vector.memset(eye_flat, 0.0)
+        nc.gpsimd.affine_select(
+            out=eye_flat,
+            in_=eye_flat,
+            compare_op=ALU.not_equal,
+            fill=1.0,
+            base=0,
+            pattern=[[-1, PACK], [1, K_PASS]],
+            channel_multiplier=-PACK,
+        )
+        tab_plane1 = sb([P, J], U8, "tab_plane1")
+        nc.vector.memset(tab_plane1[:].bitcast(I32), 0)
+        wx_plane = sb([P, 2, N], U8, "wx_plane")
+        nc.gpsimd.memset(wx_plane[:].rearrange("p a n -> p (a n)").bitcast(I32), 0)
+
+        offsets = lists.tile([P, J // 16], U16, name="offsets")
+        nc.sync.dma_start(offsets[:], offs)
+        for r in range(4):
+            nc.sync.dma_start(
+                out=scale_window[r:P:16, :].bitcast(I32),
+                in_=tab_scales.rearrange("a (q r) t -> r q a t", r=4)[r].bitcast(I32),
+            )
+        wt_rows = [sb([P, PACK, N], F32, "wt_rows%d" % a) for a in range(2)]
+        x_rows = {}
+        word_window = sb([P, T], I32, "word_window")
+        x_room = {(0, 0): "x_first", (0, 1): "wt_rows0", (1, 0): "word_window", (1, 1): "wt_rows1"}
+        wx_codes = sb([P, 2, 2 * N], U8, "wx_codes")
+        bias = sb([P, N // P], F32, "bias")
+
+        def load_wt(a):
+            nc.sync.dma_start(
+                out=wt_rows[a][:], in_=wt[K_PASS * a : K_PASS * (a + 1), :].rearrange("(p t) n -> p t n", t=PACK)
+            )
+
+        def load_x(h, a):
+            x_rows[(h, a)] = sb([P, PACK, HALF], F32, "x_rows%d%d" % (h, a), x_room[(h, a)])
+            nc.sync.dma_start(
+                out=x_rows[(h, a)][:],
+                in_=x[K_PASS * a : K_PASS * (a + 1), HALF * h : HALF * (h + 1)].rearrange("(p t) j -> p t j", t=PACK),
+            )
+
+        load_wt(0)
+        nc.sync.dma_start(out=word_window[:], in_=tab_words[0].rearrange("p t b -> p (t b)").bitcast(I32))
+        for q in range(4):
+            nc.gpsimd.dma_start(
+                out=wx_plane[32 * q : 32 * q + 4, :, :].bitcast(I32),
+                in_=wx_scales[:, 4 * q : 4 * q + 4, :].rearrange("a r n -> r a n").bitcast(I32),
+            )
+        load_wt(1)
+        nc.sync.dma_start(out=wx_codes[:].bitcast(I32), in_=wx_words.rearrange("a p b -> p a b").bitcast(I32))
+        load_x(0, 0)
+        with nc.allow_non_contiguous_dma(reason="one bias value to a partition"):
+            nc.sync.dma_start(out=bias[:], in_=b.rearrange("(m p) -> p m", p=P))
+
+        eye_codes = sb([P, K_PASS], U32, "eye_codes")
+        eye_plane = sb([P, K_PASS], U8, "eye_plane")
+        nc.vector.quantize_mx(out=eye_codes[:].bitcast(FP8X4), scales=eye_plane[:], in_=eye_flat)
+
+        q_codes = [sb([P, N], U32, "q_codes%d" % a) for a in range(2)]
+        q_plane = [sb([P, N], U8, "q_plane%d" % a) for a in range(2)]
+        r_codes = [sb([P, N], U32, "r_codes%d" % a) for a in range(2)]
+        r_plane = [sb([P, N], U8, "r_plane%d" % a) for a in range(2)]
+
+        def first_tier(a, engines):
+            for u in range(2):
+                cols = slice(PIECE * u, PIECE * (u + 1))
+                woven = sb([P, PIECE, PACK], BF16, "q_woven%d%d" % (a, u))
+                round_and_weave(engines[u], woven, wt_rows[a][:, :, cols])
+                quantize(q_codes[a][:, cols], q_plane[a][:, cols], woven)
+
+        def second_tier(a, banks):
+            for u in range(2):
+                woven = sb([P, PIECE, PACK], BF16, "r_woven%d%d" % (a, u))
+                for v in range(2):
+                    m = 2 * u + v
+                    cols = slice(P * m, P * (m + 1))
+                    back = bank(banks[m], [P, PACK, P], "back%d%d" % (a, m))
+                    for t in range(PACK):
+                        nc.tensor.matmul_mx(
+                            out=back[:, t, :],
+                            lhsT=eye_codes[:, P * t : P * (t + 1)].bitcast(FP8X4),
+                            lhsT_scale=eye_plane[:, P * t : P * (t + 1)],
+                            rhs=q_codes[a][:, cols].bitcast(FP8X4),
+                            rhs_scale=q_plane[a][:, cols],
+                            start=True,
+                            stop=True,
+                        )
+                    nc.vector.tensor_tensor(
+                        out=walk_out(woven[:, P * v : P * (v + 1), :]),
+                        in0=walk_in(wt_rows[a][:, :, cols]),
+                        in1=walk_in(back[:]),
+                        op=ALU.subtract,
+                    )
+                cols = slice(PIECE * u, PIECE * (u + 1))
+                quantize(r_codes[a][:, cols], r_plane[a][:, cols], woven)
+
+        first_tier(0, ("vector", "scalar"))
+
+        tab_plane0 = sb([P, J], U8, "tab_plane0")
+        nc.vector.tensor_copy(out=tab_plane0[:], in_=scale_window[:].indirect(offsets[:]))
+        nc.gpsimd.dma_start(out=tab_plane1[0:112, :].bitcast(I32), in_=tab_plane0[16:128, :].bitcast(I32))
+        tab_plane = [tab_plane0, tab_plane1]
+
+        second_tier(0, (4, 5, 6, 7))
+        load_x(0, 1)
+
+        tab_codes = []
+        for h in range(2):
+            picked = sb([P, HALF], U32, "picked%d" % h)
+            nc.vector.tensor_copy(
+                out=picked[:],
+                in_=word_window[:].bitcast(U32).indirect(offsets[:, HALF // 16 * h : HALF // 16 * (h + 1)]),
+            )
+            parted = sb([P, 2, 2 * HALF], U8, "parted%d" % h)
+            nc.vector.tensor_copy(
+                out=parted[:].bitcast(U16), in_=picked[:].bitcast(U16).rearrange("p (j d) -> p d j", d=2)
+            )
+            tab_codes.append(parted)
+
+        load_x(1, 0)
+        acc = {}
+
+        def table_pass(h, m, a, codes, plane):
+            first = (h, m) not in acc
+            if first:
+                acc[(h, m)] = bank(4 * h + m, [P, HALF], "acc%d%d" % (h, m))
+            cols = slice(P * m, P * (m + 1))
+            nc.tensor.matmul_mx(
+                out=acc[(h, m)][:],
+                lhsT=codes[a][:, cols].bitcast(FP8X4),
+                lhsT_scale=plane[a][:, cols],
+                rhs=tab_codes[h][:, a, :].bitcast(FP4X4),
+                rhs_scale=tab_plane[a][:, HALF * h : HALF * (h + 1)],
+                start=first,
+                stop=False,
+            )
+
+        for codes, plane in ((q_codes, q_plane), (r_codes, r_plane)):
+            for m in range(4):
+                table_pass(0, m, 0, codes, plane)
+        for codes, plane in ((q_codes, q_plane), (r_codes, r_plane)):
+            for m in range(2):
+                table_pass(1, m, 0, codes, plane)
+
+        first_tier(1, ("scalar", "scalar"))
+        second_tier(1, (6, 7, 6, 7))
+        load_x(1, 1)
+
+        for m in range(4):
+            table_pass(0, m, 1, q_codes, q_plane)
+        for m in range(2):
+            table_pass(1, m, 1, q_codes, q_plane)
+        for m in range(2, 4):
+            table_pass(1, m, 0, q_codes, q_plane)
+            table_pass(1, m, 0, r_codes, r_plane)
+            table_pass(1, m, 1, q_codes, q_plane)
+
+        weavers = {(0, 0): ("scalar", "scalar"), (0, 1): ("scalar", "vector"),
+                   (1, 0): ("vector", "scalar"), (1, 1): ("vector", "vector")}
+        for h in range(2):
+            for m in range(4):
+                table_pass(h, m, 1, r_codes, r_plane)
+            x_codes = [sb([P, HALF], U32, "x_codes%d%d" % (h, a)) for a in range(2)]
+            x_plane = [sb([P, HALF], U8, "x_plane%d%d" % (h, a)) for a in range(2)]
+            for a in range(2):
+                for u in range(2):
+                    cols = slice(PIECE * u, PIECE * (u + 1))
+                    woven = sb([P, PIECE, PACK], BF16, "x_woven%d%d%d" % (h, a, u))
+                    round_and_weave(weavers[(h, a)][u], woven, x_rows[(h, a)][:, :, cols])
+                    quantize(x_codes[a][:, cols], x_plane[a][:, cols], woven)
+            for m in range(4):
+                for a in range(2):
+                    nc.tensor.matmul_mx(
+                        out=acc[(h, m)][:],
+                        lhsT=wx_codes[:, a, 2 * P * m : 2 * P * (m + 1)].bitcast(FP4X4),
+                        lhsT_scale=wx_plane[:, a, P * m : P * (m + 1)],
+                        rhs=x_codes[a][:].bitcast(FP8X4),
+                        rhs_scale=x_plane[a][:],
+                        start=False,
+                        stop=(a == 1),
+                    )
+                result = sb([P, HALF], F32, "result%d%d" % (h, m))
+                nc.scalar.activation(
+                    out=result[:], in_=acc[(h, m)][:], func=ACT.Gelu_apprx_tanh, bias=bias[:, m : m + 1]
+                )
+                nc.sync.dma_start(out=out[P * m : P * (m + 1), HALF * h : HALF * (h + 1)], in_=result[:])

@@ -1,6 +1,7 @@
 from contextlib import ExitStack
 
 import concourse.mybir as mybir
+from concourse.masks import make_identity
 
 K, L, N, T, J = 1024, 1024, 512, 4096, 1024
 FLOPS = 2 * N * J * (2 * K + L) + 2 * 512 * K * N
@@ -21,7 +22,7 @@ PACK = 4
 K_PASS = P * PACK
 HALF = 512
 PIECE = 256
-CLEAR_SPLIT = 2048
+SCALE_ROW0 = 96
 
 
 def tile_list_tiert_gelu_kernel(
@@ -47,203 +48,267 @@ def tile_list_tiert_gelu_kernel(
 
         def round_and_weave(engine, woven, rows):
             if engine == "scalar":
-                nc.scalar.activation(out=walk_out(woven[:]), in_=walk_in(rows), func=ACT.Copy)
+                nc.scalar.activation(out=walk_out(woven), in_=walk_in(rows), func=ACT.Copy)
             else:
-                nc.vector.tensor_copy(out=walk_out(woven[:]), in_=walk_in(rows))
+                nc.vector.tensor_copy(out=walk_out(woven), in_=walk_in(rows))
 
         def quantize(codes, scales, woven):
-            nc.vector.quantize_mx(
-                out=codes.bitcast(FP8X4), scales=scales, in_=woven[:].rearrange("p c t -> p (c t)")
-            )
+            nc.vector.quantize_mx(out=codes.bitcast(FP8X4), scales=scales, in_=woven.rearrange("p c t -> p (c t)"))
 
-        scale_window = sb([P, T], U8, "scale_window")
-        nc.gpsimd.memset(scale_window[:, :CLEAR_SPLIT].bitcast(I32), 0)
-        nc.vector.memset(scale_window[:, CLEAR_SPLIT:].bitcast(I32), 0)
-        eye_woven = sb([P, PACK, P, PACK], BF16, "eye_woven")
-        eye_flat = eye_woven[:].rearrange("p t m i -> p (t m i)")
-        nc.vector.memset(eye_flat, 0.0)
-        nc.gpsimd.affine_select(
-            out=eye_flat,
-            in_=eye_flat,
-            compare_op=ALU.not_equal,
-            fill=1.0,
-            base=0,
-            pattern=[[-1, PACK], [1, K_PASS]],
-            channel_multiplier=-PACK,
-        )
-        tab_plane1 = sb([P, J], U8, "tab_plane1")
-        nc.vector.memset(tab_plane1[:].bitcast(I32), 0)
-        wx_plane = sb([P, 2, N], U8, "wx_plane")
-        nc.gpsimd.memset(wx_plane[:].rearrange("p a n -> p (a n)").bitcast(I32), 0)
+        def piece(u):
+            return slice(PIECE * u, PIECE * (u + 1))
 
         offsets = lists.tile([P, J // 16], U16, name="offsets")
-        nc.sync.dma_start(offsets[:], offs)
-        for r in range(4):
+        wt_by_pass = wt.rearrange("(a p t) n -> a p t n", p=P, t=PACK)
+
+        warm_in = sb([P, 1], F32, "warm_in")
+        warm_out = sb([P, 1], F32, "warm_out")
+        nc.gpsimd.memset(warm_in[:], 0.0)
+        nc.scalar.activation(out=warm_out[:], in_=warm_in[:], func=ACT.Gelu_apprx_tanh)
+
+        with tc.tile_pool(name="scales", bufs=1, side="right") as scales:
+            scale_window = scales.tile([P, T], U8, name="scale_window")
+            nc.sync.dma_start(offsets[:], offs)
             nc.sync.dma_start(
-                out=scale_window[r:P:16, :].bitcast(I32),
-                in_=tab_scales.rearrange("a (q r) t -> r q a t", r=4)[r].bitcast(I32),
+                out=scale_window[SCALE_ROW0:P, :].bitcast(I32), in_=tab_scales.rearrange("a q t -> (a q) t").bitcast(I32)
             )
-        wt_rows = [sb([P, PACK, N], F32, "wt_rows%d" % a) for a in range(2)]
+            word_window = sb([P, T], I32, "word_window", "room0")
+            nc.sync.dma_start(out=word_window[:], in_=tab_words[0].rearrange("p t b -> p (t b)").bitcast(I32))
+            wt_head = sb([P, PACK, PIECE], F32, "wt_head", "room8")
+            nc.sync.dma_start(out=wt_head[:], in_=wt_by_pass[0][:, :, piece(0)])
+
+            nc.gpsimd.memset(scale_window[0:SCALE_ROW0, :].bitcast(I32), 0)
+            eye = sb([P, P], BF16, "eye")
+            make_identity(nc, eye[:])
+
+            eye_woven = sb([P, PACK * (K_PASS + 8)], BF16, "eye_woven", "room10")
+            nc.vector.memset(eye_woven[:].bitcast(I32), 0)
+            tab_plane = [sb([P, J], U8, "tab_plane%d" % a) for a in range(2)]
+            for a in range(2):
+                nc.vector.memset(tab_plane[a][:].bitcast(I32), 0)
+            nc.vector.tensor_copy(
+                out=eye_woven[:, : PACK * (K_PASS + 1)].rearrange("p (t c) -> p t c", t=PACK)[:, :, 0:K_PASS:PACK],
+                in_=eye[:].rearrange("p (o m) -> p o m", o=1).to_broadcast([P, PACK, P]),
+            )
+            eye_codes = sb([P, K_PASS], U32, "eye_codes")
+            eye_plane = sb([P, K_PASS], U8, "eye_plane")
+            nc.vector.quantize_mx(
+                out=eye_codes[:].bitcast(FP8X4), scales=eye_plane[:], in_=eye_woven[:, : PACK * K_PASS]
+            )
+            picked_scales = sb([P, J], U8, "picked_scales", "room10")
+            nc.vector.tensor_copy(out=picked_scales[:], in_=scale_window[:].indirect(offsets[:]))
+
+        tokens = ctx.enter_context(tc.tile_pool(name="tokens", bufs=1, side="right"))
+
+        def late(shape, dtype, name, tag=None):
+            return tokens.tile(shape, dtype, name=name, tag=tag or name, align_bytes=64)
+
+        def spread_scales(a):
+            for q in range(4):
+                row = SCALE_ROW0 + 16 * a + 4 * q
+                nc.sync.dma_start(
+                    out=tab_plane[a][32 * q : 32 * q + 4, :].bitcast(I32), in_=picked_scales[row : row + 4, :].bitcast(I32)
+                )
+
+        wx_plane = late([P, 2, N], U8, "wx_plane")
+        nc.gpsimd.memset(wx_plane[:].rearrange("p a n -> p (a n)").bitcast(I32), 0)
+
+        spread_scales(0)
+        wt_tail = late([P, PACK, PIECE], F32, "wt_tail", "room9")
+        nc.sync.dma_start(out=wt_tail[:], in_=wt_by_pass[0][:, :, piece(1)])
+        wt_second = late([P, PACK, N], F32, "wt_second")
+        nc.sync.dma_start(out=wt_second[:], in_=wt_by_pass[1])
+        wt_rows = [[wt_head[:], wt_tail[:]], [wt_second[:, :, piece(u)] for u in range(2)]]
+
         x_rows = {}
-        word_window = sb([P, T], I32, "word_window")
-        x_room = {(0, 0): "x_first", (0, 1): "wt_rows0", (1, 0): "word_window", (1, 1): "wt_rows1"}
-        wx_codes = sb([P, 2, 2 * N], U8, "wx_codes")
-        bias = sb([P, N // P], F32, "bias")
 
-        def load_wt(a):
-            nc.sync.dma_start(
-                out=wt_rows[a][:], in_=wt[K_PASS * a : K_PASS * (a + 1), :].rearrange("(p t) n -> p t n", t=PACK)
-            )
-
-        def load_x(h, a):
-            x_rows[(h, a)] = sb([P, PACK, HALF], F32, "x_rows%d%d" % (h, a), x_room[(h, a)])
+        def load_x(h, a, pool, tag=None):
+            x_rows[(h, a)] = pool([P, PACK, HALF], F32, "x_rows%d%d" % (h, a), tag)
             nc.sync.dma_start(
                 out=x_rows[(h, a)][:],
                 in_=x[K_PASS * a : K_PASS * (a + 1), HALF * h : HALF * (h + 1)].rearrange("(p t) j -> p t j", t=PACK),
             )
 
-        load_wt(0)
-        nc.sync.dma_start(out=word_window[:], in_=tab_words[0].rearrange("p t b -> p (t b)").bitcast(I32))
+        load_x(0, 0, late)
+        spread_scales(1)
+        wx_codes = late([P, 2, 2 * N], U8, "wx_codes")
+        nc.sync.dma_start(out=wx_codes[:].bitcast(I32), in_=wx_words.rearrange("a p b -> p a b").bitcast(I32))
+        bias = late([P, N // P], F32, "bias")
+        with nc.allow_non_contiguous_dma(reason="one bias value to a partition"):
+            nc.sync.dma_start(out=bias[:], in_=b.rearrange("(m p) -> p m", p=P))
+        load_x(0, 1, late)
         for q in range(4):
-            nc.gpsimd.dma_start(
+            nc.sync.dma_start(
                 out=wx_plane[32 * q : 32 * q + 4, :, :].bitcast(I32),
                 in_=wx_scales[:, 4 * q : 4 * q + 4, :].rearrange("a r n -> r a n").bitcast(I32),
             )
-        load_wt(1)
-        nc.sync.dma_start(out=wx_codes[:].bitcast(I32), in_=wx_words.rearrange("a p b -> p a b").bitcast(I32))
-        load_x(0, 0)
-        with nc.allow_non_contiguous_dma(reason="one bias value to a partition"):
-            nc.sync.dma_start(out=bias[:], in_=b.rearrange("(m p) -> p m", p=P))
 
-        eye_codes = sb([P, K_PASS], U32, "eye_codes")
-        eye_plane = sb([P, K_PASS], U8, "eye_plane")
-        nc.vector.quantize_mx(out=eye_codes[:].bitcast(FP8X4), scales=eye_plane[:], in_=eye_flat)
+        q_codes = {}
+        r_codes = {}
+        q_plane = [late([P, N], U8, "q_plane%d" % a) for a in range(2)]
+        r_plane = [late([P, N], U8, "r_plane%d" % a) for a in range(2)]
 
-        q_codes = [sb([P, N], U32, "q_codes%d" % a) for a in range(2)]
-        q_plane = [sb([P, N], U8, "q_plane%d" % a) for a in range(2)]
-        r_codes = [sb([P, N], U32, "r_codes%d" % a) for a in range(2)]
-        r_plane = [sb([P, N], U8, "r_plane%d" % a) for a in range(2)]
+        def stationary(codes, plane, a, m):
+            within = slice(P * (m % 2), P * (m % 2 + 1))
+            return codes[(a, m // 2)][:, within].bitcast(FP8X4), plane[a][:, P * m : P * (m + 1)]
 
-        def first_tier(a, engines):
-            for u in range(2):
-                cols = slice(PIECE * u, PIECE * (u + 1))
-                woven = sb([P, PIECE, PACK], BF16, "q_woven%d%d" % (a, u))
-                round_and_weave(engines[u], woven, wt_rows[a][:, :, cols])
-                quantize(q_codes[a][:, cols], q_plane[a][:, cols], woven)
+        def left_over(a, m, woven):
+            within = slice(P * (m % 2), P * (m % 2 + 1))
+            back = bank(6 + m % 2, [P, PACK, P], "back%d%d" % (a, m))
+            codes, scales = stationary(q_codes, q_plane, a, m)
+            for t in range(PACK):
+                nc.tensor.matmul_mx(
+                    out=back[:, t, :],
+                    lhsT=eye_codes[:, P * t : P * (t + 1)].bitcast(FP8X4),
+                    lhsT_scale=eye_plane[:, P * t : P * (t + 1)],
+                    rhs=codes,
+                    rhs_scale=scales,
+                    start=True,
+                    stop=True,
+                )
+            nc.vector.tensor_tensor(
+                out=walk_out(woven[:, within, :]),
+                in0=walk_in(wt_rows[a][m // 2][:, :, within]),
+                in1=walk_in(back[:]),
+                op=ALU.subtract,
+            )
 
-        def second_tier(a, banks):
-            for u in range(2):
-                woven = sb([P, PIECE, PACK], BF16, "r_woven%d%d" % (a, u))
-                for v in range(2):
-                    m = 2 * u + v
-                    cols = slice(P * m, P * (m + 1))
-                    back = bank(banks[m], [P, PACK, P], "back%d%d" % (a, m))
-                    for t in range(PACK):
-                        nc.tensor.matmul_mx(
-                            out=back[:, t, :],
-                            lhsT=eye_codes[:, P * t : P * (t + 1)].bitcast(FP8X4),
-                            lhsT_scale=eye_plane[:, P * t : P * (t + 1)],
-                            rhs=q_codes[a][:, cols].bitcast(FP8X4),
-                            rhs_scale=q_plane[a][:, cols],
-                            start=True,
-                            stop=True,
-                        )
-                    nc.vector.tensor_tensor(
-                        out=walk_out(woven[:, P * v : P * (v + 1), :]),
-                        in0=walk_in(wt_rows[a][:, :, cols]),
-                        in1=walk_in(back[:]),
-                        op=ALU.subtract,
-                    )
-                cols = slice(PIECE * u, PIECE * (u + 1))
-                quantize(r_codes[a][:, cols], r_plane[a][:, cols], woven)
+        def second_tier(a, u, woven):
+            r_codes[(a, u)] = sb([P, PIECE], U32, "r_codes%d%d" % (a, u))[:]
+            quantize(r_codes[(a, u)], r_plane[a][:, piece(u)], woven[:])
 
-        first_tier(0, ("vector", "scalar"))
+        tab_codes = {}
+        picked = {}
 
-        tab_plane0 = sb([P, J], U8, "tab_plane0")
-        nc.vector.tensor_copy(out=tab_plane0[:], in_=scale_window[:].indirect(offsets[:]))
-        nc.gpsimd.dma_start(out=tab_plane1[0:112, :].bitcast(I32), in_=tab_plane0[16:128, :].bitcast(I32))
-        tab_plane = [tab_plane0, tab_plane1]
-
-        second_tier(0, (4, 5, 6, 7))
-        load_x(0, 1)
-
-        tab_codes = []
-        for h in range(2):
-            picked = sb([P, HALF], U32, "picked%d" % h)
+        def pick_words(h, tag):
+            picked[h] = sb([P, HALF], U32, "picked%d" % h, tag)
             nc.vector.tensor_copy(
-                out=picked[:],
+                out=picked[h][:],
                 in_=word_window[:].bitcast(U32).indirect(offsets[:, HALF // 16 * h : HALF // 16 * (h + 1)]),
             )
-            parted = sb([P, 2, 2 * HALF], U8, "parted%d" % h)
-            nc.vector.tensor_copy(
-                out=parted[:].bitcast(U16), in_=picked[:].bitcast(U16).rearrange("p (j d) -> p d j", d=2)
-            )
-            tab_codes.append(parted)
 
-        load_x(1, 0)
+        def part_words(h):
+            tab_codes[h] = sb([P, 2, 2 * HALF], U8, "parted%d" % h)
+            nc.vector.tensor_copy(
+                out=tab_codes[h][:].bitcast(U16), in_=picked[h][:].bitcast(U16).rearrange("p (j d) -> p d j", d=2)
+            )
+
         acc = {}
 
         def table_pass(h, m, a, codes, plane):
             first = (h, m) not in acc
             if first:
                 acc[(h, m)] = bank(4 * h + m, [P, HALF], "acc%d%d" % (h, m))
-            cols = slice(P * m, P * (m + 1))
+            weights, scales = stationary(codes, plane, a, m)
             nc.tensor.matmul_mx(
                 out=acc[(h, m)][:],
-                lhsT=codes[a][:, cols].bitcast(FP8X4),
-                lhsT_scale=plane[a][:, cols],
+                lhsT=weights,
+                lhsT_scale=scales,
                 rhs=tab_codes[h][:, a, :].bitcast(FP4X4),
                 rhs_scale=tab_plane[a][:, HALF * h : HALF * (h + 1)],
                 start=first,
                 stop=False,
             )
 
-        for codes, plane in ((q_codes, q_plane), (r_codes, r_plane)):
-            for m in range(4):
-                table_pass(0, m, 0, codes, plane)
-        for codes, plane in ((q_codes, q_plane), (r_codes, r_plane)):
-            for m in range(2):
-                table_pass(1, m, 0, codes, plane)
+        head_woven = [sb([P, P, PACK], BF16, "head_woven%d" % m, "room%d" % (5 + m)) for m in range(2)]
+        for m in range(2):
+            round_and_weave("scalar", head_woven[m][:], wt_head[:, :, P * m : P * (m + 1)])
+        tail_woven = sb([P, PIECE, PACK], BF16, "tail_woven", "room7")
+        round_and_weave("scalar", tail_woven[:], wt_tail[:])
 
-        first_tier(1, ("scalar", "scalar"))
-        second_tier(1, (6, 7, 6, 7))
-        load_x(1, 1)
+        pick_words(0, "room1")
+        part_words(0)
+        q_codes[(0, 0)] = sb([P, PIECE], U32, "q_codes00", "room1")[:]
+        quantize(q_codes[(0, 0)][:, :P], q_plane[0][:, :P], head_woven[0][:])
+        pick_words(1, "room5")
+        quantize(q_codes[(0, 0)][:, P:], q_plane[0][:, P:PIECE], head_woven[1][:])
+        q_codes[(0, 1)] = sb([P, PIECE], U32, "q_codes01", "room0")[:]
+        quantize(q_codes[(0, 1)], q_plane[0][:, piece(1)], tail_woven[:])
+        load_x(1, 0, sb, "room7")
+        part_words(1)
+        r_woven = [sb([P, PIECE, PACK], BF16, "r_woven00"), sb([P, PIECE, PACK], BF16, "r_woven01")]
+        for m in range(2):
+            left_over(0, m, r_woven[0])
+        load_x(1, 1, sb, "room8")
+        left_over(0, 2, r_woven[1])
+        second_tier(0, 0, r_woven[0])
+        left_over(0, 3, r_woven[1])
 
+        q_woven = sb([P, N, PACK], BF16, "q_woven1", "room2")
+        for u in range(2):
+            round_and_weave("scalar", q_woven[:, piece(u), :], wt_rows[1][u])
+        q_second = late([P, N], U32, "q_codes1", "room9")
+        quantize(q_second[:], q_plane[1][:], q_woven[:])
+        second_tier(0, 1, r_woven[1])
+        for u in range(2):
+            q_codes[(1, u)] = q_second[:, piece(u)]
+
+        x_codes = {}
+        x_plane = {}
+
+        def quantize_x(h, a, engines, woven_tags, codes_tag):
+            x_codes[(h, a)] = sb([P, HALF], U32, "x_codes%d%d" % (h, a), codes_tag)
+            x_plane[(h, a)] = sb([P, HALF], U8, "x_plane%d%d" % (h, a))
+            width = HALF // len(woven_tags)
+            woven = [
+                sb([P, width, PACK], BF16, "x_woven%d%d%d" % (h, a, i), tag) for i, tag in enumerate(woven_tags)
+            ]
+            for u in range(2):
+                first = PIECE * u % width
+                round_and_weave(
+                    engines[u], woven[PIECE * u // width][:, first : first + PIECE, :], x_rows[(h, a)][:, :, piece(u)]
+                )
+            for i, tile in enumerate(woven):
+                cols = slice(width * i, width * (i + 1))
+                quantize(x_codes[(h, a)][:, cols], x_plane[(h, a)][:, cols], tile[:])
+
+        def token_pass(h, m, a):
+            nc.tensor.matmul_mx(
+                out=acc[(h, m)][:],
+                lhsT=wx_codes[:, a, 2 * P * m : 2 * P * (m + 1)].bitcast(FP4X4),
+                lhsT_scale=wx_plane[:, a, P * m : P * (m + 1)],
+                rhs=x_codes[(h, a)][:].bitcast(FP8X4),
+                rhs_scale=x_plane[(h, a)][:],
+                start=False,
+                stop=(a == 1),
+            )
+
+        def finish(h, m):
+            result = results[h][:, m, :]
+            nc.scalar.activation(out=result, in_=acc[(h, m)][:], func=ACT.Gelu_apprx_tanh, bias=bias[:, m : m + 1])
+            nc.sync.dma_start(out=out[P * m : P * (m + 1), HALF * h : HALF * (h + 1)], in_=result)
+
+        quantize_x(0, 0, ("scalar", "scalar"), ("x_woven_a",), "room2")
+        r_woven = [sb([P, PIECE, PACK], BF16, "r_woven1%d" % u, "room%d" % (3 + u)) for u in range(2)]
+        for m in range(3):
+            left_over(1, m, r_woven[m // 2])
+        second_tier(1, 0, r_woven[0])
+        left_over(1, 3, r_woven[1])
+        quantize_x(0, 1, ("scalar", "scalar"), ("x_woven_b",), "room3")
+        second_tier(1, 1, r_woven[1])
+        quantize_x(1, 0, ("scalar", "scalar"), ("x_woven_a",), "room4")
+        quantize_x(1, 1, ("vector", "vector"), ("x_woven_a",), None)
+        results = [sb([P, N // P, HALF], F32, "results0", "room7"), sb([P, N // P, HALF], F32, "results1")]
+
+        for u in range(2):
+            for codes, plane in ((q_codes, q_plane), (r_codes, r_plane)):
+                for m in range(2 * u, 2 * u + 2):
+                    table_pass(0, m, 0, codes, plane)
         for m in range(4):
             table_pass(0, m, 1, q_codes, q_plane)
-        for m in range(2):
-            table_pass(1, m, 1, q_codes, q_plane)
-        for m in range(2, 4):
+        for m in range(4):
+            token_pass(0, m, 0)
+        for m in range(4):
+            table_pass(0, m, 1, r_codes, r_plane)
+            token_pass(0, m, 1)
+            finish(0, m)
+
+        for m in range(4):
             table_pass(1, m, 0, q_codes, q_plane)
             table_pass(1, m, 0, r_codes, r_plane)
             table_pass(1, m, 1, q_codes, q_plane)
-
-        weavers = {(0, 0): ("scalar", "scalar"), (0, 1): ("scalar", "vector"),
-                   (1, 0): ("vector", "scalar"), (1, 1): ("vector", "vector")}
-        for h in range(2):
-            for m in range(4):
-                table_pass(h, m, 1, r_codes, r_plane)
-            x_codes = [sb([P, HALF], U32, "x_codes%d%d" % (h, a)) for a in range(2)]
-            x_plane = [sb([P, HALF], U8, "x_plane%d%d" % (h, a)) for a in range(2)]
-            for a in range(2):
-                for u in range(2):
-                    cols = slice(PIECE * u, PIECE * (u + 1))
-                    woven = sb([P, PIECE, PACK], BF16, "x_woven%d%d%d" % (h, a, u))
-                    round_and_weave(weavers[(h, a)][u], woven, x_rows[(h, a)][:, :, cols])
-                    quantize(x_codes[a][:, cols], x_plane[a][:, cols], woven)
-            for m in range(4):
-                for a in range(2):
-                    nc.tensor.matmul_mx(
-                        out=acc[(h, m)][:],
-                        lhsT=wx_codes[:, a, 2 * P * m : 2 * P * (m + 1)].bitcast(FP4X4),
-                        lhsT_scale=wx_plane[:, a, P * m : P * (m + 1)],
-                        rhs=x_codes[a][:].bitcast(FP8X4),
-                        rhs_scale=x_plane[a][:],
-                        start=False,
-                        stop=(a == 1),
-                    )
-                result = sb([P, HALF], F32, "result%d%d" % (h, m))
-                nc.scalar.activation(
-                    out=result[:], in_=acc[(h, m)][:], func=ACT.Gelu_apprx_tanh, bias=bias[:, m : m + 1]
-                )
-                nc.sync.dma_start(out=out[P * m : P * (m + 1), HALF * h : HALF * (h + 1)], in_=result[:])
+        for m in range(4):
+            table_pass(1, m, 1, r_codes, r_plane)
+            token_pass(1, m, 0)
+            token_pass(1, m, 1)
+            finish(1, m)

@@ -4,7 +4,6 @@ import concourse.mybir as mybir
 from concourse.masks import make_identity
 
 K, L, N, T, J = 1024, 1024, 512, 4096, 1024
-FLOPS = 2 * N * J * (2 * K + L) + 2 * 512 * K * N
 
 F32 = mybir.dt.float32
 BF16 = mybir.dt.bfloat16
@@ -20,9 +19,17 @@ ALU = mybir.AluOpType
 P = 128
 PACK = 4
 K_PASS = P * PACK
+PASSES = K // K_PASS
+TILES = N // P
 HALF = 512
 PIECE = 256
-SCALE_ROW0 = 96
+QUADRANTS = 4
+GROUP = 16
+SCALE_ROW0 = P - PASSES * GROUP
+BACK_BANK = 6
+SUM_BANKS = 7
+
+FLOPS = 2 * N * J * (2 * K + L) + 2 * K_PASS * K * N
 
 
 def tile_list_tiert_gelu_kernel(
@@ -40,25 +47,25 @@ def tile_list_tiert_gelu_kernel(
         def bank(index, shape, name):
             return psum.tile(shape, F32, name=name, tag="bank%d" % index)
 
-        def walk_out(ap):
+        def walk_woven(ap):
             return ap.rearrange("p (c i) t -> p c t i", i=4)
 
-        def walk_in(ap):
+        def walk_rows(ap):
             return ap.rearrange("p t (c i) -> p c t i", i=4)
 
         def round_and_weave(engine, woven, rows):
             if engine == "scalar":
-                nc.scalar.activation(out=walk_out(woven), in_=walk_in(rows), func=ACT.Copy)
+                nc.scalar.activation(out=walk_woven(woven), in_=walk_rows(rows), func=ACT.Copy)
             else:
-                nc.vector.tensor_copy(out=walk_out(woven), in_=walk_in(rows))
+                nc.vector.tensor_copy(out=walk_woven(woven), in_=walk_rows(rows))
 
-        def quantize(codes, scales, woven):
-            nc.vector.quantize_mx(out=codes.bitcast(FP8X4), scales=scales, in_=woven.rearrange("p c t -> p (c t)"))
+        def quantize(codes, plane, woven):
+            nc.vector.quantize_mx(out=codes.bitcast(FP8X4), scales=plane, in_=woven.rearrange("p c t -> p (c t)"))
 
         def piece(u):
             return slice(PIECE * u, PIECE * (u + 1))
 
-        offsets = lists.tile([P, J // 16], U16, name="offsets")
+        offsets = lists.tile([P, J // GROUP], U16, name="offsets")
         wt_by_pass = wt.rearrange("(a p t) n -> a p t n", p=P, t=PACK)
 
         warm_in = sb([P, 1], F32, "warm_in")
@@ -72,20 +79,22 @@ def tile_list_tiert_gelu_kernel(
             nc.sync.dma_start(
                 out=scale_window[SCALE_ROW0:P, :].bitcast(I32), in_=tab_scales.rearrange("a q t -> (a q) t").bitcast(I32)
             )
-            word_window = sb([P, T], I32, "word_window", "room0")
+            word_window = sb([P, T], I32, "word_window", "words_then_q_tail")
             nc.sync.dma_start(out=word_window[:], in_=tab_words[0].rearrange("p t b -> p (t b)").bitcast(I32))
-            wt_head = sb([P, PACK, PIECE], F32, "wt_head", "room8")
+            wt_head = sb([P, PACK, PIECE], F32, "wt_head", "wt_head_then_x11")
             nc.sync.dma_start(out=wt_head[:], in_=wt_by_pass[0][:, :, piece(0)])
 
             nc.gpsimd.memset(scale_window[0:SCALE_ROW0, :].bitcast(I32), 0)
             eye = sb([P, P], BF16, "eye")
             make_identity(nc, eye[:])
 
-            eye_woven = sb([P, PACK * (K_PASS + 8)], BF16, "eye_woven", "room10")
+            eye_woven = sb([P, PACK * (K_PASS + 8)], BF16, "eye_woven", "eye_then_picked0_then_q_head")
             nc.vector.memset(eye_woven[:].bitcast(I32), 0)
-            tab_plane = [sb([P, J], U8, "tab_plane%d" % a) for a in range(2)]
-            for a in range(2):
+            tab_plane = [sb([P, J], U8, "tab_plane%d" % a) for a in range(PASSES)]
+            for a in range(PASSES):
                 nc.vector.memset(tab_plane[a][:].bitcast(I32), 0)
+            picked_scales = sb([P, J], U8, "picked_scales")
+            nc.vector.tensor_copy(out=picked_scales[:], in_=scale_window[:].indirect(offsets[:]))
             nc.vector.tensor_copy(
                 out=eye_woven[:, : PACK * (K_PASS + 1)].rearrange("p (t c) -> p t c", t=PACK)[:, :, 0:K_PASS:PACK],
                 in_=eye[:].rearrange("p (o m) -> p o m", o=1).to_broadcast([P, PACK, P]),
@@ -95,26 +104,24 @@ def tile_list_tiert_gelu_kernel(
             nc.vector.quantize_mx(
                 out=eye_codes[:].bitcast(FP8X4), scales=eye_plane[:], in_=eye_woven[:, : PACK * K_PASS]
             )
-            picked_scales = sb([P, J], U8, "picked_scales", "room10")
-            nc.vector.tensor_copy(out=picked_scales[:], in_=scale_window[:].indirect(offsets[:]))
 
-        tokens = ctx.enter_context(tc.tile_pool(name="tokens", bufs=1, side="right"))
+        after_gather = ctx.enter_context(tc.tile_pool(name="after_gather", bufs=1, side="right"))
 
         def late(shape, dtype, name, tag=None):
-            return tokens.tile(shape, dtype, name=name, tag=tag or name, align_bytes=64)
+            return after_gather.tile(shape, dtype, name=name, tag=tag or name, align_bytes=64)
 
         def spread_scales(a):
-            for q in range(4):
-                row = SCALE_ROW0 + 16 * a + 4 * q
+            for q in range(QUADRANTS):
+                row = SCALE_ROW0 + GROUP * a + 4 * q
                 nc.sync.dma_start(
                     out=tab_plane[a][32 * q : 32 * q + 4, :].bitcast(I32), in_=picked_scales[row : row + 4, :].bitcast(I32)
                 )
 
-        wx_plane = late([P, 2, N], U8, "wx_plane")
+        wx_plane = late([P, PASSES, N], U8, "wx_plane")
         nc.gpsimd.memset(wx_plane[:].rearrange("p a n -> p (a n)").bitcast(I32), 0)
 
         spread_scales(0)
-        wt_tail = late([P, PACK, PIECE], F32, "wt_tail", "room9")
+        wt_tail = late([P, PACK, PIECE], F32, "wt_tail", "wt_tail_then_q_second")
         nc.sync.dma_start(out=wt_tail[:], in_=wt_by_pass[0][:, :, piece(1)])
         wt_second = late([P, PACK, N], F32, "wt_second")
         nc.sync.dma_start(out=wt_second[:], in_=wt_by_pass[1])
@@ -122,8 +129,8 @@ def tile_list_tiert_gelu_kernel(
 
         x_rows = {}
 
-        def load_x(h, a, pool, tag=None):
-            x_rows[(h, a)] = pool([P, PACK, HALF], F32, "x_rows%d%d" % (h, a), tag)
+        def load_x(h, a, make_tile, tag=None):
+            x_rows[(h, a)] = make_tile([P, PACK, HALF], F32, "x_rows%d%d" % (h, a), tag)
             nc.sync.dma_start(
                 out=x_rows[(h, a)][:],
                 in_=x[K_PASS * a : K_PASS * (a + 1), HALF * h : HALF * (h + 1)].rearrange("(p t) j -> p t j", t=PACK),
@@ -131,13 +138,13 @@ def tile_list_tiert_gelu_kernel(
 
         load_x(0, 0, late)
         spread_scales(1)
-        wx_codes = late([P, 2, 2 * N], U8, "wx_codes")
+        wx_codes = late([P, PASSES, 2 * N], U8, "wx_codes")
         nc.sync.dma_start(out=wx_codes[:].bitcast(I32), in_=wx_words.rearrange("a p b -> p a b").bitcast(I32))
-        bias = late([P, N // P], F32, "bias")
+        bias = late([P, TILES], F32, "bias")
         with nc.allow_non_contiguous_dma(reason="one bias value to a partition"):
             nc.sync.dma_start(out=bias[:], in_=b.rearrange("(m p) -> p m", p=P))
         load_x(0, 1, late)
-        for q in range(4):
+        for q in range(QUADRANTS):
             nc.sync.dma_start(
                 out=wx_plane[32 * q : 32 * q + 4, :, :].bitcast(I32),
                 in_=wx_scales[:, 4 * q : 4 * q + 4, :].rearrange("a r n -> r a n").bitcast(I32),
@@ -145,31 +152,32 @@ def tile_list_tiert_gelu_kernel(
 
         q_codes = {}
         r_codes = {}
-        q_plane = [late([P, N], U8, "q_plane%d" % a) for a in range(2)]
-        r_plane = [late([P, N], U8, "r_plane%d" % a) for a in range(2)]
+        q_plane = [late([P, N], U8, "q_plane%d" % a) for a in range(PASSES)]
+        r_plane = [late([P, N], U8, "r_plane%d" % a) for a in range(PASSES)]
 
-        def stationary(codes, plane, a, m):
-            within = slice(P * (m % 2), P * (m % 2 + 1))
-            return codes[(a, m // 2)][:, within].bitcast(FP8X4), plane[a][:, P * m : P * (m + 1)]
+        def within_piece(m):
+            return slice(P * (m % 2), P * (m % 2 + 1))
+
+        def tier_tile(codes, plane, a, m):
+            return codes[(a, m // 2)][:, within_piece(m)].bitcast(FP8X4), plane[a][:, P * m : P * (m + 1)]
 
         def left_over(a, m, woven):
-            within = slice(P * (m % 2), P * (m % 2 + 1))
-            back = bank(6 + m % 2, [P, PACK, P], "back%d%d" % (a, m))
-            codes, scales = stationary(q_codes, q_plane, a, m)
+            back = bank(BACK_BANK + m % 2, [P, PACK, P], "back%d%d" % (a, m))
+            codes, plane = tier_tile(q_codes, q_plane, a, m)
             for t in range(PACK):
                 nc.tensor.matmul_mx(
                     out=back[:, t, :],
                     lhsT=eye_codes[:, P * t : P * (t + 1)].bitcast(FP8X4),
                     lhsT_scale=eye_plane[:, P * t : P * (t + 1)],
                     rhs=codes,
-                    rhs_scale=scales,
+                    rhs_scale=plane,
                     start=True,
                     stop=True,
                 )
             nc.vector.tensor_tensor(
-                out=walk_out(woven[:, within, :]),
-                in0=walk_in(wt_rows[a][m // 2][:, :, within]),
-                in1=walk_in(back[:]),
+                out=walk_woven(woven[:, within_piece(m), :]),
+                in0=walk_rows(wt_rows[a][m // 2][:, :, within_piece(m)]),
+                in1=walk_rows(back[:]),
                 op=ALU.subtract,
             )
 
@@ -177,68 +185,56 @@ def tile_list_tiert_gelu_kernel(
             r_codes[(a, u)] = sb([P, PIECE], U32, "r_codes%d%d" % (a, u))[:]
             quantize(r_codes[(a, u)], r_plane[a][:, piece(u)], woven[:])
 
+        picked_words = {}
         tab_codes = {}
-        picked = {}
 
         def pick_words(h, tag):
-            picked[h] = sb([P, HALF], U32, "picked%d" % h, tag)
+            columns = HALF // GROUP
+            picked_words[h] = sb([P, HALF], U32, "picked_words%d" % h, tag)
             nc.vector.tensor_copy(
-                out=picked[h][:],
-                in_=word_window[:].bitcast(U32).indirect(offsets[:, HALF // 16 * h : HALF // 16 * (h + 1)]),
+                out=picked_words[h][:],
+                in_=word_window[:].bitcast(U32).indirect(offsets[:, columns * h : columns * (h + 1)]),
             )
 
         def part_words(h):
-            tab_codes[h] = sb([P, 2, 2 * HALF], U8, "parted%d" % h)
+            tab_codes[h] = sb([P, PASSES, 2 * HALF], U8, "tab_codes%d" % h)
             nc.vector.tensor_copy(
-                out=tab_codes[h][:].bitcast(U16), in_=picked[h][:].bitcast(U16).rearrange("p (j d) -> p d j", d=2)
+                out=tab_codes[h][:].bitcast(U16),
+                in_=picked_words[h][:].bitcast(U16).rearrange("p (j a) -> p a j", a=PASSES),
             )
 
-        acc = {}
-
-        def table_pass(h, m, a, codes, plane):
-            first = (h, m) not in acc
-            if first:
-                acc[(h, m)] = bank(4 * h + m, [P, HALF], "acc%d%d" % (h, m))
-            weights, scales = stationary(codes, plane, a, m)
-            nc.tensor.matmul_mx(
-                out=acc[(h, m)][:],
-                lhsT=weights,
-                lhsT_scale=scales,
-                rhs=tab_codes[h][:, a, :].bitcast(FP4X4),
-                rhs_scale=tab_plane[a][:, HALF * h : HALF * (h + 1)],
-                start=first,
-                stop=False,
-            )
-
-        head_woven = [sb([P, P, PACK], BF16, "head_woven%d" % m, "room%d" % (5 + m)) for m in range(2)]
+        head_woven = [
+            sb([P, P, PACK], BF16, "head_woven0", "head_woven0_then_picked1"),
+            sb([P, P, PACK], BF16, "head_woven1"),
+        ]
         for m in range(2):
-            round_and_weave("scalar", head_woven[m][:], wt_head[:, :, P * m : P * (m + 1)])
-        tail_woven = sb([P, PIECE, PACK], BF16, "tail_woven", "room7")
+            round_and_weave("scalar", head_woven[m][:], wt_head[:, :, within_piece(m)])
+        tail_woven = sb([P, PIECE, PACK], BF16, "tail_woven", "tail_woven_then_x10_then_results0")
         round_and_weave("scalar", tail_woven[:], wt_tail[:])
 
-        pick_words(0, "room1")
+        pick_words(0, "eye_then_picked0_then_q_head")
         part_words(0)
-        q_codes[(0, 0)] = sb([P, PIECE], U32, "q_codes00", "room1")[:]
+        q_codes[(0, 0)] = sb([P, PIECE], U32, "q_head", "eye_then_picked0_then_q_head")[:]
         quantize(q_codes[(0, 0)][:, :P], q_plane[0][:, :P], head_woven[0][:])
-        pick_words(1, "room5")
+        pick_words(1, "head_woven0_then_picked1")
         quantize(q_codes[(0, 0)][:, P:], q_plane[0][:, P:PIECE], head_woven[1][:])
-        q_codes[(0, 1)] = sb([P, PIECE], U32, "q_codes01", "room0")[:]
+        q_codes[(0, 1)] = sb([P, PIECE], U32, "q_tail", "words_then_q_tail")[:]
         quantize(q_codes[(0, 1)], q_plane[0][:, piece(1)], tail_woven[:])
-        load_x(1, 0, sb, "room7")
+        load_x(1, 0, sb, "tail_woven_then_x10_then_results0")
         part_words(1)
-        r_woven = [sb([P, PIECE, PACK], BF16, "r_woven00"), sb([P, PIECE, PACK], BF16, "r_woven01")]
+        r_woven = [sb([P, PIECE, PACK], BF16, "r_woven0%d" % u) for u in range(2)]
         for m in range(2):
             left_over(0, m, r_woven[0])
-        load_x(1, 1, sb, "room8")
+        load_x(1, 1, sb, "wt_head_then_x11")
         left_over(0, 2, r_woven[1])
         second_tier(0, 0, r_woven[0])
         left_over(0, 3, r_woven[1])
 
-        q_woven = sb([P, N, PACK], BF16, "q_woven1", "room2")
+        second_woven = sb([P, N, PACK], BF16, "second_woven", "second_woven_then_x_codes00")
         for u in range(2):
-            round_and_weave("scalar", q_woven[:, piece(u), :], wt_rows[1][u])
-        q_second = late([P, N], U32, "q_codes1", "room9")
-        quantize(q_second[:], q_plane[1][:], q_woven[:])
+            round_and_weave("scalar", second_woven[:, piece(u), :], wt_rows[1][u])
+        q_second = late([P, N], U32, "q_second", "wt_tail_then_q_second")
+        quantize(q_second[:], q_plane[1][:], second_woven[:])
         second_tier(0, 1, r_woven[1])
         for u in range(2):
             q_codes[(1, u)] = q_second[:, piece(u)]
@@ -246,21 +242,48 @@ def tile_list_tiert_gelu_kernel(
         x_codes = {}
         x_plane = {}
 
-        def quantize_x(h, a, engines, woven_tags, codes_tag):
+        def quantize_x(h, a, engine, woven_tag, codes_tag):
             x_codes[(h, a)] = sb([P, HALF], U32, "x_codes%d%d" % (h, a), codes_tag)
             x_plane[(h, a)] = sb([P, HALF], U8, "x_plane%d%d" % (h, a))
-            width = HALF // len(woven_tags)
-            woven = [
-                sb([P, width, PACK], BF16, "x_woven%d%d%d" % (h, a, i), tag) for i, tag in enumerate(woven_tags)
-            ]
+            woven = sb([P, HALF, PACK], BF16, "x_woven%d%d" % (h, a), woven_tag)
             for u in range(2):
-                first = PIECE * u % width
-                round_and_weave(
-                    engines[u], woven[PIECE * u // width][:, first : first + PIECE, :], x_rows[(h, a)][:, :, piece(u)]
-                )
-            for i, tile in enumerate(woven):
-                cols = slice(width * i, width * (i + 1))
-                quantize(x_codes[(h, a)][:, cols], x_plane[(h, a)][:, cols], tile[:])
+                round_and_weave(engine, woven[:, piece(u), :], x_rows[(h, a)][:, :, piece(u)])
+            quantize(x_codes[(h, a)][:], x_plane[(h, a)][:], woven[:])
+
+        quantize_x(0, 0, "scalar", "x_woven_ring", "second_woven_then_x_codes00")
+        r_woven = [
+            sb([P, PIECE, PACK], BF16, "r_woven10", "r_woven10_then_x_codes01"),
+            sb([P, PIECE, PACK], BF16, "r_woven11", "r_woven11_then_x_codes10"),
+        ]
+        for m in range(3):
+            left_over(1, m, r_woven[m // 2])
+        second_tier(1, 0, r_woven[0])
+        left_over(1, 3, r_woven[1])
+        quantize_x(0, 1, "scalar", None, "r_woven10_then_x_codes01")
+        second_tier(1, 1, r_woven[1])
+        quantize_x(1, 0, "scalar", "x_woven_ring", "r_woven11_then_x_codes10")
+        quantize_x(1, 1, "vector", "x_woven_ring", None)
+
+        results = [
+            sb([P, TILES, HALF], F32, "results0", "tail_woven_then_x10_then_results0"),
+            sb([P, TILES, HALF], F32, "results1"),
+        ]
+        acc = {}
+
+        def table_pass(h, m, a, codes, plane):
+            first = (h, m) not in acc
+            if first:
+                acc[(h, m)] = bank((TILES * h + m) % SUM_BANKS, [P, HALF], "acc%d%d" % (h, m))
+            weights, weights_plane = tier_tile(codes, plane, a, m)
+            nc.tensor.matmul_mx(
+                out=acc[(h, m)][:],
+                lhsT=weights,
+                lhsT_scale=weights_plane,
+                rhs=tab_codes[h][:, a, :].bitcast(FP4X4),
+                rhs_scale=tab_plane[a][:, HALF * h : HALF * (h + 1)],
+                start=first,
+                stop=False,
+            )
 
         def token_pass(h, m, a):
             nc.tensor.matmul_mx(
@@ -270,7 +293,7 @@ def tile_list_tiert_gelu_kernel(
                 rhs=x_codes[(h, a)][:].bitcast(FP8X4),
                 rhs_scale=x_plane[(h, a)][:],
                 start=False,
-                stop=(a == 1),
+                stop=(a == PASSES - 1),
             )
 
         def finish(h, m):
@@ -278,36 +301,24 @@ def tile_list_tiert_gelu_kernel(
             nc.scalar.activation(out=result, in_=acc[(h, m)][:], func=ACT.Gelu_apprx_tanh, bias=bias[:, m : m + 1])
             nc.sync.dma_start(out=out[P * m : P * (m + 1), HALF * h : HALF * (h + 1)], in_=result)
 
-        quantize_x(0, 0, ("scalar", "scalar"), ("x_woven_a",), "room2")
-        r_woven = [sb([P, PIECE, PACK], BF16, "r_woven1%d" % u, "room%d" % (3 + u)) for u in range(2)]
-        for m in range(3):
-            left_over(1, m, r_woven[m // 2])
-        second_tier(1, 0, r_woven[0])
-        left_over(1, 3, r_woven[1])
-        quantize_x(0, 1, ("scalar", "scalar"), ("x_woven_b",), "room3")
-        second_tier(1, 1, r_woven[1])
-        quantize_x(1, 0, ("scalar", "scalar"), ("x_woven_a",), "room4")
-        quantize_x(1, 1, ("vector", "vector"), ("x_woven_a",), None)
-        results = [sb([P, N // P, HALF], F32, "results0", "room7"), sb([P, N // P, HALF], F32, "results1")]
-
         for u in range(2):
             for codes, plane in ((q_codes, q_plane), (r_codes, r_plane)):
                 for m in range(2 * u, 2 * u + 2):
                     table_pass(0, m, 0, codes, plane)
-        for m in range(4):
+        for m in range(TILES):
             table_pass(0, m, 1, q_codes, q_plane)
-        for m in range(4):
+        for m in range(TILES):
             token_pass(0, m, 0)
-        for m in range(4):
+        for m in range(TILES):
             table_pass(0, m, 1, r_codes, r_plane)
             token_pass(0, m, 1)
             finish(0, m)
 
-        for m in range(4):
+        for m in range(TILES):
             table_pass(1, m, 0, q_codes, q_plane)
             table_pass(1, m, 0, r_codes, r_plane)
             table_pass(1, m, 1, q_codes, q_plane)
-        for m in range(4):
+        for m in range(TILES):
             table_pass(1, m, 1, r_codes, r_plane)
             token_pass(1, m, 0)
             token_pass(1, m, 1)

@@ -1,7 +1,6 @@
 from contextlib import ExitStack
 
 import concourse.mybir as mybir
-from concourse.masks import make_identity
 
 K, L, N, T, J = 1024, 1024, 512, 4096, 1024
 
@@ -27,7 +26,13 @@ QUADRANTS = 4
 GROUP = 16
 SCALE_ROW0 = P - PASSES * GROUP
 BACK_BANK = 6
-SUM_BANKS = 7
+ROOM = 2 * HALF * PACK
+WINDOW_AT = 2 * ROOM
+FIRST_AT = WINDOW_AT + 4 * T
+SECOND_HALF_AT = FIRST_AT + ROOM // 2
+SUM_BANK = ((0, 1, 2, 3), (4, 5, 6, 3))
+SPARE_AT = SECOND_HALF_AT + 4 * ROOM
+EYE_RUN = K_PASS + 1
 
 FLOPS = 2 * N * J * (2 * K + L) + 2 * K_PASS * K * N
 
@@ -39,10 +44,14 @@ def tile_list_tiert_gelu_kernel(
     with ExitStack() as ctx:
         lists = ctx.enter_context(tc.tile_pool(name="lists", bufs=1))
         keep = ctx.enter_context(tc.tile_pool(name="keep", bufs=1))
+        rooms = ctx.enter_context(tc.tile_pool(name="rooms", bufs=1))
         psum = ctx.enter_context(tc.psum_pool(name="psum", bufs=1))
 
         def sb(shape, dtype, name, tag=None):
             return keep.tile(shape, dtype, name=name, tag=tag or name, align_bytes=64)
+
+        def placed(shape, dtype, name, offset):
+            return rooms.tile(shape, dtype, name=name, align_bytes=64, offset=offset)
 
         def bank(index, shape, name):
             return psum.tile(shape, F32, name=name, tag="bank%d" % index)
@@ -53,11 +62,11 @@ def tile_list_tiert_gelu_kernel(
         def walk_rows(ap):
             return ap.rearrange("p t (c i) -> p c t i", i=4)
 
-        def round_and_weave(engine, woven, rows):
-            if engine == "scalar":
-                nc.scalar.activation(out=walk_woven(woven), in_=walk_rows(rows), func=ACT.Copy)
-            else:
-                nc.vector.tensor_copy(out=walk_woven(woven), in_=walk_rows(rows))
+        def weave_on_scalar(woven, rows):
+            nc.scalar.activation(out=walk_woven(woven), in_=walk_rows(rows), func=ACT.Copy)
+
+        def weave_on_vector(woven, rows):
+            nc.vector.tensor_copy(out=walk_woven(woven), in_=walk_rows(rows))
 
         def quantize(codes, plane, woven):
             nc.vector.quantize_mx(out=codes.bitcast(FP8X4), scales=plane, in_=woven.rearrange("p c t -> p (c t)"))
@@ -65,12 +74,15 @@ def tile_list_tiert_gelu_kernel(
         def piece(u):
             return slice(PIECE * u, PIECE * (u + 1))
 
+        def within_piece(m):
+            return slice(P * (m % 2), P * (m % 2 + 1))
+
         offsets = lists.tile([P, J // GROUP], U16, name="offsets")
         wt_by_pass = wt.rearrange("(a p t) n -> a p t n", p=P, t=PACK)
 
         warm_in = sb([P, 1], F32, "warm_in")
         warm_out = sb([P, 1], F32, "warm_out")
-        nc.gpsimd.memset(warm_in[:], 0.0)
+        nc.vector.memset(warm_in[:], 0.0)
         nc.scalar.activation(out=warm_out[:], in_=warm_in[:], func=ACT.Gelu_apprx_tanh)
 
         with tc.tile_pool(name="scales", bufs=1, side="right") as scales:
@@ -79,31 +91,35 @@ def tile_list_tiert_gelu_kernel(
             nc.sync.dma_start(
                 out=scale_window[SCALE_ROW0:P, :].bitcast(I32), in_=tab_scales.rearrange("a q t -> (a q) t").bitcast(I32)
             )
-            word_window = sb([P, T], I32, "word_window", "words_then_q_tail")
+            wt_first = [placed([P, PACK, PIECE], F32, "wt_first%d" % u, FIRST_AT + 3 * ROOM * u) for u in range(2)]
+            for u in range(2):
+                nc.sync.dma_start(out=wt_first[u][:], in_=wt_by_pass[0][:, :, piece(u)])
+            word_window = placed([P, T], I32, "word_window", WINDOW_AT)
             nc.sync.dma_start(out=word_window[:], in_=tab_words[0].rearrange("p t b -> p (t b)").bitcast(I32))
-            wt_head = sb([P, PACK, PIECE], F32, "wt_head", "wt_head_then_x11")
-            nc.sync.dma_start(out=wt_head[:], in_=wt_by_pass[0][:, :, piece(0)])
 
-            nc.gpsimd.memset(scale_window[0:SCALE_ROW0, :].bitcast(I32), 0)
-            eye = sb([P, P], BF16, "eye")
-            make_identity(nc, eye[:])
+            eye_run = placed([P, EYE_RUN + 3], BF16, "eye_run", ROOM + ROOM // 2 - 512)
+            nc.gpsimd.memset(eye_run[:].bitcast(I32), 0)
+            nc.gpsimd.affine_select(
+                out=eye_run[:],
+                in_=eye_run[:],
+                compare_op=ALU.not_equal,
+                fill=1.0,
+                base=0,
+                pattern=[[-1, EYE_RUN + 3]],
+                channel_multiplier=PACK,
+            )
+            eye_woven = sb([P, PACK * EYE_RUN], BF16, "eye_woven")
+            nc.scalar.copy(
+                out=eye_woven[:].rearrange("p (t c) -> p t c", t=PACK),
+                in_=eye_run[:, :EYE_RUN].rearrange("p (o c) -> p o c", o=1).to_broadcast([P, PACK, EYE_RUN]),
+            )
 
-            eye_woven = sb([P, PACK * (K_PASS + 8)], BF16, "eye_woven", "eye_then_picked0_then_q_head")
-            nc.vector.memset(eye_woven[:].bitcast(I32), 0)
+            nc.vector.memset(scale_window[0:SCALE_ROW0, :].bitcast(I32), 0)
             tab_plane = [sb([P, J], U8, "tab_plane%d" % a) for a in range(PASSES)]
             for a in range(PASSES):
                 nc.vector.memset(tab_plane[a][:].bitcast(I32), 0)
             picked_scales = sb([P, J], U8, "picked_scales")
             nc.vector.tensor_copy(out=picked_scales[:], in_=scale_window[:].indirect(offsets[:]))
-            nc.vector.tensor_copy(
-                out=eye_woven[:, : PACK * (K_PASS + 1)].rearrange("p (t c) -> p t c", t=PACK)[:, :, 0:K_PASS:PACK],
-                in_=eye[:].rearrange("p (o m) -> p o m", o=1).to_broadcast([P, PACK, P]),
-            )
-            eye_codes = sb([P, K_PASS], U32, "eye_codes")
-            eye_plane = sb([P, K_PASS], U8, "eye_plane")
-            nc.vector.quantize_mx(
-                out=eye_codes[:].bitcast(FP8X4), scales=eye_plane[:], in_=eye_woven[:, : PACK * K_PASS]
-            )
 
         after_gather = ctx.enter_context(tc.tile_pool(name="after_gather", bufs=1, side="right"))
 
@@ -117,169 +133,133 @@ def tile_list_tiert_gelu_kernel(
                     out=tab_plane[a][32 * q : 32 * q + 4, :].bitcast(I32), in_=picked_scales[row : row + 4, :].bitcast(I32)
                 )
 
-        wx_plane = late([P, PASSES, N], U8, "wx_plane")
-        nc.gpsimd.memset(wx_plane[:].rearrange("p a n -> p (a n)").bitcast(I32), 0)
-
-        spread_scales(0)
-        wt_tail = late([P, PACK, PIECE], F32, "wt_tail", "wt_tail_then_q_second")
-        nc.sync.dma_start(out=wt_tail[:], in_=wt_by_pass[0][:, :, piece(1)])
-        wt_second = late([P, PACK, N], F32, "wt_second")
-        nc.sync.dma_start(out=wt_second[:], in_=wt_by_pass[1])
-        wt_rows = [[wt_head[:], wt_tail[:]], [wt_second[:, :, piece(u)] for u in range(2)]]
-
         x_rows = {}
 
-        def load_x(h, a, make_tile, tag=None):
-            x_rows[(h, a)] = make_tile([P, PACK, HALF], F32, "x_rows%d%d" % (h, a), tag)
+        def load_x(h, a, make_tile, first=0, width=HALF):
+            rows = make_tile([P, PACK, width], F32, "x_rows%d%d_%d" % (h, a, first))
+            j0 = HALF * h + first
             nc.sync.dma_start(
-                out=x_rows[(h, a)][:],
-                in_=x[K_PASS * a : K_PASS * (a + 1), HALF * h : HALF * (h + 1)].rearrange("(p t) j -> p t j", t=PACK),
+                out=rows[:],
+                in_=x[K_PASS * a : K_PASS * (a + 1), j0 : j0 + width].rearrange("(p t) j -> p t j", t=PACK),
             )
+            for u in range(width // PIECE):
+                x_rows[(h, a, first // PIECE + u)] = rows[:, :, piece(u)]
 
-        load_x(0, 0, late)
-        spread_scales(1)
+        def at_offset(offset):
+            return lambda shape, dtype, name: placed(shape, dtype, name, offset)
+
+        spread_scales(0)
+        wt_second = late([P, PACK, N], F32, "wt_second")
+        nc.sync.dma_start(out=wt_second[:], in_=wt_by_pass[1])
         wx_codes = late([P, PASSES, 2 * N], U8, "wx_codes")
         nc.sync.dma_start(out=wx_codes[:].bitcast(I32), in_=wx_words.rearrange("a p b -> p a b").bitcast(I32))
         bias = late([P, TILES], F32, "bias")
         with nc.allow_non_contiguous_dma(reason="one bias value to a partition"):
             nc.sync.dma_start(out=bias[:], in_=b.rearrange("(m p) -> p m", p=P))
+        spread_scales(1)
+        load_x(0, 0, late)
         load_x(0, 1, late)
-        for q in range(QUADRANTS):
-            nc.sync.dma_start(
-                out=wx_plane[32 * q : 32 * q + 4, :, :].bitcast(I32),
-                in_=wx_scales[:, 4 * q : 4 * q + 4, :].rearrange("a r n -> r a n").bitcast(I32),
+        wt_rows = [[wt_first[u][:] for u in range(2)], [wt_second[:, :, piece(u)] for u in range(2)]]
+
+
+        eye_codes = late([P, K_PASS], U32, "eye_codes")
+        eye_plane = late([P, K_PASS], U8, "eye_plane")
+        nc.vector.quantize_mx(out=eye_codes[:].bitcast(FP8X4), scales=eye_plane[:], in_=eye_woven[:, : PACK * K_PASS])
+
+        codes = {}
+        planes = {}
+        woven = {}
+
+        def quantize_tier(tier, a, u, make_tile):
+            codes[(tier, a, u)] = make_tile([P, PIECE], U32, "%s_codes%d%d" % (tier, a, u))
+            planes[(tier, a, u)] = sb([P, PIECE], U8, "%s_plane%d%d" % (tier, a, u))
+            quantize(codes[(tier, a, u)][:], planes[(tier, a, u)][:], woven[(tier, a, u)][:])
+
+        def round_wt(a, u):
+            woven[("q", a, u)] = placed([P, PIECE, PACK], BF16, "q_woven%d%d" % (a, u), ROOM + ROOM // 2 * u)
+            weave_on_scalar(woven[("q", a, u)][:], wt_rows[a][u])
+
+        def tier_tile(tier, a, m):
+            return (
+                codes[(tier, a, m // 2)][:, within_piece(m)].bitcast(FP8X4),
+                planes[(tier, a, m // 2)][:, within_piece(m)],
             )
 
-        q_codes = {}
-        r_codes = {}
-        q_plane = [late([P, N], U8, "q_plane%d" % a) for a in range(PASSES)]
-        r_plane = [late([P, N], U8, "r_plane%d" % a) for a in range(PASSES)]
+        back = {}
 
-        def within_piece(m):
-            return slice(P * (m % 2), P * (m % 2 + 1))
-
-        def tier_tile(codes, plane, a, m):
-            return codes[(a, m // 2)][:, within_piece(m)].bitcast(FP8X4), plane[a][:, P * m : P * (m + 1)]
-
-        def left_over(a, m, woven):
-            back = bank(BACK_BANK + m % 2, [P, PACK, P], "back%d%d" % (a, m))
-            codes, plane = tier_tile(q_codes, q_plane, a, m)
+        def bring_back(a, m):
+            back[(a, m)] = bank(BACK_BANK + m % 2, [P, PACK, P], "back%d%d" % (a, m))
+            q_codes, q_plane = tier_tile("q", a, m)
             for t in range(PACK):
                 nc.tensor.matmul_mx(
-                    out=back[:, t, :],
+                    out=back[(a, m)][:, t, :],
                     lhsT=eye_codes[:, P * t : P * (t + 1)].bitcast(FP8X4),
                     lhsT_scale=eye_plane[:, P * t : P * (t + 1)],
-                    rhs=codes,
-                    rhs_scale=plane,
+                    rhs=q_codes,
+                    rhs_scale=q_plane,
                     start=True,
                     stop=True,
                 )
+
+        def left_over(a, m):
+            u = m // 2
+            if ("r", a, u) not in woven:
+                woven[("r", a, u)] = sb([P, PIECE, PACK], BF16, "r_woven%d%d" % (a, u), "left_over%d%d" % (a, u))
             nc.vector.tensor_tensor(
-                out=walk_woven(woven[:, within_piece(m), :]),
-                in0=walk_rows(wt_rows[a][m // 2][:, :, within_piece(m)]),
-                in1=walk_rows(back[:]),
+                out=walk_woven(woven[("r", a, u)][:, within_piece(m), :]),
+                in0=walk_rows(wt_rows[a][u][:, :, within_piece(m)]),
+                in1=walk_rows(back[(a, m)][:]),
                 op=ALU.subtract,
             )
-
-        def second_tier(a, u, woven):
-            r_codes[(a, u)] = sb([P, PIECE], U32, "r_codes%d%d" % (a, u))[:]
-            quantize(r_codes[(a, u)], r_plane[a][:, piece(u)], woven[:])
 
         picked_words = {}
         tab_codes = {}
 
-        def pick_words(h, tag):
+        def pick_words(h, tile):
             columns = HALF // GROUP
-            picked_words[h] = sb([P, HALF], U32, "picked_words%d" % h, tag)
+            picked_words[h] = tile
             nc.vector.tensor_copy(
                 out=picked_words[h][:],
                 in_=word_window[:].bitcast(U32).indirect(offsets[:, columns * h : columns * (h + 1)]),
             )
 
-        def part_words(h):
-            tab_codes[h] = sb([P, PASSES, 2 * HALF], U8, "tab_codes%d" % h)
+        def part_words(h, a, make_tile):
+            tab_codes[(h, a)] = make_tile([P, 2 * HALF], U8, "tab_codes%d%d" % (h, a))
             nc.vector.tensor_copy(
-                out=tab_codes[h][:].bitcast(U16),
-                in_=picked_words[h][:].bitcast(U16).rearrange("p (j a) -> p a j", a=PASSES),
+                out=tab_codes[(h, a)][:].bitcast(U16),
+                in_=picked_words[h][:].bitcast(U16).rearrange("p (j a) -> p a j", a=PASSES)[:, a, :],
             )
 
-        head_woven = [
-            sb([P, P, PACK], BF16, "head_woven0", "head_woven0_then_picked1"),
-            sb([P, P, PACK], BF16, "head_woven1"),
-        ]
-        for m in range(2):
-            round_and_weave("scalar", head_woven[m][:], wt_head[:, :, within_piece(m)])
-        tail_woven = sb([P, PIECE, PACK], BF16, "tail_woven", "tail_woven_then_x10_then_results0")
-        round_and_weave("scalar", tail_woven[:], wt_tail[:])
-
-        pick_words(0, "eye_then_picked0_then_q_head")
-        part_words(0)
-        q_codes[(0, 0)] = sb([P, PIECE], U32, "q_head", "eye_then_picked0_then_q_head")[:]
-        quantize(q_codes[(0, 0)][:, :P], q_plane[0][:, :P], head_woven[0][:])
-        pick_words(1, "head_woven0_then_picked1")
-        quantize(q_codes[(0, 0)][:, P:], q_plane[0][:, P:PIECE], head_woven[1][:])
-        q_codes[(0, 1)] = sb([P, PIECE], U32, "q_tail", "words_then_q_tail")[:]
-        quantize(q_codes[(0, 1)], q_plane[0][:, piece(1)], tail_woven[:])
-        load_x(1, 0, sb, "tail_woven_then_x10_then_results0")
-        part_words(1)
-        r_woven = [sb([P, PIECE, PACK], BF16, "r_woven0%d" % u) for u in range(2)]
-        for m in range(2):
-            left_over(0, m, r_woven[0])
-        load_x(1, 1, sb, "wt_head_then_x11")
-        left_over(0, 2, r_woven[1])
-        second_tier(0, 0, r_woven[0])
-        left_over(0, 3, r_woven[1])
-
-        second_woven = sb([P, N, PACK], BF16, "second_woven", "second_woven_then_x_codes00")
-        for u in range(2):
-            round_and_weave("scalar", second_woven[:, piece(u), :], wt_rows[1][u])
-        q_second = late([P, N], U32, "q_second", "wt_tail_then_q_second")
-        quantize(q_second[:], q_plane[1][:], second_woven[:])
-        second_tier(0, 1, r_woven[1])
-        for u in range(2):
-            q_codes[(1, u)] = q_second[:, piece(u)]
-
+        x_woven = {}
         x_codes = {}
         x_plane = {}
 
-        def quantize_x(h, a, engine, woven_tag, codes_tag):
-            x_codes[(h, a)] = sb([P, HALF], U32, "x_codes%d%d" % (h, a), codes_tag)
-            x_plane[(h, a)] = sb([P, HALF], U8, "x_plane%d%d" % (h, a))
-            woven = sb([P, HALF, PACK], BF16, "x_woven%d%d" % (h, a), woven_tag)
+        def round_x(h, a, u, weave):
+            weave(x_woven[(h, a, u)], x_rows[(h, a, u)])
+
+        def quantize_x(h, a, columns, woven_ap, tag=None):
+            if (h, a) not in x_codes:
+                x_codes[(h, a)] = sb([P, HALF], U32, "x_codes%d%d" % (h, a), tag)
+                x_plane[(h, a)] = sb([P, HALF], U8, "x_plane%d%d" % (h, a))
+            quantize(x_codes[(h, a)][:, columns], x_plane[(h, a)][:, columns], woven_ap)
+
+        def woven_half(h, a, tile):
             for u in range(2):
-                round_and_weave(engine, woven[:, piece(u), :], x_rows[(h, a)][:, :, piece(u)])
-            quantize(x_codes[(h, a)][:], x_plane[(h, a)][:], woven[:])
+                x_woven[(h, a, u)] = tile[:, piece(u), :]
+            return tile[:]
 
-        quantize_x(0, 0, "scalar", "x_woven_ring", "second_woven_then_x_codes00")
-        r_woven = [
-            sb([P, PIECE, PACK], BF16, "r_woven10", "r_woven10_then_x_codes01"),
-            sb([P, PIECE, PACK], BF16, "r_woven11", "r_woven11_then_x_codes10"),
-        ]
-        for m in range(3):
-            left_over(1, m, r_woven[m // 2])
-        second_tier(1, 0, r_woven[0])
-        left_over(1, 3, r_woven[1])
-        quantize_x(0, 1, "scalar", None, "r_woven10_then_x_codes01")
-        second_tier(1, 1, r_woven[1])
-        quantize_x(1, 0, "scalar", "x_woven_ring", "r_woven11_then_x_codes10")
-        quantize_x(1, 1, "vector", "x_woven_ring", None)
-
-        results = [
-            sb([P, TILES, HALF], F32, "results0", "tail_woven_then_x10_then_results0"),
-            sb([P, TILES, HALF], F32, "results1"),
-        ]
         acc = {}
 
-        def table_pass(h, m, a, codes, plane):
+        def table_pass(h, m, tier, a):
             first = (h, m) not in acc
             if first:
-                acc[(h, m)] = bank((TILES * h + m) % SUM_BANKS, [P, HALF], "acc%d%d" % (h, m))
-            weights, weights_plane = tier_tile(codes, plane, a, m)
+                acc[(h, m)] = bank(SUM_BANK[h][m], [P, HALF], "acc%d%d" % (h, m))
+            weights, weights_plane = tier_tile(tier, a, m)
             nc.tensor.matmul_mx(
                 out=acc[(h, m)][:],
                 lhsT=weights,
                 lhsT_scale=weights_plane,
-                rhs=tab_codes[h][:, a, :].bitcast(FP4X4),
+                rhs=tab_codes[(h, a)][:].bitcast(FP4X4),
                 rhs_scale=tab_plane[a][:, HALF * h : HALF * (h + 1)],
                 start=first,
                 stop=False,
@@ -297,29 +277,107 @@ def tile_list_tiert_gelu_kernel(
             )
 
         def finish(h, m):
-            result = results[h][:, m, :]
-            nc.scalar.activation(out=result, in_=acc[(h, m)][:], func=ACT.Gelu_apprx_tanh, bias=bias[:, m : m + 1])
-            nc.sync.dma_start(out=out[P * m : P * (m + 1), HALF * h : HALF * (h + 1)], in_=result)
+            name = "result%d%d" % (h, m)
+            result = placed([P, HALF], F32, name, SECOND_HALF_AT + 4 * HALF * m) if h == 0 else sb([P, HALF], F32, name)
+            nc.scalar.activation(out=result[:], in_=acc[(h, m)][:], func=ACT.Gelu_apprx_tanh, bias=bias[:, m : m + 1])
+            nc.sync.dma_start(out=out[P * m : P * (m + 1), HALF * h : HALF * (h + 1)], in_=result[:])
 
         for u in range(2):
-            for codes, plane in ((q_codes, q_plane), (r_codes, r_plane)):
-                for m in range(2 * u, 2 * u + 2):
-                    table_pass(0, m, 0, codes, plane)
+            round_wt(0, u)
+            quantize_tier("q", 0, u, late)
+        wx_plane = late([P, PASSES, N], U8, "wx_plane")
+        nc.vector.memset(wx_plane[:].rearrange("p a n -> p (a n)").bitcast(I32), 0)
+        for q in range(QUADRANTS):
+            nc.sync.dma_start(
+                out=wx_plane[32 * q : 32 * q + 4, :, :].bitcast(I32),
+                in_=wx_scales[:, 4 * q : 4 * q + 4, :].rearrange("a r n -> r a n").bitcast(I32),
+            )
+        for m in range(3):
+            bring_back(0, m)
+            left_over(0, m)
+        bring_back(0, 3)
+        warm_sum = bank(BACK_BANK, [P, HALF], "warm_sum")
+        for w in range(4):
+            nc.tensor.matmul_mx(
+                out=warm_sum[:],
+                lhsT=eye_codes[:, :P].bitcast(FP8X4),
+                lhsT_scale=eye_plane[:, :P],
+                rhs=eye_codes[:].bitcast(FP8X4),
+                rhs_scale=eye_plane[:],
+                start=True,
+                stop=True,
+            )
+        pick_words(0, placed([P, HALF], U32, "picked_words0", FIRST_AT))
+        quantize_tier("r", 0, 0, sb)
+        part_words(0, 0, sb)
+        left_over(0, 3)
+        load_x(1, 0, at_offset(SECOND_HALF_AT))
+        for u in range(2):
+            load_x(1, 1, at_offset(SECOND_HALF_AT + ROOM * (2 + u)), PIECE * u, PIECE)
+
+        quantize_tier("r", 0, 1, sb)
+        pick_words(1, sb([P, HALF], U32, "picked_words1", "left_over01"))
+        for tier in ("q", "r"):
+            for m in range(TILES):
+                table_pass(0, m, tier, 0)
+
+        for u in range(2):
+            round_wt(1, u)
+            quantize_tier("q", 1, u, at_offset(WINDOW_AT + 4 * PIECE * u))
+            if u == 0:
+                part_words(1, 0, at_offset(ROOM + 2 * HALF))
+        for m in range(2):
+            bring_back(1, m)
+            left_over(1, m)
+        part_words(0, 1, at_offset(ROOM + ROOM // 2))
+        for m in range(2):
+            table_pass(1, m, "q", 0)
+        bring_back(1, 2)
+        left_over(1, 2)
+        quantize_tier("r", 1, 0, sb)
+        for m in range(2):
+            table_pass(1, m, "r", 0)
+        bring_back(1, 3)
+        left_over(1, 3)
         for m in range(TILES):
-            table_pass(0, m, 1, q_codes, q_plane)
+            table_pass(0, m, "q", 1)
+        for m in range(2):
+            table_pass(0, m, "r", 1)
+        for tier in ("q", "r"):
+            table_pass(1, 2, tier, 0)
+
+        whole = slice(0, HALF)
+        first_half = [woven_half(0, a, placed([P, HALF, PACK], BF16, "x_woven0%d" % a, (2 * HALF, SPARE_AT)[a])) for a in range(PASSES)]
+        for u in range(2):
+            round_x(0, 0, u, weave_on_scalar)
+        quantize_x(0, 0, whole, first_half[0], "left_over10")
+        quantize_tier("r", 1, 1, sb)
+        for u in range(2):
+            round_x(0, 1, u, weave_on_scalar)
+        quantize_x(0, 1, whole, first_half[1], "left_over11")
+        part_words(1, 1, at_offset(SPARE_AT + ROOM // 2))
+        shared = woven_half(1, 0, late([P, HALF, PACK], BF16, "x_woven10", "wt_second"))
+        round_x(1, 0, 0, weave_on_scalar)
+        round_x(1, 0, 1, weave_on_vector)
+        x_woven[(1, 1, 0)] = placed([P, PIECE, PACK], BF16, "x_woven110", SPARE_AT)[:]
+        round_x(1, 1, 0, weave_on_vector)
+        quantize_x(1, 0, whole, shared)
+        x_woven[(1, 1, 1)] = late([P, PIECE, PACK], BF16, "x_woven111", "wt_second")[:]
+        quantize_x(1, 1, piece(0), x_woven[(1, 1, 0)])
+        round_x(1, 1, 1, weave_on_vector)
+        quantize_x(1, 1, piece(1), x_woven[(1, 1, 1)])
+
+        for m in range(2, TILES):
+            table_pass(0, m, "r", 1)
         for m in range(TILES):
             token_pass(0, m, 0)
         for m in range(TILES):
-            table_pass(0, m, 1, r_codes, r_plane)
             token_pass(0, m, 1)
             finish(0, m)
-
         for m in range(TILES):
-            table_pass(1, m, 0, q_codes, q_plane)
-            table_pass(1, m, 0, r_codes, r_plane)
-            table_pass(1, m, 1, q_codes, q_plane)
-        for m in range(TILES):
-            table_pass(1, m, 1, r_codes, r_plane)
-            token_pass(1, m, 0)
-            token_pass(1, m, 1)
+            for a in range(0 if m == 3 else 1, PASSES):
+                for tier in ("q", "r"):
+                    table_pass(1, m, tier, a)
+            for a in range(PASSES):
+                token_pass(1, m, a)
             finish(1, m)

@@ -32,6 +32,7 @@ FIRST_AT = WINDOW_AT + 4 * T
 SECOND_HALF_AT = FIRST_AT + ROOM // 2
 SUM_BANK = ((0, 1, 2, 3), (4, 5, 6, 3))
 SPARE_AT = SECOND_HALF_AT + 4 * ROOM
+BLOCK = 32
 EYE_RUN = K_PASS + 1
 
 FLOPS = 2 * N * J * (2 * K + L) + 2 * K_PASS * K * N
@@ -118,6 +119,9 @@ def tile_list_tiert_gelu_kernel(
             tab_plane = [sb([P, J], U8, "tab_plane%d" % a) for a in range(PASSES)]
             for a in range(PASSES):
                 nc.vector.memset(tab_plane[a][:].bitcast(I32), 0)
+            bias_runs = sb([P, BLOCK], F32, "bias_runs")
+            nc.vector.memset(bias_runs[:], 0.0)
+            nc.sync.dma_start(out=bias_runs[0:P:8, :], in_=b.rearrange("(m g c) -> g m c", m=TILES, g=QUADRANTS))
             picked_scales = sb([P, J], U8, "picked_scales")
             nc.vector.tensor_copy(out=picked_scales[:], in_=scale_window[:].indirect(offsets[:]))
 
@@ -153,9 +157,6 @@ def tile_list_tiert_gelu_kernel(
         nc.sync.dma_start(out=wt_second[:], in_=wt_by_pass[1])
         wx_codes = late([P, PASSES, 2 * N], U8, "wx_codes")
         nc.sync.dma_start(out=wx_codes[:].bitcast(I32), in_=wx_words.rearrange("a p b -> p a b").bitcast(I32))
-        bias = late([P, TILES], F32, "bias")
-        with nc.allow_non_contiguous_dma(reason="one bias value to a partition"):
-            nc.sync.dma_start(out=bias[:], in_=b.rearrange("(m p) -> p m", p=P))
         spread_scales(1)
         load_x(0, 0, late)
         load_x(0, 1, late)
@@ -279,7 +280,7 @@ def tile_list_tiert_gelu_kernel(
         def finish(h, m):
             name = "result%d%d" % (h, m)
             result = placed([P, HALF], F32, name, SECOND_HALF_AT + 4 * HALF * m) if h == 0 else sb([P, HALF], F32, name)
-            nc.scalar.activation(out=result[:], in_=acc[(h, m)][:], func=ACT.Gelu_apprx_tanh, bias=bias[:, m : m + 1])
+            nc.scalar.activation(out=result[:], in_=acc[(h, m)][:], func=ACT.Gelu_apprx_tanh, bias=bias[:, 8 * m : 8 * m + 1])
             nc.sync.dma_start(out=out[P * m : P * (m + 1), HALF * h : HALF * (h + 1)], in_=result[:])
 
         for u in range(2):
@@ -339,6 +340,8 @@ def tile_list_tiert_gelu_kernel(
             table_pass(1, m, "r", 0)
         bring_back(1, 3)
         left_over(1, 3)
+        bias = placed([P, BLOCK], F32, "bias", WINDOW_AT + 8 * PIECE)
+        nc.vector.transpose(out=bias[:], in_=bias_runs[:])
         for m in range(TILES):
             table_pass(0, m, "q", 1)
         for m in range(2):

@@ -297,17 +297,6 @@ def tile_list_tiert_gelu_kernel(
             bring_back(0, m)
             left_over(0, m)
         bring_back(0, 3)
-        warm_sum = bank(BACK_BANK, [P, HALF], "warm_sum")
-        for w in range(4):
-            nc.tensor.matmul_mx(
-                out=warm_sum[:],
-                lhsT=eye_codes[:, :P].bitcast(FP8X4),
-                lhsT_scale=eye_plane[:, :P],
-                rhs=eye_codes[:].bitcast(FP8X4),
-                rhs_scale=eye_plane[:],
-                start=True,
-                stop=True,
-            )
         pick_words(0, placed([P, HALF], U32, "picked_words0", FIRST_AT))
         quantize_tier("r", 0, 0, sb)
         part_words(0, 0, sb)

@@ -58,10 +58,10 @@ def tile_list_tiert_gelu_kernel(
             return psum.tile(shape, F32, name=name, tag="bank%d" % index)
 
         def walk_woven(ap):
-            return ap.rearrange("p (c i) t -> p c t i", i=4)
+            return ap.rearrange("p (c i) t -> p c t i", i=2)
 
         def walk_rows(ap):
-            return ap.rearrange("p t (c i) -> p c t i", i=4)
+            return ap.rearrange("p t (c i) -> p c t i", i=2)
 
         def weave_on_scalar(woven, rows):
             nc.scalar.activation(out=walk_woven(woven), in_=walk_rows(rows), func=ACT.Copy)

@@ -29,10 +29,12 @@ BACK_BANK = 6
 ROOM = 2 * HALF * PACK
 WINDOW_AT = 2 * ROOM
 FIRST_AT = WINDOW_AT + 4 * T
-SECOND_HALF_AT = FIRST_AT + ROOM // 2
-SUM_BANK = ((0, 1, 2, 3), (4, 5, 6, 3))
+SECOND_HALF_AT = FIRST_AT + 4 * ROOM
+SUM_BANK = ((0, 1, 2, 3), (4, 5, 6))
+LAST_BANKS = (3, 4)
 SPARE_AT = SECOND_HALF_AT + 4 * ROOM
 BLOCK = 32
+KIB = 1024
 EYE_RUN = K_PASS + 1
 
 FLOPS = 2 * N * J * (2 * K + L) + 2 * K_PASS * K * N
@@ -163,8 +165,8 @@ def tile_list_tiert_gelu_kernel(
         wt_rows = [[wt_first[u][:] for u in range(2)], [wt_second[:, :, piece(u)] for u in range(2)]]
 
 
-        eye_codes = late([P, K_PASS], U32, "eye_codes")
-        eye_plane = late([P, K_PASS], U8, "eye_plane")
+        eye_codes = sb([P, K_PASS], U32, "eye_codes")
+        eye_plane = sb([P, K_PASS], U8, "eye_plane")
         nc.vector.quantize_mx(out=eye_codes[:].bitcast(FP8X4), scales=eye_plane[:], in_=eye_woven[:, : PACK * K_PASS])
 
         codes = {}
@@ -205,7 +207,11 @@ def tile_list_tiert_gelu_kernel(
         def left_over(a, m):
             u = m // 2
             if ("r", a, u) not in woven:
-                woven[("r", a, u)] = sb([P, PIECE, PACK], BF16, "r_woven%d%d" % (a, u), "left_over%d%d" % (a, u))
+                name = "r_woven%d%d" % (a, u)
+                if (a, u) == (0, 1):
+                    woven[("r", a, u)] = placed([P, PIECE, PACK], BF16, name, SECOND_HALF_AT)
+                else:
+                    woven[("r", a, u)] = sb([P, PIECE, PACK], BF16, name, "left_over%d%d" % (a, u))
             nc.vector.tensor_tensor(
                 out=walk_woven(woven[("r", a, u)][:, within_piece(m), :]),
                 in0=walk_rows(wt_rows[a][u][:, :, within_piece(m)]),
@@ -250,49 +256,51 @@ def tile_list_tiert_gelu_kernel(
             return tile[:]
 
         acc = {}
+        whole = slice(0, HALF)
+
+        def open_sum(h, m, index, columns):
+            acc[(h, m)] = (bank(index, [P, columns.stop - columns.start], "acc%d%d_%d" % (h, m, columns.start)), columns)
 
         def table_pass(h, m, tier, a):
-            first = (h, m) not in acc
-            if first:
-                acc[(h, m)] = bank(SUM_BANK[h][m], [P, HALF], "acc%d%d" % (h, m))
+            if (h, m) not in acc:
+                open_sum(h, m, SUM_BANK[h][m], whole)
+            total, columns = acc[(h, m)]
             weights, weights_plane = tier_tile(tier, a, m)
             nc.tensor.matmul_mx(
-                out=acc[(h, m)][:],
+                out=total[:],
                 lhsT=weights,
                 lhsT_scale=weights_plane,
-                rhs=tab_codes[(h, a)][:].bitcast(FP4X4),
-                rhs_scale=tab_plane[a][:, HALF * h : HALF * (h + 1)],
-                start=first,
+                rhs=tab_codes[(h, a)][:, 2 * columns.start : 2 * columns.stop].bitcast(FP4X4),
+                rhs_scale=tab_plane[a][:, HALF * h + columns.start : HALF * h + columns.stop],
+                start=(tier, a) == ("q", 0),
                 stop=False,
             )
 
         def token_pass(h, m, a):
+            total, columns = acc[(h, m)]
             nc.tensor.matmul_mx(
-                out=acc[(h, m)][:],
+                out=total[:],
                 lhsT=wx_codes[:, a, 2 * P * m : 2 * P * (m + 1)].bitcast(FP4X4),
                 lhsT_scale=wx_plane[:, a, P * m : P * (m + 1)],
-                rhs=x_codes[(h, a)][:].bitcast(FP8X4),
-                rhs_scale=x_plane[(h, a)][:],
+                rhs=x_codes[(h, a)][:, columns].bitcast(FP8X4),
+                rhs_scale=x_plane[(h, a)][:, columns],
                 start=False,
                 stop=(a == PASSES - 1),
             )
 
         def finish(h, m):
-            name = "result%d%d" % (h, m)
-            result = placed([P, HALF], F32, name, SECOND_HALF_AT + 4 * HALF * m) if h == 0 else sb([P, HALF], F32, name)
-            nc.scalar.activation(out=result[:], in_=acc[(h, m)][:], func=ACT.Gelu_apprx_tanh, bias=bias[:, 8 * m : 8 * m + 1])
-            nc.sync.dma_start(out=out[P * m : P * (m + 1), HALF * h : HALF * (h + 1)], in_=result[:])
+            total, columns = acc[(h, m)]
+            shape = [P, columns.stop - columns.start]
+            name = "result%d%d_%d" % (h, m, columns.start)
+            result = placed(shape, F32, name, SECOND_HALF_AT + 4 * HALF * m) if h == 0 else sb(shape, F32, name)
+            nc.scalar.activation(out=result[:], in_=total[:], func=ACT.Gelu_apprx_tanh, bias=bias[:, 8 * m : 8 * m + 1])
+            nc.sync.dma_start(
+                out=out[P * m : P * (m + 1), HALF * h + columns.start : HALF * h + columns.stop], in_=result[:]
+            )
 
         for u in range(2):
             round_wt(0, u)
             quantize_tier("q", 0, u, late)
-        wx_plane = late([P, PASSES, N], U8, "wx_plane")
-        nc.vector.memset(wx_plane[:].rearrange("p a n -> p (a n)").bitcast(I32), 0)
-        for q in range(QUADRANTS):
-            nc.sync.dma_start(
-                out=wx_plane[32 * q : 32 * q + 4, :, :].bitcast(I32),
-                in_=wx_scales[:, 4 * q : 4 * q + 4, :].rearrange("a r n -> r a n").bitcast(I32),
-            )
         for m in range(3):
             bring_back(0, m)
             left_over(0, m)
@@ -301,12 +309,18 @@ def tile_list_tiert_gelu_kernel(
         quantize_tier("r", 0, 0, sb)
         part_words(0, 0, sb)
         left_over(0, 3)
-        load_x(1, 0, at_offset(SECOND_HALF_AT))
-        for u in range(2):
-            load_x(1, 1, at_offset(SECOND_HALF_AT + ROOM * (2 + u)), PIECE * u, PIECE)
+        wx_plane = placed([P, PASSES, N], U8, "wx_plane", FIRST_AT + 2 * KIB)
+        nc.vector.memset(wx_plane[:].rearrange("p a n -> p (a n)").bitcast(I32), 0)
+        for q in range(QUADRANTS):
+            nc.sync.dma_start(
+                out=wx_plane[32 * q : 32 * q + 4, :, :].bitcast(I32),
+                in_=wx_scales[:, 4 * q : 4 * q + 4, :].rearrange("a r n -> r a n").bitcast(I32),
+            )
 
         quantize_tier("r", 0, 1, sb)
-        pick_words(1, sb([P, HALF], U32, "picked_words1", "left_over01"))
+        load_x(1, 0, at_offset(SECOND_HALF_AT))
+        pick_words(1, placed([P, HALF], U32, "picked_words1", FIRST_AT + 3 * ROOM))
+        part_words(0, 1, at_offset(FIRST_AT + 3 * ROOM + 2 * KIB))
         for tier in ("q", "r"):
             for m in range(TILES):
                 table_pass(0, m, tier, 0)
@@ -316,10 +330,11 @@ def tile_list_tiert_gelu_kernel(
             quantize_tier("q", 1, u, at_offset(WINDOW_AT + 4 * PIECE * u))
             if u == 0:
                 part_words(1, 0, at_offset(ROOM + 2 * HALF))
+        for u in range(2):
+            load_x(1, 1, at_offset(WINDOW_AT + ROOM * (1 + u)), PIECE * u, PIECE)
         for m in range(2):
             bring_back(1, m)
             left_over(1, m)
-        part_words(0, 1, at_offset(ROOM + ROOM // 2))
         for m in range(2):
             table_pass(1, m, "q", 0)
         bring_back(1, 2)
@@ -338,7 +353,6 @@ def tile_list_tiert_gelu_kernel(
         for tier in ("q", "r"):
             table_pass(1, 2, tier, 0)
 
-        whole = slice(0, HALF)
         first_half = [woven_half(0, a, placed([P, HALF, PACK], BF16, "x_woven0%d" % a, (2 * HALF, SPARE_AT)[a])) for a in range(PASSES)]
         for u in range(2):
             round_x(0, 0, u, weave_on_scalar)
@@ -366,10 +380,17 @@ def tile_list_tiert_gelu_kernel(
         for m in range(TILES):
             token_pass(0, m, 1)
             finish(0, m)
-        for m in range(TILES):
-            for a in range(0 if m == 3 else 1, PASSES):
-                for tier in ("q", "r"):
-                    table_pass(1, m, tier, a)
+        for m in range(3):
+            for tier in ("q", "r"):
+                table_pass(1, m, tier, 1)
             for a in range(PASSES):
                 token_pass(1, m, a)
             finish(1, m)
+        for u in range(2):
+            open_sum(1, 3, LAST_BANKS[u], piece(u))
+            for a in range(PASSES):
+                for tier in ("q", "r"):
+                    table_pass(1, 3, tier, a)
+            for a in range(PASSES):
+                token_pass(1, 3, a)
+            finish(1, 3)

@@ -51,10 +51,10 @@ def tile_list_tiert_gelu_kernel(
         psum = ctx.enter_context(tc.psum_pool(name="psum", bufs=1))
 
         def sb(shape, dtype, name, tag=None):
-            return keep.tile(shape, dtype, name=name, tag=tag or name, align_bytes=64)
+            return keep.tile(shape, dtype, name=name, tag=tag or name, align_bytes=256)
 
         def placed(shape, dtype, name, offset):
-            return rooms.tile(shape, dtype, name=name, align_bytes=64, offset=offset)
+            return rooms.tile(shape, dtype, name=name, align_bytes=256, offset=offset)
 
         def bank(index, shape, name):
             return psum.tile(shape, F32, name=name, tag="bank%d" % index)
@@ -130,7 +130,7 @@ def tile_list_tiert_gelu_kernel(
         after_gather = ctx.enter_context(tc.tile_pool(name="after_gather", bufs=1, side="right"))
 
         def late(shape, dtype, name, tag=None):
-            return after_gather.tile(shape, dtype, name=name, tag=tag or name, align_bytes=64)
+            return after_gather.tile(shape, dtype, name=name, tag=tag or name, align_bytes=256)
 
         def spread_scales(a):
             for q in range(QUADRANTS):

@@ -35,6 +35,7 @@ LAST_BANKS = (3, 4)
 SPARE_AT = SECOND_HALF_AT + 4 * ROOM
 BLOCK = 32
 KIB = 1024
+PLANES_AT = SPARE_AT + ROOM + 128
 EYE_RUN = K_PASS + 1
 
 FLOPS = 2 * N * J * (2 * K + L) + 2 * K_PASS * K * N
@@ -55,6 +56,9 @@ def tile_list_tiert_gelu_kernel(
 
         def placed(shape, dtype, name, offset):
             return rooms.tile(shape, dtype, name=name, align_bytes=256, offset=offset)
+
+        def moving_plane(width, name, index):
+            return rooms.tile([P, width], U8, name=name, align_bytes=128, offset=PLANES_AT + KIB * index)
 
         def bank(index, shape, name):
             return psum.tile(shape, F32, name=name, tag="bank%d" % index)
@@ -118,7 +122,7 @@ def tile_list_tiert_gelu_kernel(
             )
 
             nc.vector.memset(scale_window[0:SCALE_ROW0, :].bitcast(I32), 0)
-            tab_plane = [sb([P, J], U8, "tab_plane%d" % a) for a in range(PASSES)]
+            tab_plane = [moving_plane(J, "tab_plane%d" % a, a) for a in range(PASSES)]
             for a in range(PASSES):
                 nc.vector.memset(tab_plane[a][:].bitcast(I32), 0)
             bias_runs = sb([P, BLOCK], F32, "bias_runs")
@@ -247,7 +251,7 @@ def tile_list_tiert_gelu_kernel(
         def quantize_x(h, a, columns, woven_ap, tag=None):
             if (h, a) not in x_codes:
                 x_codes[(h, a)] = sb([P, HALF], U32, "x_codes%d%d" % (h, a), tag)
-                x_plane[(h, a)] = sb([P, HALF], U8, "x_plane%d%d" % (h, a))
+                x_plane[(h, a)] = moving_plane(HALF, "x_plane%d%d" % (h, a), PASSES * (1 + h) + a)
             quantize(x_codes[(h, a)][:, columns], x_plane[(h, a)][:, columns], woven_ap)
 
         def woven_half(h, a, tile):

@@ -25,18 +25,24 @@ PIECE = 256
 QUADRANTS = 4
 GROUP = 16
 SCALE_ROW0 = P - PASSES * GROUP
-BACK_BANK = 6
-ROOM = 2 * HALF * PACK
-WINDOW_AT = 2 * ROOM
-FIRST_AT = WINDOW_AT + 4 * T
-SECOND_HALF_AT = FIRST_AT + 4 * ROOM
-SUM_BANK = ((0, 1, 2, 3), (4, 5, 6))
-LAST_BANKS = (3, 4)
-SPARE_AT = SECOND_HALF_AT + 4 * ROOM
 BLOCK = 32
-KIB = 1024
-PLANES_AT = SPARE_AT + ROOM + 128
 EYE_RUN = K_PASS + 1
+KIB = 1024
+
+WINDOW_AT = 0
+LAST_ROWS_AT = WINDOW_AT + 16 * KIB
+WT_FIRST_AT = LAST_ROWS_AT + 2 * KIB
+LEFT_OVER0_AT = WT_FIRST_AT + 10 * KIB
+SECOND_WOVEN_AT = LEFT_OVER0_AT + 5 * KIB
+SECOND_ROWS_AT = SECOND_WOVEN_AT + 5 * KIB
+THIRD_ROWS_AT = SECOND_ROWS_AT + 8 * KIB
+EYE_AT = THIRD_ROWS_AT + 8 * KIB
+PLANES_AT = EYE_AT + 5 * KIB + 128
+WT_SECOND_AT = 0
+WX_AT = WT_SECOND_AT + 8 * KIB
+X_ROWS_AT = WX_AT + 2 * KIB
+X_WOVEN_AT = X_ROWS_AT + 8 * KIB
+WX_PLANE_AT = X_WOVEN_AT + 16 * KIB
 
 FLOPS = 2 * N * J * (2 * K + L) + 2 * K_PASS * K * N
 
@@ -48,17 +54,17 @@ def tile_list_tiert_gelu_kernel(
     with ExitStack() as ctx:
         lists = ctx.enter_context(tc.tile_pool(name="lists", bufs=1))
         keep = ctx.enter_context(tc.tile_pool(name="keep", bufs=1))
-        rooms = ctx.enter_context(tc.tile_pool(name="rooms", bufs=1))
+        early = ctx.enter_context(tc.tile_pool(name="early", bufs=1))
         psum = ctx.enter_context(tc.psum_pool(name="psum", bufs=1))
 
-        def sb(shape, dtype, name, tag=None):
-            return keep.tile(shape, dtype, name=name, tag=tag or name, align_bytes=256)
+        def sb(shape, dtype, name):
+            return keep.tile(shape, dtype, name=name, align_bytes=256)
 
-        def placed(shape, dtype, name, offset):
-            return rooms.tile(shape, dtype, name=name, align_bytes=256, offset=offset)
+        def early_at(offset):
+            return lambda shape, dtype, name: early.tile(shape, dtype, name=name, align_bytes=256, offset=offset)
 
         def moving_plane(width, name, index):
-            return rooms.tile([P, width], U8, name=name, align_bytes=128, offset=PLANES_AT + KIB * index)
+            return early.tile([P, width], U8, name=name, align_bytes=128, offset=PLANES_AT + KIB * index)
 
         def bank(index, shape, name):
             return psum.tile(shape, F32, name=name, tag="bank%d" % index)
@@ -69,14 +75,14 @@ def tile_list_tiert_gelu_kernel(
         def walk_rows(ap):
             return ap.rearrange("p t (c i) -> p c t i", i=2)
 
-        def weave_on_scalar(woven, rows):
-            nc.scalar.activation(out=walk_woven(woven), in_=walk_rows(rows), func=ACT.Copy)
+        def weave_on_scalar(woven_ap, rows):
+            nc.scalar.activation(out=walk_woven(woven_ap), in_=walk_rows(rows), func=ACT.Copy)
 
-        def weave_on_vector(woven, rows):
-            nc.vector.tensor_copy(out=walk_woven(woven), in_=walk_rows(rows))
+        def weave_on_vector(woven_ap, rows):
+            nc.vector.tensor_copy(out=walk_woven(woven_ap), in_=walk_rows(rows))
 
-        def quantize(codes, plane, woven):
-            nc.vector.quantize_mx(out=codes.bitcast(FP8X4), scales=plane, in_=woven.rearrange("p c t -> p (c t)"))
+        def quantize(codes_ap, plane_ap, woven_ap):
+            nc.vector.quantize_mx(out=codes_ap.bitcast(FP8X4), scales=plane_ap, in_=woven_ap.rearrange("p c t -> p (c t)"))
 
         def piece(u):
             return slice(PIECE * u, PIECE * (u + 1))
@@ -93,48 +99,50 @@ def tile_list_tiert_gelu_kernel(
         nc.scalar.activation(out=warm_out[:], in_=warm_in[:], func=ACT.Gelu_apprx_tanh)
 
         with tc.tile_pool(name="scales", bufs=1, side="right") as scales:
-            scale_window = scales.tile([P, T], U8, name="scale_window")
+            scale_window = scales.tile([P, T], U8, name="scale_window", align_bytes=256)
             nc.sync.dma_start(offsets[:], offs)
             nc.sync.dma_start(
                 out=scale_window[SCALE_ROW0:P, :].bitcast(I32), in_=tab_scales.rearrange("a q t -> (a q) t").bitcast(I32)
             )
-            wt_first = [placed([P, PACK, PIECE], F32, "wt_first%d" % u, FIRST_AT + 3 * ROOM * u) for u in range(2)]
+            wt_first = [early_at(WT_FIRST_AT + 6 * KIB * u)([P, PACK, PIECE], F32, "wt_first%d" % u) for u in range(2)]
             for u in range(2):
                 nc.sync.dma_start(out=wt_first[u][:], in_=wt_by_pass[0][:, :, piece(u)])
-            word_window = placed([P, T], I32, "word_window", WINDOW_AT)
+            word_window = early_at(WINDOW_AT)([P, T], I32, "word_window")
             nc.sync.dma_start(out=word_window[:], in_=tab_words[0].rearrange("p t b -> p (t b)").bitcast(I32))
 
-            eye_run = placed([P, EYE_RUN + 3], BF16, "eye_run", ROOM + ROOM // 2 - 512)
-            nc.gpsimd.memset(eye_run[:].bitcast(I32), 0)
+            eye_run = sb([P, EYE_RUN // 2 + 2], F32, "eye_run")
+            nc.gpsimd.memset(eye_run[:], 0.0)
             nc.gpsimd.affine_select(
                 out=eye_run[:],
                 in_=eye_run[:],
                 compare_op=ALU.not_equal,
                 fill=1.0,
                 base=0,
-                pattern=[[-1, EYE_RUN + 3]],
-                channel_multiplier=PACK,
+                pattern=[[-1, EYE_RUN // 2 + 2]],
+                channel_multiplier=PACK // 2,
             )
-            eye_woven = sb([P, PACK * EYE_RUN], BF16, "eye_woven")
-            nc.scalar.copy(
-                out=eye_woven[:].rearrange("p (t c) -> p t c", t=PACK),
-                in_=eye_run[:, :EYE_RUN].rearrange("p (o c) -> p o c", o=1).to_broadcast([P, PACK, EYE_RUN]),
-            )
-
             nc.vector.memset(scale_window[0:SCALE_ROW0, :].bitcast(I32), 0)
+            eye_woven = early_at(EYE_AT)([P, PACK * EYE_RUN], BF16, "eye_woven")
+            nc.vector.tensor_copy(
+                out=eye_woven[:].rearrange("p (t c) -> p t c", t=PACK),
+                in_=eye_run[:].bitcast(BF16)[:, 1 : EYE_RUN + 1].rearrange("p (o c) -> p o c", o=1).to_broadcast([P, PACK, EYE_RUN]),
+            )
             tab_plane = [moving_plane(J, "tab_plane%d" % a, a) for a in range(PASSES)]
             for a in range(PASSES):
                 nc.vector.memset(tab_plane[a][:].bitcast(I32), 0)
             bias_runs = sb([P, BLOCK], F32, "bias_runs")
             nc.vector.memset(bias_runs[:], 0.0)
             nc.sync.dma_start(out=bias_runs[0:P:8, :], in_=b.rearrange("(m g c) -> g m c", m=TILES, g=QUADRANTS))
-            picked_scales = sb([P, J], U8, "picked_scales")
+            eye_codes = sb([P, K_PASS], U32, "eye_codes")
+            eye_plane = sb([P, K_PASS], U8, "eye_plane")
+            nc.vector.quantize_mx(out=eye_codes[:].bitcast(FP8X4), scales=eye_plane[:], in_=eye_woven[:, : PACK * K_PASS])
+            picked_scales = early_at(EYE_AT + 2 * KIB)([P, J], U8, "picked_scales")
             nc.vector.tensor_copy(out=picked_scales[:], in_=scale_window[:].indirect(offsets[:]))
 
-        after_gather = ctx.enter_context(tc.tile_pool(name="after_gather", bufs=1, side="right"))
+        late = ctx.enter_context(tc.tile_pool(name="late", bufs=1, side="right"))
 
-        def late(shape, dtype, name, tag=None):
-            return after_gather.tile(shape, dtype, name=name, tag=tag or name, align_bytes=256)
+        def late_at(offset):
+            return lambda shape, dtype, name: late.tile(shape, dtype, name=name, align_bytes=256, offset=offset)
 
         def spread_scales(a):
             for q in range(QUADRANTS):
@@ -145,46 +153,39 @@ def tile_list_tiert_gelu_kernel(
 
         x_rows = {}
 
-        def load_x(h, a, make_tile, first=0, width=HALF):
-            rows = make_tile([P, PACK, width], F32, "x_rows%d%d_%d" % (h, a, first))
-            j0 = HALF * h + first
+        def load_x(h, a, columns, make_tile):
+            width = columns.stop - columns.start
+            rows = make_tile([P, PACK, width], F32, "x_rows%d%d_%d" % (h, a, columns.start))
+            x_rows[(h, a, columns.start)] = rows
             nc.sync.dma_start(
                 out=rows[:],
-                in_=x[K_PASS * a : K_PASS * (a + 1), j0 : j0 + width].rearrange("(p t) j -> p t j", t=PACK),
+                in_=x[K_PASS * a : K_PASS * (a + 1), HALF * h + columns.start : HALF * h + columns.stop].rearrange(
+                    "(p t) j -> p t j", t=PACK
+                ),
             )
-            for u in range(width // PIECE):
-                x_rows[(h, a, first // PIECE + u)] = rows[:, :, piece(u)]
 
-        def at_offset(offset):
-            return lambda shape, dtype, name: placed(shape, dtype, name, offset)
-
+        whole = slice(0, HALF)
         spread_scales(0)
-        wt_second = late([P, PACK, N], F32, "wt_second")
+        wt_second = late_at(WT_SECOND_AT)([P, PACK, N], F32, "wt_second")
         nc.sync.dma_start(out=wt_second[:], in_=wt_by_pass[1])
-        wx_codes = late([P, PASSES, 2 * N], U8, "wx_codes")
+        wx_codes = late_at(WX_AT)([P, PASSES, 2 * N], U8, "wx_codes")
         nc.sync.dma_start(out=wx_codes[:].bitcast(I32), in_=wx_words.rearrange("a p b -> p a b").bitcast(I32))
         spread_scales(1)
-        load_x(0, 0, late)
-        load_x(0, 1, late)
+        load_x(0, 0, whole, late_at(X_ROWS_AT))
         wt_rows = [[wt_first[u][:] for u in range(2)], [wt_second[:, :, piece(u)] for u in range(2)]]
-
-
-        eye_codes = sb([P, K_PASS], U32, "eye_codes")
-        eye_plane = sb([P, K_PASS], U8, "eye_plane")
-        nc.vector.quantize_mx(out=eye_codes[:].bitcast(FP8X4), scales=eye_plane[:], in_=eye_woven[:, : PACK * K_PASS])
 
         codes = {}
         planes = {}
         woven = {}
 
+        def round_wt(a, u, make_tile=sb):
+            woven[("q", a, u)] = make_tile([P, PIECE, PACK], BF16, "q_woven%d%d" % (a, u))
+            weave_on_scalar(woven[("q", a, u)][:], wt_rows[a][u])
+
         def quantize_tier(tier, a, u, make_tile):
             codes[(tier, a, u)] = make_tile([P, PIECE], U32, "%s_codes%d%d" % (tier, a, u))
             planes[(tier, a, u)] = sb([P, PIECE], U8, "%s_plane%d%d" % (tier, a, u))
             quantize(codes[(tier, a, u)][:], planes[(tier, a, u)][:], woven[(tier, a, u)][:])
-
-        def round_wt(a, u):
-            woven[("q", a, u)] = placed([P, PIECE, PACK], BF16, "q_woven%d%d" % (a, u), ROOM + ROOM // 2 * u)
-            weave_on_scalar(woven[("q", a, u)][:], wt_rows[a][u])
 
         def tier_tile(tier, a, m):
             return (
@@ -194,8 +195,8 @@ def tile_list_tiert_gelu_kernel(
 
         back = {}
 
-        def bring_back(a, m):
-            back[(a, m)] = bank(BACK_BANK + m % 2, [P, PACK, P], "back%d%d" % (a, m))
+        def bring_back(a, m, index):
+            back[(a, m)] = bank(index, [P, PACK, P], "back%d%d" % (a, m))
             q_codes, q_plane = tier_tile("q", a, m)
             for t in range(PACK):
                 nc.tensor.matmul_mx(
@@ -211,11 +212,8 @@ def tile_list_tiert_gelu_kernel(
         def left_over(a, m):
             u = m // 2
             if ("r", a, u) not in woven:
-                name = "r_woven%d%d" % (a, u)
-                if (a, u) == (0, 1):
-                    woven[("r", a, u)] = placed([P, PIECE, PACK], BF16, name, SECOND_HALF_AT)
-                else:
-                    woven[("r", a, u)] = sb([P, PIECE, PACK], BF16, name, "left_over%d%d" % (a, u))
+                make_tile = early_at(LEFT_OVER0_AT + 2 * KIB * u) if a == 0 else (early_at(SECOND_WOVEN_AT + 3 * KIB), late_at(X_WOVEN_AT))[u]
+                woven[("r", a, u)] = make_tile([P, PIECE, PACK], BF16, "r_woven%d%d" % (a, u))
             nc.vector.tensor_tensor(
                 out=walk_woven(woven[("r", a, u)][:, within_piece(m), :]),
                 in0=walk_rows(wt_rows[a][u][:, :, within_piece(m)]),
@@ -224,59 +222,57 @@ def tile_list_tiert_gelu_kernel(
             )
 
         picked_words = {}
-        tab_codes = {}
 
-        def pick_words(h, tile):
-            columns = HALF // GROUP
-            picked_words[h] = tile
+        def pick_words(tokens, offset):
+            tile = early_at(offset)([P, tokens.stop - tokens.start], U32, "picked_words%d" % tokens.start)
+            picked_words[tokens.start] = tile
             nc.vector.tensor_copy(
-                out=picked_words[h][:],
-                in_=word_window[:].bitcast(U32).indirect(offsets[:, columns * h : columns * (h + 1)]),
+                out=tile[:],
+                in_=word_window[:].bitcast(U32).indirect(offsets[:, tokens.start // GROUP : tokens.stop // GROUP]),
             )
 
-        def part_words(h, a, make_tile):
-            tab_codes[(h, a)] = make_tile([P, 2 * HALF], U8, "tab_codes%d%d" % (h, a))
+        tab_codes = {}
+
+        def part_words(tokens, a, make_tile=sb):
+            h, first = divmod(tokens.start, HALF)
+            if (h, a) not in tab_codes:
+                tab_codes[(h, a)] = make_tile([P, 2 * HALF], U8, "tab_codes%d%d" % (h, a))
             nc.vector.tensor_copy(
-                out=tab_codes[(h, a)][:].bitcast(U16),
-                in_=picked_words[h][:].bitcast(U16).rearrange("p (j a) -> p a j", a=PASSES)[:, a, :],
+                out=tab_codes[(h, a)][:].bitcast(U16)[:, first : first + tokens.stop - tokens.start],
+                in_=picked_words[tokens.start][:].bitcast(U16).rearrange("p (j a) -> p a j", a=PASSES)[:, a, :],
             )
 
         x_woven = {}
         x_codes = {}
         x_plane = {}
 
-        def round_x(h, a, u, weave):
-            weave(x_woven[(h, a, u)], x_rows[(h, a, u)])
+        def round_x(h, a, columns, weave, make_tile):
+            key = (h, a, columns.start)
+            x_woven[key] = make_tile([P, columns.stop - columns.start, PACK], BF16, "x_woven%d%d_%d" % key)
+            weave(x_woven[key][:], x_rows[key][:])
 
-        def quantize_x(h, a, columns, woven_ap, tag=None):
+        def quantize_x(h, a, columns, make_tile):
             if (h, a) not in x_codes:
-                x_codes[(h, a)] = sb([P, HALF], U32, "x_codes%d%d" % (h, a), tag)
+                x_codes[(h, a)] = make_tile([P, HALF], U32, "x_codes%d%d" % (h, a))
                 x_plane[(h, a)] = moving_plane(HALF, "x_plane%d%d" % (h, a), PASSES * (1 + h) + a)
-            quantize(x_codes[(h, a)][:, columns], x_plane[(h, a)][:, columns], woven_ap)
-
-        def woven_half(h, a, tile):
-            for u in range(2):
-                x_woven[(h, a, u)] = tile[:, piece(u), :]
-            return tile[:]
+            quantize(x_codes[(h, a)][:, columns], x_plane[(h, a)][:, columns], x_woven[(h, a, columns.start)][:])
 
         acc = {}
-        whole = slice(0, HALF)
 
         def open_sum(h, m, index, columns):
             acc[(h, m)] = (bank(index, [P, columns.stop - columns.start], "acc%d%d_%d" % (h, m, columns.start)), columns)
 
-        def table_pass(h, m, tier, a):
-            if (h, m) not in acc:
-                open_sum(h, m, SUM_BANK[h][m], whole)
-            total, columns = acc[(h, m)]
+        def table_pass(h, m, tier, a, columns=None):
+            total, span = acc[(h, m)]
+            columns = columns or span
             weights, weights_plane = tier_tile(tier, a, m)
             nc.tensor.matmul_mx(
-                out=total[:],
+                out=total[:, columns.start - span.start : columns.stop - span.start],
                 lhsT=weights,
                 lhsT_scale=weights_plane,
                 rhs=tab_codes[(h, a)][:, 2 * columns.start : 2 * columns.stop].bitcast(FP4X4),
                 rhs_scale=tab_plane[a][:, HALF * h + columns.start : HALF * h + columns.stop],
-                start=(tier, a) == ("q", 0),
+                start=(tier, a, columns.start) == ("q", 0, span.start),
                 stop=False,
             )
 
@@ -294,104 +290,126 @@ def tile_list_tiert_gelu_kernel(
 
         def finish(h, m):
             total, columns = acc[(h, m)]
-            shape = [P, columns.stop - columns.start]
-            name = "result%d%d_%d" % (h, m, columns.start)
-            result = placed(shape, F32, name, SECOND_HALF_AT + 4 * HALF * m) if h == 0 else sb(shape, F32, name)
+            make_tile = early_at(THIRD_ROWS_AT + 4 * HALF * m) if h == 0 else sb
+            result = make_tile([P, columns.stop - columns.start], F32, "result%d%d_%d" % (h, m, columns.start))
             nc.scalar.activation(out=result[:], in_=total[:], func=ACT.Gelu_apprx_tanh, bias=bias[:, 8 * m : 8 * m + 1])
             nc.sync.dma_start(
                 out=out[P * m : P * (m + 1), HALF * h + columns.start : HALF * h + columns.stop], in_=result[:]
             )
 
-        for u in range(2):
-            round_wt(0, u)
-            quantize_tier("q", 0, u, late)
-        for m in range(3):
-            bring_back(0, m)
-            left_over(0, m)
-        bring_back(0, 3)
-        pick_words(0, placed([P, HALF], U32, "picked_words0", FIRST_AT))
-        quantize_tier("r", 0, 0, sb)
-        part_words(0, 0, sb)
-        left_over(0, 3)
-        wx_plane = placed([P, PASSES, N], U8, "wx_plane", FIRST_AT + 2 * KIB)
+        round_wt(0, 0)
+        round_wt(0, 1, early_at(THIRD_ROWS_AT - KIB))
+        quantize_tier("q", 0, 0, early_at(EYE_AT))
+        wx_plane = late_at(WX_PLANE_AT)([P, PASSES, N], U8, "wx_plane")
         nc.vector.memset(wx_plane[:].rearrange("p a n -> p (a n)").bitcast(I32), 0)
         for q in range(QUADRANTS):
             nc.sync.dma_start(
                 out=wx_plane[32 * q : 32 * q + 4, :, :].bitcast(I32),
                 in_=wx_scales[:, 4 * q : 4 * q + 4, :].rearrange("a r n -> r a n").bitcast(I32),
             )
+        quantize_tier("q", 0, 1, early_at(EYE_AT + KIB))
+        load_x(0, 1, whole, early_at(SECOND_ROWS_AT))
+        load_x(1, 0, whole, early_at(THIRD_ROWS_AT))
+        for m in range(TILES):
+            bring_back(0, m, TILES + m)
+        def keep_warm(index, weights, weights_plane):
+            nc.tensor.matmul_mx(
+                out=bank(index, [P, HALF], "warm")[:],
+                lhsT=weights,
+                lhsT_scale=weights_plane,
+                rhs=eye_codes[:].bitcast(FP8X4),
+                rhs_scale=eye_plane[:],
+                start=True,
+                stop=True,
+            )
 
+        for m in range(TILES):
+            left_over(0, m)
+            if m > 0:
+                keep_warm(TILES + m, *tier_tile("q", 0, m))
+        for u in range(2):
+            load_x(1, 1, piece(u), early_at(LAST_ROWS_AT + 4 * KIB * u))
+        quantize_tier("r", 0, 0, sb)
+        keep_warm(7, *tier_tile("r", 0, 0))
+
+        for m in range(TILES):
+            open_sum(0, m, m, whole)
+        for m in range(2):
+            open_sum(1, m, TILES + m, whole)
+
+        def first_passes(quarter, tiles):
+            for tier in ("q", "r"):
+                for m in tiles:
+                    table_pass(quarter // 2, m, tier, 0, piece(quarter % 2))
+
+        pick_words(piece(0), WT_FIRST_AT + 6 * KIB)
         quantize_tier("r", 0, 1, sb)
-        load_x(1, 0, at_offset(SECOND_HALF_AT))
-        pick_words(1, placed([P, HALF], U32, "picked_words1", FIRST_AT + 3 * ROOM))
-        part_words(0, 1, at_offset(FIRST_AT + 3 * ROOM + 2 * KIB))
-        for tier in ("q", "r"):
-            for m in range(TILES):
-                table_pass(0, m, tier, 0)
+        keep_warm(7, *tier_tile("r", 0, 2))
+        part_words(piece(0), 0)
+        first_passes(0, range(TILES))
+        pick_words(piece(1), LEFT_OVER0_AT + 2 * KIB)
+        part_words(piece(0), 1)
+        part_words(piece(1), 0)
+        first_passes(1, range(TILES))
+        pick_words(piece(2), WT_FIRST_AT + 6 * KIB)
+        part_words(piece(1), 1)
+        part_words(piece(2), 0)
+        first_passes(2, range(2))
 
         for u in range(2):
-            round_wt(1, u)
-            quantize_tier("q", 1, u, at_offset(WINDOW_AT + 4 * PIECE * u))
-            if u == 0:
-                part_words(1, 0, at_offset(ROOM + 2 * HALF))
-        for u in range(2):
-            load_x(1, 1, at_offset(WINDOW_AT + ROOM * (1 + u)), PIECE * u, PIECE)
+            round_wt(1, u, early_at(SECOND_WOVEN_AT + 2 * KIB * u))
+        for h, a in ((0, 0), (0, 1), (1, 0)):
+            round_x(h, a, whole, weave_on_scalar, late_at(X_WOVEN_AT + 4 * KIB * (PASSES * h + a)))
+        pick_words(piece(3), LEFT_OVER0_AT + 2 * KIB + KIB // 2)
+        quantize_tier("q", 1, 0, early_at(LEFT_OVER0_AT + KIB + KIB // 2))
+        part_words(piece(3), 0)
+        quantize_tier("q", 1, 1, early_at(WINDOW_AT))
         for m in range(2):
-            bring_back(1, m)
+            bring_back(1, m, 6 + m)
             left_over(1, m)
-        for m in range(2):
-            table_pass(1, m, "q", 0)
-        bring_back(1, 2)
-        left_over(1, 2)
-        quantize_tier("r", 1, 0, sb)
-        for m in range(2):
-            table_pass(1, m, "r", 0)
-        bring_back(1, 3)
-        left_over(1, 3)
-        bias = placed([P, BLOCK], F32, "bias", WINDOW_AT + 8 * PIECE)
-        nc.vector.transpose(out=bias[:], in_=bias_runs[:])
         for m in range(TILES):
             table_pass(0, m, "q", 1)
-        for m in range(2):
-            table_pass(0, m, "r", 1)
-        for tier in ("q", "r"):
-            table_pass(1, 2, tier, 0)
-
-        first_half = [woven_half(0, a, placed([P, HALF, PACK], BF16, "x_woven0%d" % a, (2 * HALF, SPARE_AT)[a])) for a in range(PASSES)]
-        for u in range(2):
-            round_x(0, 0, u, weave_on_scalar)
-        quantize_x(0, 0, whole, first_half[0], "left_over10")
-        quantize_tier("r", 1, 1, sb)
-        for u in range(2):
-            round_x(0, 1, u, weave_on_scalar)
-        quantize_x(0, 1, whole, first_half[1], "left_over11")
-        part_words(1, 1, at_offset(SPARE_AT + ROOM // 2))
-        shared = woven_half(1, 0, late([P, HALF, PACK], BF16, "x_woven10", "wt_second"))
-        round_x(1, 0, 0, weave_on_scalar)
-        round_x(1, 0, 1, weave_on_vector)
-        x_woven[(1, 1, 0)] = placed([P, PIECE, PACK], BF16, "x_woven110", SPARE_AT)[:]
-        round_x(1, 1, 0, weave_on_vector)
-        quantize_x(1, 0, whole, shared)
-        x_woven[(1, 1, 1)] = late([P, PIECE, PACK], BF16, "x_woven111", "wt_second")[:]
-        quantize_x(1, 1, piece(0), x_woven[(1, 1, 0)])
-        round_x(1, 1, 1, weave_on_vector)
-        quantize_x(1, 1, piece(1), x_woven[(1, 1, 1)])
-
+        bring_back(1, 2, 6)
+        first_passes(3, range(2))
+        bring_back(1, 3, 7)
+        quantize_tier("r", 1, 0, sb)
+        quantize_x(0, 0, whole, sb)
         for m in range(2, TILES):
+            left_over(1, m)
+        bias = early_at(WINDOW_AT + 2 * KIB)([P, BLOCK], F32, "bias")
+        nc.vector.transpose(out=bias[:], in_=bias_runs[:])
+        quantize_x(0, 1, whole, late_at(X_WOVEN_AT + 2 * KIB))
+        quantize_tier("r", 1, 1, late_at(X_WOVEN_AT + 4 * KIB))
+        round_x(1, 1, piece(0), weave_on_vector, late_at(X_WOVEN_AT + 5 * KIB))
+        for quarter in (2, 3):
+            part_words(piece(quarter), 1, late_at(X_WOVEN_AT))
+        round_x(1, 1, piece(1), weave_on_vector, early_at(LAST_ROWS_AT))
+        for u in range(2):
+            quantize_x(1, 1, piece(u), sb)
+        quantize_x(1, 0, whole, sb)
+
+        for m in range(2):
             table_pass(0, m, "r", 1)
         for m in range(TILES):
             token_pass(0, m, 0)
+        open_sum(1, 2, 6, whole)
+        for tier in ("q", "r"):
+            table_pass(1, 2, tier, 0)
         for m in range(TILES):
+            if m >= 2:
+                table_pass(0, m, "r", 1)
             token_pass(0, m, 1)
             finish(0, m)
+
         for m in range(3):
             for tier in ("q", "r"):
                 table_pass(1, m, tier, 1)
+        for m in range(3):
             for a in range(PASSES):
                 token_pass(1, m, a)
             finish(1, m)
         for u in range(2):
-            open_sum(1, 3, LAST_BANKS[u], piece(u))
+            open_sum(1, 3, TILES + u, piece(u))
             for a in range(PASSES):
                 for tier in ("q", "r"):
                     table_pass(1, 3, tier, a)

@@ -31,17 +31,17 @@ KIB = 1024
 
 WINDOW_AT = 0
 LAST_ROWS_AT = WINDOW_AT + 16 * KIB
-WT_FIRST_AT = LAST_ROWS_AT + 2 * KIB
-LEFT_OVER0_AT = WT_FIRST_AT + 10 * KIB
+WT_FIRST_AT = (LAST_ROWS_AT + 10 * KIB, LAST_ROWS_AT + 2 * KIB)
+FOURTH_ROWS_AT = WT_FIRST_AT[0] + 2 * KIB
+LEFT_OVER0_AT = FOURTH_ROWS_AT + 7 * KIB
 SECOND_WOVEN_AT = LEFT_OVER0_AT + 5 * KIB
-SECOND_ROWS_AT = SECOND_WOVEN_AT + 5 * KIB
-THIRD_ROWS_AT = SECOND_ROWS_AT + 8 * KIB
-EYE_AT = THIRD_ROWS_AT + 8 * KIB
+THIRD_ROWS_AT = SECOND_WOVEN_AT + 9 * KIB
+EYE_AT = THIRD_ROWS_AT + 4 * KIB
 PLANES_AT = EYE_AT + 5 * KIB + 128
 WT_SECOND_AT = 0
 WX_AT = WT_SECOND_AT + 8 * KIB
 X_ROWS_AT = WX_AT + 2 * KIB
-X_WOVEN_AT = X_ROWS_AT + 8 * KIB
+X_WOVEN_AT = X_ROWS_AT + 12 * KIB
 WX_PLANE_AT = X_WOVEN_AT + 16 * KIB
 
 FLOPS = 2 * N * J * (2 * K + L) + 2 * K_PASS * K * N
@@ -104,7 +104,7 @@ def tile_list_tiert_gelu_kernel(
             nc.sync.dma_start(
                 out=scale_window[SCALE_ROW0:P, :].bitcast(I32), in_=tab_scales.rearrange("a q t -> (a q) t").bitcast(I32)
             )
-            wt_first = [early_at(WT_FIRST_AT + 6 * KIB * u)([P, PACK, PIECE], F32, "wt_first%d" % u) for u in range(2)]
+            wt_first = [early_at(WT_FIRST_AT[u])([P, PACK, PIECE], F32, "wt_first%d" % u) for u in range(2)]
             for u in range(2):
                 nc.sync.dma_start(out=wt_first[u][:], in_=wt_by_pass[0][:, :, piece(u)])
             word_window = early_at(WINDOW_AT)([P, T], I32, "word_window")
@@ -153,26 +153,25 @@ def tile_list_tiert_gelu_kernel(
 
         x_rows = {}
 
-        def load_x(h, a, columns, make_tile):
-            width = columns.stop - columns.start
-            rows = make_tile([P, PACK, width], F32, "x_rows%d%d_%d" % (h, a, columns.start))
-            x_rows[(h, a, columns.start)] = rows
+        def load_x(h, a, u, make_tile):
+            x_rows[(h, a, u)] = make_tile([P, PACK, PIECE], F32, "x_rows%d%d%d" % (h, a, u))
+            j0 = HALF * h + PIECE * u
             nc.sync.dma_start(
-                out=rows[:],
-                in_=x[K_PASS * a : K_PASS * (a + 1), HALF * h + columns.start : HALF * h + columns.stop].rearrange(
-                    "(p t) j -> p t j", t=PACK
-                ),
+                out=x_rows[(h, a, u)][:],
+                in_=x[K_PASS * a : K_PASS * (a + 1), j0 : j0 + PIECE].rearrange("(p t) j -> p t j", t=PACK),
             )
 
         whole = slice(0, HALF)
         spread_scales(0)
-        wt_second = late_at(WT_SECOND_AT)([P, PACK, N], F32, "wt_second")
-        nc.sync.dma_start(out=wt_second[:], in_=wt_by_pass[1])
+        wt_second = [late_at(WT_SECOND_AT + 4 * KIB * u)([P, PACK, PIECE], F32, "wt_second%d" % u) for u in range(2)]
+        for u in range(2):
+            nc.sync.dma_start(out=wt_second[u][:], in_=wt_by_pass[1][:, :, piece(u)])
+        spread_scales(1)
         wx_codes = late_at(WX_AT)([P, PASSES, 2 * N], U8, "wx_codes")
         nc.sync.dma_start(out=wx_codes[:].bitcast(I32), in_=wx_words.rearrange("a p b -> p a b").bitcast(I32))
-        spread_scales(1)
-        load_x(0, 0, whole, late_at(X_ROWS_AT))
-        wt_rows = [[wt_first[u][:] for u in range(2)], [wt_second[:, :, piece(u)] for u in range(2)]]
+        for index, (a, u) in enumerate(((0, 0), (0, 1), (1, 0))):
+            load_x(0, a, u, late_at(X_ROWS_AT + 4 * KIB * index))
+        wt_rows = [wt_first, wt_second]
 
         codes = {}
         planes = {}
@@ -180,7 +179,7 @@ def tile_list_tiert_gelu_kernel(
 
         def round_wt(a, u, make_tile=sb):
             woven[("q", a, u)] = make_tile([P, PIECE, PACK], BF16, "q_woven%d%d" % (a, u))
-            weave_on_scalar(woven[("q", a, u)][:], wt_rows[a][u])
+            weave_on_scalar(woven[("q", a, u)][:], wt_rows[a][u][:])
 
         def quantize_tier(tier, a, u, make_tile):
             codes[(tier, a, u)] = make_tile([P, PIECE], U32, "%s_codes%d%d" % (tier, a, u))
@@ -212,7 +211,7 @@ def tile_list_tiert_gelu_kernel(
         def left_over(a, m):
             u = m // 2
             if ("r", a, u) not in woven:
-                make_tile = early_at(LEFT_OVER0_AT + 2 * KIB * u) if a == 0 else (early_at(SECOND_WOVEN_AT + 3 * KIB), late_at(X_WOVEN_AT))[u]
+                make_tile = early_at(LEFT_OVER0_AT + 2 * KIB * u) if a == 0 else (early_at(SECOND_WOVEN_AT + 3 * KIB), late_at(X_WOVEN_AT + 6 * KIB))[u]
                 woven[("r", a, u)] = make_tile([P, PIECE, PACK], BF16, "r_woven%d%d" % (a, u))
             nc.vector.tensor_tensor(
                 out=walk_woven(woven[("r", a, u)][:, within_piece(m), :]),
@@ -246,16 +245,19 @@ def tile_list_tiert_gelu_kernel(
         x_codes = {}
         x_plane = {}
 
-        def round_x(h, a, columns, weave, make_tile):
-            key = (h, a, columns.start)
-            x_woven[key] = make_tile([P, columns.stop - columns.start, PACK], BF16, "x_woven%d%d_%d" % key)
-            weave(x_woven[key][:], x_rows[key][:])
+        def round_x(h, a, u, weave, make_tile, pieces):
+            if (h, a, u) not in x_woven:
+                tile = make_tile([P, PIECE * pieces, PACK], BF16, "x_woven%d%d%d" % (h, a, u))
+                for i in range(pieces):
+                    x_woven[(h, a, u + i)] = (tile, piece(i))
+            tile, columns = x_woven[(h, a, u)]
+            weave(tile[:, columns, :], x_rows[(h, a, u)][:])
 
         def quantize_x(h, a, columns, make_tile):
             if (h, a) not in x_codes:
                 x_codes[(h, a)] = make_tile([P, HALF], U32, "x_codes%d%d" % (h, a))
                 x_plane[(h, a)] = moving_plane(HALF, "x_plane%d%d" % (h, a), PASSES * (1 + h) + a)
-            quantize(x_codes[(h, a)][:, columns], x_plane[(h, a)][:, columns], x_woven[(h, a, columns.start)][:])
+            quantize(x_codes[(h, a)][:, columns], x_plane[(h, a)][:, columns], x_woven[(h, a, columns.start // PIECE)][0][:])
 
         acc = {}
 
@@ -290,7 +292,7 @@ def tile_list_tiert_gelu_kernel(
 
         def finish(h, m):
             total, columns = acc[(h, m)]
-            make_tile = early_at(THIRD_ROWS_AT + 4 * HALF * m) if h == 0 else sb
+            make_tile = early_at(FOURTH_ROWS_AT - KIB + 4 * HALF * m) if h == 0 and m < 3 else sb
             result = make_tile([P, columns.stop - columns.start], F32, "result%d%d_%d" % (h, m, columns.start))
             nc.scalar.activation(out=result[:], in_=total[:], func=ACT.Gelu_apprx_tanh, bias=bias[:, 8 * m : 8 * m + 1])
             nc.sync.dma_start(
@@ -308,8 +310,8 @@ def tile_list_tiert_gelu_kernel(
                 in_=wx_scales[:, 4 * q : 4 * q + 4, :].rearrange("a r n -> r a n").bitcast(I32),
             )
         quantize_tier("q", 0, 1, early_at(EYE_AT + KIB))
-        load_x(0, 1, whole, early_at(SECOND_ROWS_AT))
-        load_x(1, 0, whole, early_at(THIRD_ROWS_AT))
+        load_x(0, 1, 1, early_at(THIRD_ROWS_AT - 4 * KIB))
+        load_x(1, 0, 0, early_at(THIRD_ROWS_AT))
         for m in range(TILES):
             bring_back(0, m, TILES + m)
         def keep_warm(index, weights, weights_plane):
@@ -325,91 +327,94 @@ def tile_list_tiert_gelu_kernel(
 
         for m in range(TILES):
             left_over(0, m)
-            if m > 0:
-                keep_warm(TILES + m, *tier_tile("q", 0, m))
+            keep_warm(TILES + m, *tier_tile("q", 0, m))
+        load_x(1, 0, 1, early_at(FOURTH_ROWS_AT))
         for u in range(2):
-            load_x(1, 1, piece(u), early_at(LAST_ROWS_AT + 4 * KIB * u))
-        quantize_tier("r", 0, 0, sb)
-        keep_warm(7, *tier_tile("r", 0, 0))
+            load_x(1, 1, u, early_at(LAST_ROWS_AT + 4 * KIB * u))
 
         for m in range(TILES):
             open_sum(0, m, m, whole)
-        for m in range(2):
-            open_sum(1, m, TILES + m, whole)
 
-        def first_passes(quarter, tiles):
+        def first_passes(u):
             for tier in ("q", "r"):
-                for m in tiles:
-                    table_pass(quarter // 2, m, tier, 0, piece(quarter % 2))
+                for m in range(TILES):
+                    table_pass(0, m, tier, 0, piece(u))
 
-        pick_words(piece(0), WT_FIRST_AT + 6 * KIB)
-        quantize_tier("r", 0, 1, sb)
-        keep_warm(7, *tier_tile("r", 0, 2))
+        second_half = slice(HALF, J)
+        pick_words(piece(0), WT_FIRST_AT[0])
+        quantize_tier("r", 0, 0, sb)
+        keep_warm(7, *tier_tile("r", 0, 0))
         part_words(piece(0), 0)
-        first_passes(0, range(TILES))
-        pick_words(piece(1), LEFT_OVER0_AT + 2 * KIB)
+        quantize_tier("r", 0, 1, sb)
+        first_passes(0)
+        pick_words(piece(1), LEFT_OVER0_AT)
         part_words(piece(0), 1)
         part_words(piece(1), 0)
-        first_passes(1, range(TILES))
-        pick_words(piece(2), WT_FIRST_AT + 6 * KIB)
+        first_passes(1)
         part_words(piece(1), 1)
-        part_words(piece(2), 0)
-        first_passes(2, range(2))
 
         for u in range(2):
             round_wt(1, u, early_at(SECOND_WOVEN_AT + 2 * KIB * u))
         for h, a in ((0, 0), (0, 1), (1, 0)):
-            round_x(h, a, whole, weave_on_scalar, late_at(X_WOVEN_AT + 4 * KIB * (PASSES * h + a)))
-        pick_words(piece(3), LEFT_OVER0_AT + 2 * KIB + KIB // 2)
-        quantize_tier("q", 1, 0, early_at(LEFT_OVER0_AT + KIB + KIB // 2))
-        part_words(piece(3), 0)
-        quantize_tier("q", 1, 1, early_at(WINDOW_AT))
+            for u in range(2):
+                round_x(h, a, u, weave_on_scalar, late_at(X_WOVEN_AT + 4 * KIB * (PASSES * h + a)), 2)
+        quantize_tier("q", 1, 0, early_at(WT_FIRST_AT[0]))
+        quantize_tier("q", 1, 1, early_at(LEFT_OVER0_AT))
+        pick_words(second_half, SECOND_WOVEN_AT + KIB)
         for m in range(2):
             bring_back(1, m, 6 + m)
-            left_over(1, m)
+        left_over(1, 0)
+        part_words(second_half, 0)
+        left_over(1, 1)
         for m in range(TILES):
             table_pass(0, m, "q", 1)
         bring_back(1, 2, 6)
-        first_passes(3, range(2))
+        for m in range(2):
+            open_sum(1, m, TILES + m, whole)
+            for tier in ("q", "r"):
+                table_pass(1, m, tier, 0)
         bring_back(1, 3, 7)
-        quantize_tier("r", 1, 0, sb)
         quantize_x(0, 0, whole, sb)
-        for m in range(2, TILES):
-            left_over(1, m)
+        quantize_tier("r", 1, 0, sb)
+        part_words(second_half, 1, late_at(WT_SECOND_AT))
+        quantize_x(0, 1, whole, late_at(X_WOVEN_AT))
         bias = early_at(WINDOW_AT + 2 * KIB)([P, BLOCK], F32, "bias")
         nc.vector.transpose(out=bias[:], in_=bias_runs[:])
-        quantize_x(0, 1, whole, late_at(X_WOVEN_AT + 2 * KIB))
-        quantize_tier("r", 1, 1, late_at(X_WOVEN_AT + 4 * KIB))
-        round_x(1, 1, piece(0), weave_on_vector, late_at(X_WOVEN_AT + 5 * KIB))
-        for quarter in (2, 3):
-            part_words(piece(quarter), 1, late_at(X_WOVEN_AT))
-        round_x(1, 1, piece(1), weave_on_vector, early_at(LAST_ROWS_AT))
-        for u in range(2):
-            quantize_x(1, 1, piece(u), sb)
+        for m in range(2, TILES):
+            left_over(1, m)
         quantize_x(1, 0, whole, sb)
+        quantize_tier("r", 1, 1, sb)
+        round_x(1, 1, 0, weave_on_vector, late_at(X_WOVEN_AT + 6 * KIB), 1)
+        round_x(1, 1, 1, weave_on_vector, early_at(LAST_ROWS_AT), 1)
+        for u in range(2):
+            quantize_x(1, 1, piece(u), late_at(X_WOVEN_AT + 8 * KIB))
 
-        for m in range(2):
-            table_pass(0, m, "r", 1)
         for m in range(TILES):
             token_pass(0, m, 0)
-        open_sum(1, 2, 6, whole)
+        for m in range(2):
+            table_pass(0, m, "r", 1)
+        for m in range(2):
+            token_pass(0, m, 1)
+            finish(0, m)
         for tier in ("q", "r"):
-            table_pass(1, 2, tier, 0)
-        for m in range(TILES):
-            if m >= 2:
-                table_pass(0, m, "r", 1)
+            for m in range(2):
+                table_pass(1, m, tier, 1)
+        open_sum(1, 2, 6, whole)
+        for tier, a in (("q", 0), ("r", 0), ("q", 1)):
+            table_pass(1, 2, tier, a)
+        for m in range(2, TILES):
+            table_pass(0, m, "r", 1)
             token_pass(0, m, 1)
             finish(0, m)
 
+        table_pass(1, 2, "r", 1)
         for m in range(3):
-            for tier in ("q", "r"):
-                table_pass(1, m, tier, 1)
+            token_pass(1, m, 0)
         for m in range(3):
-            for a in range(PASSES):
-                token_pass(1, m, a)
+            token_pass(1, m, 1)
             finish(1, m)
         for u in range(2):
-            open_sum(1, 3, TILES + u, piece(u))
+            open_sum(1, 3, TILES - 1 + u, piece(u))
             for a in range(PASSES):
                 for tier in ("q", "r"):
                     table_pass(1, 3, tier, a)

@@ -32,7 +32,7 @@ KIB = 1024
 WINDOW_AT = 0
 LAST_ROWS_AT = WINDOW_AT + 16 * KIB
 WT_FIRST_AT = (LAST_ROWS_AT + 10 * KIB, LAST_ROWS_AT + 2 * KIB)
-FOURTH_ROWS_AT = WT_FIRST_AT[0] + 2 * KIB
+FOURTH_ROWS_AT = WT_FIRST_AT[0] + 3 * KIB
 LEFT_OVER0_AT = FOURTH_ROWS_AT + 7 * KIB
 SECOND_WOVEN_AT = LEFT_OVER0_AT + 5 * KIB
 THIRD_ROWS_AT = SECOND_WOVEN_AT + 9 * KIB
@@ -42,7 +42,7 @@ WT_SECOND_AT = 0
 WX_AT = WT_SECOND_AT + 8 * KIB
 X_ROWS_AT = WX_AT + 2 * KIB
 X_WOVEN_AT = X_ROWS_AT + 12 * KIB
-WX_PLANE_AT = X_WOVEN_AT + 16 * KIB
+ON_WINDOW_AT = X_WOVEN_AT + 16 * KIB
 
 FLOPS = 2 * N * J * (2 * K + L) + 2 * K_PASS * K * N
 
@@ -127,9 +127,6 @@ def tile_list_tiert_gelu_kernel(
                 out=eye_woven[:].rearrange("p (t c) -> p t c", t=PACK),
                 in_=eye_run[:].bitcast(BF16)[:, 1 : EYE_RUN + 1].rearrange("p (o c) -> p o c", o=1).to_broadcast([P, PACK, EYE_RUN]),
             )
-            tab_plane = [moving_plane(J, "tab_plane%d" % a, a) for a in range(PASSES)]
-            for a in range(PASSES):
-                nc.vector.memset(tab_plane[a][:].bitcast(I32), 0)
             bias_runs = sb([P, BLOCK], F32, "bias_runs")
             nc.vector.memset(bias_runs[:], 0.0)
             nc.sync.dma_start(out=bias_runs[0:P:8, :], in_=b.rearrange("(m g c) -> g m c", m=TILES, g=QUADRANTS))
@@ -143,6 +140,12 @@ def tile_list_tiert_gelu_kernel(
 
         def late_at(offset):
             return lambda shape, dtype, name: late.tile(shape, dtype, name=name, align_bytes=256, offset=offset)
+
+        tab_plane = [
+            late.tile([P, J], U8, name="tab_plane%d" % a, align_bytes=128, offset=ON_WINDOW_AT + 128 + KIB * a)
+            for a in range(PASSES)
+        ]
+        wx_plane = late_at(ON_WINDOW_AT + 3 * KIB)([P, PASSES, N], U8, "wx_plane")
 
         def spread_scales(a):
             for q in range(QUADRANTS):
@@ -169,8 +172,14 @@ def tile_list_tiert_gelu_kernel(
         spread_scales(1)
         wx_codes = late_at(WX_AT)([P, PASSES, 2 * N], U8, "wx_codes")
         nc.sync.dma_start(out=wx_codes[:].bitcast(I32), in_=wx_words.rearrange("a p b -> p a b").bitcast(I32))
-        for index, (a, u) in enumerate(((0, 0), (0, 1), (1, 0))):
-            load_x(0, a, u, late_at(X_ROWS_AT + 4 * KIB * index))
+        for u in range(2):
+            load_x(0, 0, u, late_at(X_ROWS_AT + 4 * KIB * u))
+        for q in range(QUADRANTS):
+            nc.sync.dma_start(
+                out=wx_plane[32 * q : 32 * q + 4, :, :].bitcast(I32),
+                in_=wx_scales[:, 4 * q : 4 * q + 4, :].rearrange("a r n -> r a n").bitcast(I32),
+            )
+        load_x(0, 1, 0, late_at(X_ROWS_AT + 8 * KIB))
         wt_rows = [wt_first, wt_second]
 
         codes = {}
@@ -211,7 +220,7 @@ def tile_list_tiert_gelu_kernel(
         def left_over(a, m):
             u = m // 2
             if ("r", a, u) not in woven:
-                make_tile = early_at(LEFT_OVER0_AT + 2 * KIB * u) if a == 0 else (early_at(SECOND_WOVEN_AT + 3 * KIB), late_at(X_WOVEN_AT + 6 * KIB))[u]
+                make_tile = early_at(LEFT_OVER0_AT + 2 * KIB * u) if a == 0 else (early_at(SECOND_WOVEN_AT + 3 * KIB), late_at(X_WOVEN_AT))[u]
                 woven[("r", a, u)] = make_tile([P, PIECE, PACK], BF16, "r_woven%d%d" % (a, u))
             nc.vector.tensor_tensor(
                 out=walk_woven(woven[("r", a, u)][:, within_piece(m), :]),
@@ -261,8 +270,11 @@ def tile_list_tiert_gelu_kernel(
 
         acc = {}
 
-        def open_sum(h, m, index, columns):
+        opening_pass = {}
+
+        def open_sum(h, m, index, columns, first=("q", 0)):
             acc[(h, m)] = (bank(index, [P, columns.stop - columns.start], "acc%d%d_%d" % (h, m, columns.start)), columns)
+            opening_pass[(h, m)] = first
 
         def table_pass(h, m, tier, a, columns=None):
             total, span = acc[(h, m)]
@@ -274,7 +286,7 @@ def tile_list_tiert_gelu_kernel(
                 lhsT_scale=weights_plane,
                 rhs=tab_codes[(h, a)][:, 2 * columns.start : 2 * columns.stop].bitcast(FP4X4),
                 rhs_scale=tab_plane[a][:, HALF * h + columns.start : HALF * h + columns.stop],
-                start=(tier, a, columns.start) == ("q", 0, span.start),
+                start=(tier, a) == opening_pass[(h, m)] and columns.start == span.start,
                 stop=False,
             )
 
@@ -290,25 +302,25 @@ def tile_list_tiert_gelu_kernel(
                 stop=(a == PASSES - 1),
             )
 
+        first_results = {}
+
         def finish(h, m):
             total, columns = acc[(h, m)]
-            make_tile = early_at(FOURTH_ROWS_AT - KIB + 4 * HALF * m) if h == 0 and m < 3 else sb
-            result = make_tile([P, columns.stop - columns.start], F32, "result%d%d_%d" % (h, m, columns.start))
-            nc.scalar.activation(out=result[:], in_=total[:], func=ACT.Gelu_apprx_tanh, bias=bias[:, 8 * m : 8 * m + 1])
+            if h == 0:
+                if m // 2 not in first_results:
+                    make_tile = early_at(FOURTH_ROWS_AT - 2 * KIB + 4 * KIB * (m // 2))
+                    first_results[m // 2] = make_tile([P, 2 * HALF], F32, "first_results%d" % (m // 2))
+                result = first_results[m // 2][:, HALF * (m % 2) : HALF * (m % 2 + 1)]
+            else:
+                result = sb([P, columns.stop - columns.start], F32, "result%d_%d" % (m, columns.start))[:]
+            nc.scalar.activation(out=result, in_=total[:], func=ACT.Gelu_apprx_tanh, bias=bias[:, 8 * m : 8 * m + 1])
             nc.sync.dma_start(
-                out=out[P * m : P * (m + 1), HALF * h + columns.start : HALF * h + columns.stop], in_=result[:]
+                out=out[P * m : P * (m + 1), HALF * h + columns.start : HALF * h + columns.stop], in_=result
             )
 
         round_wt(0, 0)
         round_wt(0, 1, early_at(THIRD_ROWS_AT - KIB))
         quantize_tier("q", 0, 0, early_at(EYE_AT))
-        wx_plane = late_at(WX_PLANE_AT)([P, PASSES, N], U8, "wx_plane")
-        nc.vector.memset(wx_plane[:].rearrange("p a n -> p (a n)").bitcast(I32), 0)
-        for q in range(QUADRANTS):
-            nc.sync.dma_start(
-                out=wx_plane[32 * q : 32 * q + 4, :, :].bitcast(I32),
-                in_=wx_scales[:, 4 * q : 4 * q + 4, :].rearrange("a r n -> r a n").bitcast(I32),
-            )
         quantize_tier("q", 0, 1, early_at(EYE_AT + KIB))
         load_x(0, 1, 1, early_at(THIRD_ROWS_AT - 4 * KIB))
         load_x(1, 0, 0, early_at(THIRD_ROWS_AT))
@@ -327,7 +339,8 @@ def tile_list_tiert_gelu_kernel(
 
         for m in range(TILES):
             left_over(0, m)
-            keep_warm(TILES + m, *tier_tile("q", 0, m))
+            if m >= 2:
+                keep_warm(TILES + m, *tier_tile("q", 0, m))
         load_x(1, 0, 1, early_at(FOURTH_ROWS_AT))
         for u in range(2):
             load_x(1, 1, u, early_at(LAST_ROWS_AT + 4 * KIB * u))
@@ -341,17 +354,18 @@ def tile_list_tiert_gelu_kernel(
                     table_pass(0, m, tier, 0, piece(u))
 
         second_half = slice(HALF, J)
-        pick_words(piece(0), WT_FIRST_AT[0])
         quantize_tier("r", 0, 0, sb)
-        keep_warm(7, *tier_tile("r", 0, 0))
+        for m in range(2):
+            keep_warm(7, *tier_tile("r", 0, m))
+        pick_words(piece(0), WT_FIRST_AT[0])
+        quantize_tier("r", 0, 1, early_at(LEFT_OVER0_AT + KIB))
+        keep_warm(7, *tier_tile("r", 0, 2))
         part_words(piece(0), 0)
-        quantize_tier("r", 0, 1, sb)
         first_passes(0)
-        pick_words(piece(1), LEFT_OVER0_AT)
+        pick_words(piece(1), LEFT_OVER0_AT + 2 * KIB)
         part_words(piece(0), 1)
         part_words(piece(1), 0)
         first_passes(1)
-        part_words(piece(1), 1)
 
         for u in range(2):
             round_wt(1, u, early_at(SECOND_WOVEN_AT + 2 * KIB * u))
@@ -359,32 +373,32 @@ def tile_list_tiert_gelu_kernel(
             for u in range(2):
                 round_x(h, a, u, weave_on_scalar, late_at(X_WOVEN_AT + 4 * KIB * (PASSES * h + a)), 2)
         quantize_tier("q", 1, 0, early_at(WT_FIRST_AT[0]))
-        quantize_tier("q", 1, 1, early_at(LEFT_OVER0_AT))
-        pick_words(second_half, SECOND_WOVEN_AT + KIB)
+        part_words(piece(1), 1)
+        pick_words(second_half, SECOND_WOVEN_AT)
+        quantize_tier("q", 1, 1, early_at(LEFT_OVER0_AT + 2 * KIB))
         for m in range(2):
             bring_back(1, m, 6 + m)
-        left_over(1, 0)
         part_words(second_half, 0)
-        left_over(1, 1)
+        for m in range(2):
+            left_over(1, m)
         for m in range(TILES):
             table_pass(0, m, "q", 1)
-        bring_back(1, 2, 6)
         for m in range(2):
             open_sum(1, m, TILES + m, whole)
             for tier in ("q", "r"):
                 table_pass(1, m, tier, 0)
-        bring_back(1, 3, 7)
+            bring_back(1, 2 + m, 6 + m)
         quantize_x(0, 0, whole, sb)
         quantize_tier("r", 1, 0, sb)
         part_words(second_half, 1, late_at(WT_SECOND_AT))
-        quantize_x(0, 1, whole, late_at(X_WOVEN_AT))
         bias = early_at(WINDOW_AT + 2 * KIB)([P, BLOCK], F32, "bias")
         nc.vector.transpose(out=bias[:], in_=bias_runs[:])
         for m in range(2, TILES):
             left_over(1, m)
-        quantize_x(1, 0, whole, sb)
-        quantize_tier("r", 1, 1, sb)
+        quantize_x(0, 1, whole, late_at(X_WOVEN_AT + 2 * KIB))
+        quantize_tier("r", 1, 1, late_at(X_WOVEN_AT + 4 * KIB))
         round_x(1, 1, 0, weave_on_vector, late_at(X_WOVEN_AT + 6 * KIB), 1)
+        quantize_x(1, 0, whole, sb)
         round_x(1, 1, 1, weave_on_vector, early_at(LAST_ROWS_AT), 1)
         for u in range(2):
             quantize_x(1, 1, piece(u), late_at(X_WOVEN_AT + 8 * KIB))
@@ -393,21 +407,20 @@ def tile_list_tiert_gelu_kernel(
             token_pass(0, m, 0)
         for m in range(2):
             table_pass(0, m, "r", 1)
-        for m in range(2):
-            token_pass(0, m, 1)
-            finish(0, m)
         for tier in ("q", "r"):
             for m in range(2):
                 table_pass(1, m, tier, 1)
-        open_sum(1, 2, 6, whole)
-        for tier, a in (("q", 0), ("r", 0), ("q", 1)):
-            table_pass(1, 2, tier, a)
+        for m in range(2):
+            token_pass(0, m, 1)
+            finish(0, m)
         for m in range(2, TILES):
             table_pass(0, m, "r", 1)
             token_pass(0, m, 1)
             finish(0, m)
 
-        table_pass(1, 2, "r", 1)
+        open_sum(1, 2, 6, whole, ("r", 1))
+        for tier, a in (("r", 1), ("q", 1), ("r", 0), ("q", 0)):
+            table_pass(1, 2, tier, a)
         for m in range(3):
             token_pass(1, m, 0)
         for m in range(3):

@@ -36,7 +36,8 @@ FOURTH_ROWS_AT = WT_FIRST_AT[0] + 3 * KIB
 LEFT_OVER0_AT = FOURTH_ROWS_AT + 7 * KIB
 SECOND_WOVEN_AT = LEFT_OVER0_AT + 5 * KIB
 THIRD_ROWS_AT = SECOND_WOVEN_AT + 9 * KIB
-EYE_AT = THIRD_ROWS_AT + 4 * KIB
+BIAS_RUNS_AT = THIRD_ROWS_AT + 4 * KIB
+EYE_AT = BIAS_RUNS_AT + KIB
 PLANES_AT = EYE_AT + 5 * KIB + 128
 WT_SECOND_AT = 0
 WX_AT = WT_SECOND_AT + 8 * KIB
@@ -127,7 +128,7 @@ def tile_list_tiert_gelu_kernel(
                 out=eye_woven[:].rearrange("p (t c) -> p t c", t=PACK),
                 in_=eye_run[:].bitcast(BF16)[:, 1 : EYE_RUN + 1].rearrange("p (o c) -> p o c", o=1).to_broadcast([P, PACK, EYE_RUN]),
             )
-            bias_runs = sb([P, BLOCK], F32, "bias_runs")
+            bias_runs = early_at(BIAS_RUNS_AT)([P, BLOCK], F32, "bias_runs")
             nc.vector.memset(bias_runs[:], 0.0)
             nc.sync.dma_start(out=bias_runs[0:P:8, :], in_=b.rearrange("(m g c) -> g m c", m=TILES, g=QUADRANTS))
             eye_codes = sb([P, K_PASS], U32, "eye_codes")
@@ -270,11 +271,13 @@ def tile_list_tiert_gelu_kernel(
 
         acc = {}
 
-        opening_pass = {}
+        first_pass = {}
+        last_pass = {}
 
-        def open_sum(h, m, index, columns, first=("q", 0)):
+        def open_sum(h, m, index, columns, first=("q", 0), last=("x", 1)):
             acc[(h, m)] = (bank(index, [P, columns.stop - columns.start], "acc%d%d_%d" % (h, m, columns.start)), columns)
-            opening_pass[(h, m)] = first
+            first_pass[(h, m)] = first
+            last_pass[(h, m)] = last
 
         def table_pass(h, m, tier, a, columns=None):
             total, span = acc[(h, m)]
@@ -286,8 +289,8 @@ def tile_list_tiert_gelu_kernel(
                 lhsT_scale=weights_plane,
                 rhs=tab_codes[(h, a)][:, 2 * columns.start : 2 * columns.stop].bitcast(FP4X4),
                 rhs_scale=tab_plane[a][:, HALF * h + columns.start : HALF * h + columns.stop],
-                start=(tier, a) == opening_pass[(h, m)] and columns.start == span.start,
-                stop=False,
+                start=(tier, a) == first_pass[(h, m)] and columns.start == span.start,
+                stop=(tier, a) == last_pass[(h, m)],
             )
 
         def token_pass(h, m, a):
@@ -298,8 +301,8 @@ def tile_list_tiert_gelu_kernel(
                 lhsT_scale=wx_plane[:, a, P * m : P * (m + 1)],
                 rhs=x_codes[(h, a)][:, columns].bitcast(FP8X4),
                 rhs_scale=x_plane[(h, a)][:, columns],
-                start=False,
-                stop=(a == PASSES - 1),
+                start=("x", a) == first_pass[(h, m)],
+                stop=("x", a) == last_pass[(h, m)],
             )
 
         first_results = {}
@@ -355,14 +358,15 @@ def tile_list_tiert_gelu_kernel(
 
         second_half = slice(HALF, J)
         quantize_tier("r", 0, 0, sb)
-        for m in range(2):
-            keep_warm(7, *tier_tile("r", 0, m))
-        pick_words(piece(0), WT_FIRST_AT[0])
-        quantize_tier("r", 0, 1, early_at(LEFT_OVER0_AT + KIB))
-        keep_warm(7, *tier_tile("r", 0, 2))
+        quantize_tier("r", 0, 1, sb)
+        for m in range(1, TILES):
+            keep_warm(7, *tier_tile("r", 0, 2 + m % 2))
+        pick_words(piece(0), LEFT_OVER0_AT)
+        bias = early_at(LEFT_OVER0_AT + 3 * KIB)([P, BLOCK], F32, "bias")
+        nc.vector.transpose(out=bias[:], in_=bias_runs[:])
         part_words(piece(0), 0)
         first_passes(0)
-        pick_words(piece(1), LEFT_OVER0_AT + 2 * KIB)
+        pick_words(piece(1), BIAS_RUNS_AT)
         part_words(piece(0), 1)
         part_words(piece(1), 0)
         first_passes(1)
@@ -372,10 +376,10 @@ def tile_list_tiert_gelu_kernel(
         for h, a in ((0, 0), (0, 1), (1, 0)):
             for u in range(2):
                 round_x(h, a, u, weave_on_scalar, late_at(X_WOVEN_AT + 4 * KIB * (PASSES * h + a)), 2)
-        quantize_tier("q", 1, 0, early_at(WT_FIRST_AT[0]))
+        quantize_tier("q", 1, 0, early_at(LEFT_OVER0_AT))
         part_words(piece(1), 1)
         pick_words(second_half, SECOND_WOVEN_AT)
-        quantize_tier("q", 1, 1, early_at(LEFT_OVER0_AT + 2 * KIB))
+        quantize_tier("q", 1, 1, early_at(BIAS_RUNS_AT))
         for m in range(2):
             bring_back(1, m, 6 + m)
         part_words(second_half, 0)
@@ -389,19 +393,16 @@ def tile_list_tiert_gelu_kernel(
                 table_pass(1, m, tier, 0)
             bring_back(1, 2 + m, 6 + m)
         quantize_x(0, 0, whole, sb)
-        quantize_tier("r", 1, 0, sb)
-        part_words(second_half, 1, late_at(WT_SECOND_AT))
-        bias = early_at(WINDOW_AT + 2 * KIB)([P, BLOCK], F32, "bias")
-        nc.vector.transpose(out=bias[:], in_=bias_runs[:])
+        quantize_tier("r", 1, 0, late_at(X_WOVEN_AT + 2 * KIB))
+        part_words(second_half, 1, late_at(X_WOVEN_AT + 3 * KIB))
         for m in range(2, TILES):
             left_over(1, m)
-        quantize_x(0, 1, whole, late_at(X_WOVEN_AT + 2 * KIB))
+        quantize_x(0, 1, whole, sb)
         quantize_tier("r", 1, 1, late_at(X_WOVEN_AT + 4 * KIB))
-        round_x(1, 1, 0, weave_on_vector, late_at(X_WOVEN_AT + 6 * KIB), 1)
+        round_x(1, 1, 0, weave_on_vector, late_at(X_WOVEN_AT + 12 * KIB), 2)
         quantize_x(1, 0, whole, sb)
-        round_x(1, 1, 1, weave_on_vector, early_at(LAST_ROWS_AT), 1)
-        for u in range(2):
-            quantize_x(1, 1, piece(u), late_at(X_WOVEN_AT + 8 * KIB))
+        round_x(1, 1, 1, weave_on_vector, None, 2)
+        quantize_x(1, 1, whole, late_at(X_WOVEN_AT + 8 * KIB))
 
         for m in range(TILES):
             token_pass(0, m, 0)
@@ -426,11 +427,11 @@ def tile_list_tiert_gelu_kernel(
         for m in range(3):
             token_pass(1, m, 1)
             finish(1, m)
-        for u in range(2):
-            open_sum(1, 3, TILES - 1 + u, piece(u))
-            for a in range(PASSES):
-                for tier in ("q", "r"):
-                    table_pass(1, 3, tier, a)
-            for a in range(PASSES):
+        for u, index in enumerate((7, 0)):
+            open_sum(1, 3, index, piece(u), ("x", 1), ("r", 1))
+            for a in reversed(range(PASSES)):
                 token_pass(1, 3, a)
+            for tier in ("q", "r"):
+                for a in range(PASSES):
+                    table_pass(1, 3, tier, a)
             finish(1, 3)

@@ -36,8 +36,7 @@ FOURTH_ROWS_AT = WT_FIRST_AT[0] + 3 * KIB
 LEFT_OVER0_AT = FOURTH_ROWS_AT + 7 * KIB
 SECOND_WOVEN_AT = LEFT_OVER0_AT + 5 * KIB
 THIRD_ROWS_AT = SECOND_WOVEN_AT + 9 * KIB
-BIAS_RUNS_AT = THIRD_ROWS_AT + 4 * KIB
-EYE_AT = BIAS_RUNS_AT + KIB
+EYE_AT = THIRD_ROWS_AT + 4 * KIB
 PLANES_AT = EYE_AT + 5 * KIB + 128
 WT_SECOND_AT = 0
 WX_AT = WT_SECOND_AT + 8 * KIB
@@ -128,7 +127,7 @@ def tile_list_tiert_gelu_kernel(
                 out=eye_woven[:].rearrange("p (t c) -> p t c", t=PACK),
                 in_=eye_run[:].bitcast(BF16)[:, 1 : EYE_RUN + 1].rearrange("p (o c) -> p o c", o=1).to_broadcast([P, PACK, EYE_RUN]),
             )
-            bias_runs = early_at(BIAS_RUNS_AT)([P, BLOCK], F32, "bias_runs")
+            bias_runs = sb([P, BLOCK], F32, "bias_runs")
             nc.vector.memset(bias_runs[:], 0.0)
             nc.sync.dma_start(out=bias_runs[0:P:8, :], in_=b.rearrange("(m g c) -> g m c", m=TILES, g=QUADRANTS))
             eye_codes = sb([P, K_PASS], U32, "eye_codes")
@@ -342,7 +341,7 @@ def tile_list_tiert_gelu_kernel(
 
         for m in range(TILES):
             left_over(0, m)
-            if m >= 2:
+            if m >= 1:
                 keep_warm(TILES + m, *tier_tile("q", 0, m))
         load_x(1, 0, 1, early_at(FOURTH_ROWS_AT))
         for u in range(2):
@@ -358,15 +357,13 @@ def tile_list_tiert_gelu_kernel(
 
         second_half = slice(HALF, J)
         quantize_tier("r", 0, 0, sb)
-        quantize_tier("r", 0, 1, sb)
-        for m in range(1, TILES):
-            keep_warm(7, *tier_tile("r", 0, 2 + m % 2))
-        pick_words(piece(0), LEFT_OVER0_AT)
-        bias = early_at(LEFT_OVER0_AT + 3 * KIB)([P, BLOCK], F32, "bias")
-        nc.vector.transpose(out=bias[:], in_=bias_runs[:])
+        keep_warm(7, *tier_tile("r", 0, 0))
+        pick_words(piece(0), WT_FIRST_AT[0])
+        quantize_tier("r", 0, 1, early_at(LEFT_OVER0_AT + KIB))
+        keep_warm(7, *tier_tile("r", 0, 2))
         part_words(piece(0), 0)
         first_passes(0)
-        pick_words(piece(1), BIAS_RUNS_AT)
+        pick_words(piece(1), LEFT_OVER0_AT + 2 * KIB)
         part_words(piece(0), 1)
         part_words(piece(1), 0)
         first_passes(1)
@@ -376,10 +373,10 @@ def tile_list_tiert_gelu_kernel(
         for h, a in ((0, 0), (0, 1), (1, 0)):
             for u in range(2):
                 round_x(h, a, u, weave_on_scalar, late_at(X_WOVEN_AT + 4 * KIB * (PASSES * h + a)), 2)
-        quantize_tier("q", 1, 0, early_at(LEFT_OVER0_AT))
+        quantize_tier("q", 1, 0, early_at(WT_FIRST_AT[0]))
         part_words(piece(1), 1)
         pick_words(second_half, SECOND_WOVEN_AT)
-        quantize_tier("q", 1, 1, early_at(BIAS_RUNS_AT))
+        quantize_tier("q", 1, 1, early_at(LEFT_OVER0_AT + 2 * KIB))
         for m in range(2):
             bring_back(1, m, 6 + m)
         part_words(second_half, 0)
@@ -392,6 +389,8 @@ def tile_list_tiert_gelu_kernel(
             for tier in ("q", "r"):
                 table_pass(1, m, tier, 0)
             bring_back(1, 2 + m, 6 + m)
+        bias = late_at(WT_SECOND_AT)([P, BLOCK], F32, "bias")
+        nc.vector.transpose(out=bias[:], in_=bias_runs[:])
         quantize_x(0, 0, whole, sb)
         quantize_tier("r", 1, 0, late_at(X_WOVEN_AT + 2 * KIB))
         part_words(second_half, 1, late_at(X_WOVEN_AT + 3 * KIB))
@@ -427,8 +426,8 @@ def tile_list_tiert_gelu_kernel(
         for m in range(3):
             token_pass(1, m, 1)
             finish(1, m)
-        for u, index in enumerate((7, 0)):
-            open_sum(1, 3, index, piece(u), ("x", 1), ("r", 1))
+        for columns, index in ((slice(0, 256), 7), (slice(256, 384), 0), (slice(384, 512), 1)):
+            open_sum(1, 3, index, columns, ("x", 1), ("r", 1))
             for a in reversed(range(PASSES)):
                 token_pass(1, 3, a)
             for tier in ("q", "r"):

@@ -30,18 +30,14 @@ EYE_RUN = K_PASS + 1
 KIB = 1024
 
 WINDOW_AT = 0
-LAST_ROWS_AT = WINDOW_AT + 16 * KIB
-WT_FIRST_AT = (LAST_ROWS_AT + 10 * KIB, LAST_ROWS_AT + 2 * KIB)
-FOURTH_ROWS_AT = WT_FIRST_AT[0] + 3 * KIB
-LEFT_OVER0_AT = FOURTH_ROWS_AT + 7 * KIB
-SECOND_WOVEN_AT = LEFT_OVER0_AT + 5 * KIB
-THIRD_ROWS_AT = SECOND_WOVEN_AT + 9 * KIB
-EYE_AT = THIRD_ROWS_AT + 4 * KIB
+WT_AT = WINDOW_AT + 16 * KIB
+Q_WOVEN_AT = WT_AT + 32 * KIB
+R_WOVEN_AT = Q_WOVEN_AT + 16 * KIB
+EYE_AT = R_WOVEN_AT + 16 * KIB
 PLANES_AT = EYE_AT + 5 * KIB + 128
-WT_SECOND_AT = 0
-WX_AT = WT_SECOND_AT + 8 * KIB
+WX_AT = 0
 X_ROWS_AT = WX_AT + 2 * KIB
-X_WOVEN_AT = X_ROWS_AT + 12 * KIB
+X_WOVEN_AT = X_ROWS_AT + 36 * KIB
 ON_WINDOW_AT = X_WOVEN_AT + 16 * KIB
 
 FLOPS = 2 * N * J * (2 * K + L) + 2 * K_PASS * K * N
@@ -104,9 +100,13 @@ def tile_list_tiert_gelu_kernel(
             nc.sync.dma_start(
                 out=scale_window[SCALE_ROW0:P, :].bitcast(I32), in_=tab_scales.rearrange("a q t -> (a q) t").bitcast(I32)
             )
-            wt_first = [early_at(WT_FIRST_AT[u])([P, PACK, PIECE], F32, "wt_first%d" % u) for u in range(2)]
-            for u in range(2):
-                nc.sync.dma_start(out=wt_first[u][:], in_=wt_by_pass[0][:, :, piece(u)])
+            wt_rows = [
+                [early_at(WT_AT + 8 * KIB * (2 * a + u))([P, PACK, PIECE], F32, "wt_rows%d%d" % (a, u)) for u in range(2)]
+                for a in range(PASSES)
+            ]
+            for a in range(PASSES):
+                for u in range(2):
+                    nc.sync.dma_start(out=wt_rows[a][u][:], in_=wt_by_pass[a][:, :, piece(u)])
             word_window = early_at(WINDOW_AT)([P, T], I32, "word_window")
             nc.sync.dma_start(out=word_window[:], in_=tab_words[0].rearrange("p t b -> p (t b)").bitcast(I32))
 
@@ -127,7 +127,7 @@ def tile_list_tiert_gelu_kernel(
                 out=eye_woven[:].rearrange("p (t c) -> p t c", t=PACK),
                 in_=eye_run[:].bitcast(BF16)[:, 1 : EYE_RUN + 1].rearrange("p (o c) -> p o c", o=1).to_broadcast([P, PACK, EYE_RUN]),
             )
-            bias_runs = sb([P, BLOCK], F32, "bias_runs")
+            bias_runs = early_at(EYE_AT - KIB)([P, BLOCK], F32, "bias_runs")
             nc.vector.memset(bias_runs[:], 0.0)
             nc.sync.dma_start(out=bias_runs[0:P:8, :], in_=b.rearrange("(m g c) -> g m c", m=TILES, g=QUADRANTS))
             eye_codes = sb([P, K_PASS], U32, "eye_codes")
@@ -164,30 +164,39 @@ def tile_list_tiert_gelu_kernel(
                 in_=x[K_PASS * a : K_PASS * (a + 1), j0 : j0 + PIECE].rearrange("(p t) j -> p t j", t=PACK),
             )
 
+        def x_rows_at(h, a, u):
+            return X_ROWS_AT + 4 * KIB * (4 * h + 2 * a + u) + 2 * KIB * (4 * h + 2 * a + u >= 5) + 2 * KIB * (4 * h + 2 * a + u >= 6)
+
         whole = slice(0, HALF)
         spread_scales(0)
-        wt_second = [late_at(WT_SECOND_AT + 4 * KIB * u)([P, PACK, PIECE], F32, "wt_second%d" % u) for u in range(2)]
         for u in range(2):
-            nc.sync.dma_start(out=wt_second[u][:], in_=wt_by_pass[1][:, :, piece(u)])
+            load_x(0, 0, u, late_at(x_rows_at(0, 0, u)))
         spread_scales(1)
         wx_codes = late_at(WX_AT)([P, PASSES, 2 * N], U8, "wx_codes")
         nc.sync.dma_start(out=wx_codes[:].bitcast(I32), in_=wx_words.rearrange("a p b -> p a b").bitcast(I32))
         for u in range(2):
-            load_x(0, 0, u, late_at(X_ROWS_AT + 4 * KIB * u))
+            load_x(0, 1, u, late_at(x_rows_at(0, 1, u)))
         for q in range(QUADRANTS):
             nc.sync.dma_start(
                 out=wx_plane[32 * q : 32 * q + 4, :, :].bitcast(I32),
                 in_=wx_scales[:, 4 * q : 4 * q + 4, :].rearrange("a r n -> r a n").bitcast(I32),
             )
-        load_x(0, 1, 0, late_at(X_ROWS_AT + 8 * KIB))
-        wt_rows = [wt_first, wt_second]
+        for a in range(PASSES):
+            for u in range(2):
+                load_x(1, a, u, late_at(x_rows_at(1, a, u)))
 
         codes = {}
         planes = {}
         woven = {}
 
-        def round_wt(a, u, make_tile=sb):
-            woven[("q", a, u)] = make_tile([P, PIECE, PACK], BF16, "q_woven%d%d" % (a, u))
+        def q_woven_at(a, u):
+            return Q_WOVEN_AT + 4 * KIB * (2 * a + u)
+
+        def r_woven_at(a, u):
+            return R_WOVEN_AT + 4 * KIB * (2 * a + u)
+
+        def round_wt(a, u):
+            woven[("q", a, u)] = early_at(q_woven_at(a, u))([P, PIECE, PACK], BF16, "q_woven%d%d" % (a, u))
             weave_on_scalar(woven[("q", a, u)][:], wt_rows[a][u][:])
 
         def quantize_tier(tier, a, u, make_tile):
@@ -217,10 +226,10 @@ def tile_list_tiert_gelu_kernel(
                     stop=True,
                 )
 
-        def left_over(a, m):
+        def left_over(a, m, make_tile=None):
             u = m // 2
             if ("r", a, u) not in woven:
-                make_tile = early_at(LEFT_OVER0_AT + 2 * KIB * u) if a == 0 else (early_at(SECOND_WOVEN_AT + 3 * KIB), late_at(X_WOVEN_AT))[u]
+                make_tile = make_tile or early_at(r_woven_at(a, u))
                 woven[("r", a, u)] = make_tile([P, PIECE, PACK], BF16, "r_woven%d%d" % (a, u))
             nc.vector.tensor_tensor(
                 out=walk_woven(woven[("r", a, u)][:, within_piece(m), :]),
@@ -310,7 +319,7 @@ def tile_list_tiert_gelu_kernel(
             total, columns = acc[(h, m)]
             if h == 0:
                 if m // 2 not in first_results:
-                    make_tile = early_at(FOURTH_ROWS_AT - 2 * KIB + 4 * KIB * (m // 2))
+                    make_tile = late_at(x_rows_at(1, 0, 1) - 2 * KIB + 4 * KIB * (m // 2))
                     first_results[m // 2] = make_tile([P, 2 * HALF], F32, "first_results%d" % (m // 2))
                 result = first_results[m // 2][:, HALF * (m % 2) : HALF * (m % 2 + 1)]
             else:
@@ -320,32 +329,29 @@ def tile_list_tiert_gelu_kernel(
                 out=out[P * m : P * (m + 1), HALF * h + columns.start : HALF * h + columns.stop], in_=result
             )
 
-        round_wt(0, 0)
-        round_wt(0, 1, early_at(THIRD_ROWS_AT - KIB))
-        quantize_tier("q", 0, 0, early_at(EYE_AT))
-        quantize_tier("q", 0, 1, early_at(EYE_AT + KIB))
-        load_x(0, 1, 1, early_at(THIRD_ROWS_AT - 4 * KIB))
-        load_x(1, 0, 0, early_at(THIRD_ROWS_AT))
-        for m in range(TILES):
-            bring_back(0, m, TILES + m)
-        def keep_warm(index, weights, weights_plane):
-            nc.tensor.matmul_mx(
-                out=bank(index, [P, HALF], "warm")[:],
-                lhsT=weights,
-                lhsT_scale=weights_plane,
-                rhs=eye_codes[:].bitcast(FP8X4),
-                rhs_scale=eye_plane[:],
-                start=True,
-                stop=True,
-            )
-
-        for m in range(TILES):
-            left_over(0, m)
-            if m >= 1:
-                keep_warm(TILES + m, *tier_tile("q", 0, m))
-        load_x(1, 0, 1, early_at(FOURTH_ROWS_AT))
+        for a in range(PASSES):
+            for u in range(2):
+                round_wt(a, u)
+        for h, a in ((0, 0), (0, 1), (1, 0)):
+            for u in range(2):
+                round_x(h, a, u, weave_on_scalar, late_at(X_WOVEN_AT + 4 * KIB * (PASSES * h + a)), 2)
         for u in range(2):
-            load_x(1, 1, u, early_at(LAST_ROWS_AT + 4 * KIB * u))
+            quantize_tier("q", 0, u, early_at(EYE_AT + KIB * u))
+        for m in range(TILES):
+            bring_back(0, m, m)
+        for m in range(2):
+            left_over(0, m)
+        quantize_tier("q", 1, 0, early_at(q_woven_at(0, 1)))
+        for m in range(2):
+            bring_back(1, m, TILES + m)
+        for m in range(2, TILES):
+            left_over(0, m)
+        for u in range(2):
+            quantize_tier("r", 0, u, early_at(WT_AT + 8 * KIB * u))
+        left_over(1, 0, early_at(r_woven_at(0, 0)))
+        quantize_tier("q", 1, 1, early_at(r_woven_at(0, 1) + KIB))
+        for m in range(2, TILES):
+            bring_back(1, m, TILES + m)
 
         for m in range(TILES):
             open_sum(0, m, m, whole)
@@ -356,46 +362,32 @@ def tile_list_tiert_gelu_kernel(
                     table_pass(0, m, tier, 0, piece(u))
 
         second_half = slice(HALF, J)
-        quantize_tier("r", 0, 0, sb)
-        keep_warm(7, *tier_tile("r", 0, 0))
-        pick_words(piece(0), WT_FIRST_AT[0])
-        quantize_tier("r", 0, 1, early_at(LEFT_OVER0_AT + KIB))
-        keep_warm(7, *tier_tile("r", 0, 2))
+        pick_words(piece(0), r_woven_at(0, 1))
+        bias = early_at(q_woven_at(1, 1))([P, BLOCK], F32, "bias")
+        nc.vector.transpose(out=bias[:], in_=bias_runs[:])
         part_words(piece(0), 0)
         first_passes(0)
-        pick_words(piece(1), LEFT_OVER0_AT + 2 * KIB)
+        pick_words(piece(1), EYE_AT - KIB)
         part_words(piece(0), 1)
         part_words(piece(1), 0)
         first_passes(1)
-
-        for u in range(2):
-            round_wt(1, u, early_at(SECOND_WOVEN_AT + 2 * KIB * u))
-        for h, a in ((0, 0), (0, 1), (1, 0)):
-            for u in range(2):
-                round_x(h, a, u, weave_on_scalar, late_at(X_WOVEN_AT + 4 * KIB * (PASSES * h + a)), 2)
-        quantize_tier("q", 1, 0, early_at(WT_FIRST_AT[0]))
         part_words(piece(1), 1)
-        pick_words(second_half, SECOND_WOVEN_AT)
-        quantize_tier("q", 1, 1, early_at(LEFT_OVER0_AT + 2 * KIB))
-        for m in range(2):
-            bring_back(1, m, 6 + m)
-        part_words(second_half, 0)
-        for m in range(2):
-            left_over(1, m)
+        left_over(1, 1)
         for m in range(TILES):
             table_pass(0, m, "q", 1)
+        pick_words(second_half, EYE_AT - 2 * KIB)
+        quantize_tier("r", 1, 0, early_at(WT_AT + 16 * KIB))
+        part_words(second_half, 0, early_at(r_woven_at(0, 0)))
+        for m in range(2):
+            table_pass(0, m, "r", 1)
         for m in range(2):
             open_sum(1, m, TILES + m, whole)
             for tier in ("q", "r"):
                 table_pass(1, m, tier, 0)
-            bring_back(1, 2 + m, 6 + m)
-        bias = late_at(WT_SECOND_AT)([P, BLOCK], F32, "bias")
-        nc.vector.transpose(out=bias[:], in_=bias_runs[:])
         quantize_x(0, 0, whole, sb)
-        quantize_tier("r", 1, 0, late_at(X_WOVEN_AT + 2 * KIB))
-        part_words(second_half, 1, late_at(X_WOVEN_AT + 3 * KIB))
+        part_words(second_half, 1, late_at(X_WOVEN_AT + 2 * KIB))
         for m in range(2, TILES):
-            left_over(1, m)
+            left_over(1, m, late_at(X_WOVEN_AT))
         quantize_x(0, 1, whole, sb)
         quantize_tier("r", 1, 1, late_at(X_WOVEN_AT + 4 * KIB))
         round_x(1, 1, 0, weave_on_vector, late_at(X_WOVEN_AT + 12 * KIB), 2)
@@ -405,16 +397,12 @@ def tile_list_tiert_gelu_kernel(
 
         for m in range(TILES):
             token_pass(0, m, 0)
-        for m in range(2):
-            table_pass(0, m, "r", 1)
         for tier in ("q", "r"):
             for m in range(2):
                 table_pass(1, m, tier, 1)
-        for m in range(2):
-            token_pass(0, m, 1)
-            finish(0, m)
-        for m in range(2, TILES):
-            table_pass(0, m, "r", 1)
+        for m in range(TILES):
+            if m >= 2:
+                table_pass(0, m, "r", 1)
             token_pass(0, m, 1)
             finish(0, m)
 

@@ -35,7 +35,9 @@ Q_WOVEN_AT = WT_AT + 32 * KIB
 R_WOVEN_AT = Q_WOVEN_AT + 16 * KIB
 EYE_AT = R_WOVEN_AT + 16 * KIB
 PLANES_AT = EYE_AT + 5 * KIB + 128
-WX_AT = 0
+LAST_WT_AT = 0
+BIAS_RUNS_AT = LAST_WT_AT + 4 * KIB
+WX_AT = BIAS_RUNS_AT + KIB
 X_ROWS_AT = WX_AT + 2 * KIB
 X_WOVEN_AT = X_ROWS_AT + 36 * KIB
 ON_WINDOW_AT = X_WOVEN_AT + 16 * KIB
@@ -100,13 +102,20 @@ def tile_list_tiert_gelu_kernel(
             nc.sync.dma_start(
                 out=scale_window[SCALE_ROW0:P, :].bitcast(I32), in_=tab_scales.rearrange("a q t -> (a q) t").bitcast(I32)
             )
-            wt_rows = [
-                [early_at(WT_AT + 8 * KIB * (2 * a + u))([P, PACK, PIECE], F32, "wt_rows%d%d" % (a, u)) for u in range(2)]
-                for a in range(PASSES)
-            ]
-            for a in range(PASSES):
-                for u in range(2):
-                    nc.sync.dma_start(out=wt_rows[a][u][:], in_=wt_by_pass[a][:, :, piece(u)])
+            wt_rows = {}
+
+            def load_wt(a, u, make_tile):
+                wt_rows[(a, u)] = make_tile([P, PACK, PIECE], F32, "wt_rows%d%d" % (a, u))
+                nc.sync.dma_start(out=wt_rows[(a, u)][:], in_=wt_by_pass[a][:, :, piece(u)])
+
+            for a, u in ((0, 0), (0, 1), (1, 0)):
+                load_wt(a, u, early_at(WT_AT + 8 * KIB * (2 * a + u)))
+            wx_plane = sb([P, PASSES, N], U8, "wx_plane")
+            for q in range(QUADRANTS):
+                nc.sync.dma_start(
+                    out=wx_plane[32 * q : 32 * q + 4, :, :].bitcast(I32),
+                    in_=wx_scales[:, 4 * q : 4 * q + 4, :].rearrange("a r n -> r a n").bitcast(I32),
+                )
             word_window = early_at(WINDOW_AT)([P, T], I32, "word_window")
             nc.sync.dma_start(out=word_window[:], in_=tab_words[0].rearrange("p t b -> p (t b)").bitcast(I32))
 
@@ -127,9 +136,6 @@ def tile_list_tiert_gelu_kernel(
                 out=eye_woven[:].rearrange("p (t c) -> p t c", t=PACK),
                 in_=eye_run[:].bitcast(BF16)[:, 1 : EYE_RUN + 1].rearrange("p (o c) -> p o c", o=1).to_broadcast([P, PACK, EYE_RUN]),
             )
-            bias_runs = early_at(EYE_AT - KIB)([P, BLOCK], F32, "bias_runs")
-            nc.vector.memset(bias_runs[:], 0.0)
-            nc.sync.dma_start(out=bias_runs[0:P:8, :], in_=b.rearrange("(m g c) -> g m c", m=TILES, g=QUADRANTS))
             eye_codes = sb([P, K_PASS], U32, "eye_codes")
             eye_plane = sb([P, K_PASS], U8, "eye_plane")
             nc.vector.quantize_mx(out=eye_codes[:].bitcast(FP8X4), scales=eye_plane[:], in_=eye_woven[:, : PACK * K_PASS])
@@ -145,7 +151,6 @@ def tile_list_tiert_gelu_kernel(
             late.tile([P, J], U8, name="tab_plane%d" % a, align_bytes=128, offset=ON_WINDOW_AT + 128 + KIB * a)
             for a in range(PASSES)
         ]
-        wx_plane = late_at(ON_WINDOW_AT + 3 * KIB)([P, PASSES, N], U8, "wx_plane")
 
         def spread_scales(a):
             for q in range(QUADRANTS):
@@ -169,6 +174,7 @@ def tile_list_tiert_gelu_kernel(
 
         whole = slice(0, HALF)
         spread_scales(0)
+        load_wt(1, 1, late_at(LAST_WT_AT))
         for u in range(2):
             load_x(0, 0, u, late_at(x_rows_at(0, 0, u)))
         spread_scales(1)
@@ -176,11 +182,9 @@ def tile_list_tiert_gelu_kernel(
         nc.sync.dma_start(out=wx_codes[:].bitcast(I32), in_=wx_words.rearrange("a p b -> p a b").bitcast(I32))
         for u in range(2):
             load_x(0, 1, u, late_at(x_rows_at(0, 1, u)))
-        for q in range(QUADRANTS):
-            nc.sync.dma_start(
-                out=wx_plane[32 * q : 32 * q + 4, :, :].bitcast(I32),
-                in_=wx_scales[:, 4 * q : 4 * q + 4, :].rearrange("a r n -> r a n").bitcast(I32),
-            )
+        bias_runs = late_at(BIAS_RUNS_AT)([P, BLOCK], F32, "bias_runs")
+        nc.vector.memset(bias_runs[:], 0.0)
+        nc.sync.dma_start(out=bias_runs[0:P:8, :], in_=b.rearrange("(m g c) -> g m c", m=TILES, g=QUADRANTS))
         for a in range(PASSES):
             for u in range(2):
                 load_x(1, a, u, late_at(x_rows_at(1, a, u)))
@@ -197,7 +201,7 @@ def tile_list_tiert_gelu_kernel(
 
         def round_wt(a, u):
             woven[("q", a, u)] = early_at(q_woven_at(a, u))([P, PIECE, PACK], BF16, "q_woven%d%d" % (a, u))
-            weave_on_scalar(woven[("q", a, u)][:], wt_rows[a][u][:])
+            weave_on_scalar(woven[("q", a, u)][:], wt_rows[(a, u)][:])
 
         def quantize_tier(tier, a, u, make_tile):
             codes[(tier, a, u)] = make_tile([P, PIECE], U32, "%s_codes%d%d" % (tier, a, u))
@@ -233,7 +237,7 @@ def tile_list_tiert_gelu_kernel(
                 woven[("r", a, u)] = make_tile([P, PIECE, PACK], BF16, "r_woven%d%d" % (a, u))
             nc.vector.tensor_tensor(
                 out=walk_woven(woven[("r", a, u)][:, within_piece(m), :]),
-                in0=walk_rows(wt_rows[a][u][:, :, within_piece(m)]),
+                in0=walk_rows(wt_rows[(a, u)][:, :, within_piece(m)]),
                 in1=walk_rows(back[(a, m)][:]),
                 op=ALU.subtract,
             )
@@ -344,14 +348,25 @@ def tile_list_tiert_gelu_kernel(
         quantize_tier("q", 1, 0, early_at(q_woven_at(0, 1)))
         for m in range(2):
             bring_back(1, m, TILES + m)
+
+        def keep_warm(index, weights, weights_plane):
+            nc.tensor.matmul_mx(
+                out=bank(index, [P, HALF], "warm")[:],
+                lhsT=weights,
+                lhsT_scale=weights_plane,
+                rhs=eye_codes[:].bitcast(FP8X4),
+                rhs_scale=eye_plane[:],
+                start=True,
+                stop=True,
+            )
+
         for m in range(2, TILES):
             left_over(0, m)
-        for u in range(2):
-            quantize_tier("r", 0, u, early_at(WT_AT + 8 * KIB * u))
-        left_over(1, 0, early_at(r_woven_at(0, 0)))
-        quantize_tier("q", 1, 1, early_at(r_woven_at(0, 1) + KIB))
-        for m in range(2, TILES):
-            bring_back(1, m, TILES + m)
+            keep_warm(m, *tier_tile("q", 0, m))
+        quantize_tier("r", 0, 0, early_at(WT_AT))
+        keep_warm(6, *tier_tile("r", 0, 0))
+        left_over(1, 0, early_at(WT_AT + 8 * KIB))
+        keep_warm(4, *tier_tile("q", 1, 0))
 
         for m in range(TILES):
             open_sum(0, m, m, whole)
@@ -362,32 +377,33 @@ def tile_list_tiert_gelu_kernel(
                     table_pass(0, m, tier, 0, piece(u))
 
         second_half = slice(HALF, J)
-        pick_words(piece(0), r_woven_at(0, 1))
-        bias = early_at(q_woven_at(1, 1))([P, BLOCK], F32, "bias")
-        nc.vector.transpose(out=bias[:], in_=bias_runs[:])
+        pick_words(piece(0), r_woven_at(0, 0))
+        quantize_tier("r", 0, 1, early_at(r_woven_at(0, 0) + KIB))
+        keep_warm(6, *tier_tile("r", 0, 2))
         part_words(piece(0), 0)
         first_passes(0)
-        pick_words(piece(1), EYE_AT - KIB)
+        pick_words(piece(1), r_woven_at(0, 1))
         part_words(piece(0), 1)
         part_words(piece(1), 0)
         first_passes(1)
+        quantize_tier("q", 1, 1, early_at(r_woven_at(0, 0)))
+        for m in range(2, TILES):
+            bring_back(1, m, TILES + m)
         part_words(piece(1), 1)
         left_over(1, 1)
         for m in range(TILES):
             table_pass(0, m, "q", 1)
-        pick_words(second_half, EYE_AT - 2 * KIB)
-        quantize_tier("r", 1, 0, early_at(WT_AT + 16 * KIB))
-        part_words(second_half, 0, early_at(r_woven_at(0, 0)))
+        pick_words(second_half, q_woven_at(1, 1))
+        quantize_tier("r", 1, 0, early_at(WINDOW_AT))
         for m in range(2):
             table_pass(0, m, "r", 1)
-        for m in range(2):
-            open_sum(1, m, TILES + m, whole)
-            for tier in ("q", "r"):
-                table_pass(1, m, tier, 0)
-        quantize_x(0, 0, whole, sb)
-        part_words(second_half, 1, late_at(X_WOVEN_AT + 2 * KIB))
+        quantize_x(0, 0, whole, early_at(WINDOW_AT + 2 * KIB))
+        for a in range(PASSES):
+            part_words(second_half, a, late_at(X_WOVEN_AT + (2 + a) * KIB))
         for m in range(2, TILES):
             left_over(1, m, late_at(X_WOVEN_AT))
+        bias = late_at(LAST_WT_AT)([P, BLOCK], F32, "bias")
+        nc.vector.transpose(out=bias[:], in_=bias_runs[:])
         quantize_x(0, 1, whole, sb)
         quantize_tier("r", 1, 1, late_at(X_WOVEN_AT + 4 * KIB))
         round_x(1, 1, 0, weave_on_vector, late_at(X_WOVEN_AT + 12 * KIB), 2)
@@ -397,9 +413,12 @@ def tile_list_tiert_gelu_kernel(
 
         for m in range(TILES):
             token_pass(0, m, 0)
-        for tier in ("q", "r"):
+        for m in range(2):
+            open_sum(1, m, TILES + m, whole)
+        for a in range(PASSES):
             for m in range(2):
-                table_pass(1, m, tier, 1)
+                for tier in ("q", "r"):
+                    table_pass(1, m, tier, a)
         for m in range(TILES):
             if m >= 2:
                 table_pass(0, m, "r", 1)

@@ -40,7 +40,7 @@ BIAS_RUNS_AT = LAST_WT_AT + 4 * KIB
 WX_AT = BIAS_RUNS_AT + KIB
 X_ROWS_AT = WX_AT + 2 * KIB
 X_WOVEN_AT = X_ROWS_AT + 36 * KIB
-ON_WINDOW_AT = X_WOVEN_AT + 16 * KIB
+TAB_PLANES_AT = X_WOVEN_AT + 16 * KIB + 128
 
 FLOPS = 2 * N * J * (2 * K + L) + 2 * K_PASS * K * N
 
@@ -134,7 +134,10 @@ def tile_list_tiert_gelu_kernel(
             eye_woven = early_at(EYE_AT)([P, PACK * EYE_RUN], BF16, "eye_woven")
             nc.vector.tensor_copy(
                 out=eye_woven[:].rearrange("p (t c) -> p t c", t=PACK),
-                in_=eye_run[:].bitcast(BF16)[:, 1 : EYE_RUN + 1].rearrange("p (o c) -> p o c", o=1).to_broadcast([P, PACK, EYE_RUN]),
+                in_=eye_run[:]
+                .bitcast(BF16)[:, 1 : EYE_RUN + 1]
+                .rearrange("p (o c) -> p o c", o=1)
+                .to_broadcast([P, PACK, EYE_RUN]),
             )
             eye_codes = sb([P, K_PASS], U32, "eye_codes")
             eye_plane = sb([P, K_PASS], U8, "eye_plane")
@@ -148,7 +151,7 @@ def tile_list_tiert_gelu_kernel(
             return lambda shape, dtype, name: late.tile(shape, dtype, name=name, align_bytes=256, offset=offset)
 
         tab_plane = [
-            late.tile([P, J], U8, name="tab_plane%d" % a, align_bytes=128, offset=ON_WINDOW_AT + 128 + KIB * a)
+            late.tile([P, J], U8, name="tab_plane%d" % a, align_bytes=128, offset=TAB_PLANES_AT + KIB * a)
             for a in range(PASSES)
         ]
 
@@ -170,7 +173,8 @@ def tile_list_tiert_gelu_kernel(
             )
 
         def x_rows_at(h, a, u):
-            return X_ROWS_AT + 4 * KIB * (4 * h + 2 * a + u) + 2 * KIB * (4 * h + 2 * a + u >= 5) + 2 * KIB * (4 * h + 2 * a + u >= 6)
+            index = 4 * h + 2 * a + u
+            return X_ROWS_AT + 4 * KIB * index + 2 * KIB * min(2, max(0, index - 4))
 
         whole = slice(0, HALF)
         spread_scales(0)
@@ -230,6 +234,17 @@ def tile_list_tiert_gelu_kernel(
                     stop=True,
                 )
 
+        def keep_warm(index, weights, weights_plane):
+            nc.tensor.matmul_mx(
+                out=bank(index, [P, HALF], "warm")[:],
+                lhsT=weights,
+                lhsT_scale=weights_plane,
+                rhs=eye_codes[:].bitcast(FP8X4),
+                rhs_scale=eye_plane[:],
+                start=True,
+                stop=True,
+            )
+
         def left_over(a, m, make_tile=None):
             u = m // 2
             if ("r", a, u) not in woven:
@@ -267,22 +282,17 @@ def tile_list_tiert_gelu_kernel(
         x_codes = {}
         x_plane = {}
 
-        def round_x(h, a, u, weave, make_tile, pieces):
-            if (h, a, u) not in x_woven:
-                tile = make_tile([P, PIECE * pieces, PACK], BF16, "x_woven%d%d%d" % (h, a, u))
-                for i in range(pieces):
-                    x_woven[(h, a, u + i)] = (tile, piece(i))
-            tile, columns = x_woven[(h, a, u)]
-            weave(tile[:, columns, :], x_rows[(h, a, u)][:])
+        def round_x(h, a, u, weave, offset):
+            if (h, a) not in x_woven:
+                x_woven[(h, a)] = late_at(offset)([P, HALF, PACK], BF16, "x_woven%d%d" % (h, a))
+            weave(x_woven[(h, a)][:, piece(u), :], x_rows[(h, a, u)][:])
 
-        def quantize_x(h, a, columns, make_tile):
-            if (h, a) not in x_codes:
-                x_codes[(h, a)] = make_tile([P, HALF], U32, "x_codes%d%d" % (h, a))
-                x_plane[(h, a)] = moving_plane(HALF, "x_plane%d%d" % (h, a), PASSES * (1 + h) + a)
-            quantize(x_codes[(h, a)][:, columns], x_plane[(h, a)][:, columns], x_woven[(h, a, columns.start // PIECE)][0][:])
+        def quantize_x(h, a, make_tile):
+            x_codes[(h, a)] = make_tile([P, HALF], U32, "x_codes%d%d" % (h, a))
+            x_plane[(h, a)] = moving_plane(HALF, "x_plane%d%d" % (h, a), PASSES * (1 + h) + a)
+            quantize(x_codes[(h, a)][:], x_plane[(h, a)][:], x_woven[(h, a)][:])
 
         acc = {}
-
         first_pass = {}
         last_pass = {}
 
@@ -338,7 +348,8 @@ def tile_list_tiert_gelu_kernel(
                 round_wt(a, u)
         for h, a in ((0, 0), (0, 1), (1, 0)):
             for u in range(2):
-                round_x(h, a, u, weave_on_scalar, late_at(X_WOVEN_AT + 4 * KIB * (PASSES * h + a)), 2)
+                round_x(h, a, u, weave_on_scalar, X_WOVEN_AT + 4 * KIB * (PASSES * h + a))
+
         for u in range(2):
             quantize_tier("q", 0, u, early_at(EYE_AT + KIB * u))
         for m in range(TILES):
@@ -348,25 +359,14 @@ def tile_list_tiert_gelu_kernel(
         quantize_tier("q", 1, 0, early_at(q_woven_at(0, 1)))
         for m in range(2):
             bring_back(1, m, TILES + m)
-
-        def keep_warm(index, weights, weights_plane):
-            nc.tensor.matmul_mx(
-                out=bank(index, [P, HALF], "warm")[:],
-                lhsT=weights,
-                lhsT_scale=weights_plane,
-                rhs=eye_codes[:].bitcast(FP8X4),
-                rhs_scale=eye_plane[:],
-                start=True,
-                stop=True,
-            )
-
         for m in range(2, TILES):
             left_over(0, m)
             keep_warm(m, *tier_tile("q", 0, m))
         quantize_tier("r", 0, 0, early_at(WT_AT))
         keep_warm(6, *tier_tile("r", 0, 0))
         left_over(1, 0, early_at(WT_AT + 8 * KIB))
-        keep_warm(4, *tier_tile("q", 1, 0))
+        for m in range(2):
+            keep_warm(4, *tier_tile("q", 1, m))
 
         for m in range(TILES):
             open_sum(0, m, m, whole)
@@ -379,13 +379,13 @@ def tile_list_tiert_gelu_kernel(
         second_half = slice(HALF, J)
         pick_words(piece(0), r_woven_at(0, 0))
         quantize_tier("r", 0, 1, early_at(r_woven_at(0, 0) + KIB))
-        keep_warm(6, *tier_tile("r", 0, 2))
         part_words(piece(0), 0)
         first_passes(0)
         pick_words(piece(1), r_woven_at(0, 1))
         part_words(piece(0), 1)
         part_words(piece(1), 0)
         first_passes(1)
+
         quantize_tier("q", 1, 1, early_at(r_woven_at(0, 0)))
         for m in range(2, TILES):
             bring_back(1, m, TILES + m)
@@ -393,23 +393,23 @@ def tile_list_tiert_gelu_kernel(
         left_over(1, 1)
         for m in range(TILES):
             table_pass(0, m, "q", 1)
-        pick_words(second_half, q_woven_at(1, 1))
-        quantize_tier("r", 1, 0, early_at(WINDOW_AT))
+        pick_words(second_half, q_woven_at(1, 1) + KIB // 2)
+        quantize_tier("r", 1, 0, early_at(q_woven_at(1, 1) - KIB // 2))
         for m in range(2):
             table_pass(0, m, "r", 1)
-        quantize_x(0, 0, whole, early_at(WINDOW_AT + 2 * KIB))
+        quantize_x(0, 0, sb)
         for a in range(PASSES):
             part_words(second_half, a, late_at(X_WOVEN_AT + (2 + a) * KIB))
         for m in range(2, TILES):
             left_over(1, m, late_at(X_WOVEN_AT))
         bias = late_at(LAST_WT_AT)([P, BLOCK], F32, "bias")
         nc.vector.transpose(out=bias[:], in_=bias_runs[:])
-        quantize_x(0, 1, whole, sb)
+        quantize_x(0, 1, sb)
         quantize_tier("r", 1, 1, late_at(X_WOVEN_AT + 4 * KIB))
-        round_x(1, 1, 0, weave_on_vector, late_at(X_WOVEN_AT + 12 * KIB), 2)
-        quantize_x(1, 0, whole, sb)
-        round_x(1, 1, 1, weave_on_vector, None, 2)
-        quantize_x(1, 1, whole, late_at(X_WOVEN_AT + 8 * KIB))
+        round_x(1, 1, 0, weave_on_vector, X_WOVEN_AT + 12 * KIB)
+        quantize_x(1, 0, sb)
+        round_x(1, 1, 1, weave_on_vector, X_WOVEN_AT + 12 * KIB)
+        quantize_x(1, 1, late_at(X_WOVEN_AT + 8 * KIB))
 
         for m in range(TILES):
             token_pass(0, m, 0)

@@ -31,14 +31,15 @@ KIB = 1024
 
 WINDOW_AT = 0
 WT_AT = WINDOW_AT + 16 * KIB
-Q_WOVEN_AT = WT_AT + 32 * KIB
-R_WOVEN_AT = Q_WOVEN_AT + 16 * KIB
-EYE_AT = R_WOVEN_AT + 16 * KIB
+Q_WOVEN_AT = WT_AT + 8 * KIB
+R_WOVEN_AT = Q_WOVEN_AT + 17 * KIB
+EYE_AT = R_WOVEN_AT + 10 * KIB
 PLANES_AT = EYE_AT + 5 * KIB + 128
-LAST_WT_AT = 0
-BIAS_RUNS_AT = LAST_WT_AT + 4 * KIB
+LATE_WT_AT = 0
+BIAS_RUNS_AT = LATE_WT_AT + 8 * KIB
 WX_AT = BIAS_RUNS_AT + KIB
-X_ROWS_AT = WX_AT + 2 * KIB
+WX_PLANE_AT = WX_AT + 2 * KIB
+X_ROWS_AT = WX_PLANE_AT + KIB
 X_WOVEN_AT = X_ROWS_AT + 36 * KIB
 TAB_PLANES_AT = X_WOVEN_AT + 16 * KIB + 128
 
@@ -108,14 +109,8 @@ def tile_list_tiert_gelu_kernel(
                 wt_rows[(a, u)] = make_tile([P, PACK, PIECE], F32, "wt_rows%d%d" % (a, u))
                 nc.sync.dma_start(out=wt_rows[(a, u)][:], in_=wt_by_pass[a][:, :, piece(u)])
 
-            for a, u in ((0, 0), (0, 1), (1, 0)):
-                load_wt(a, u, early_at(WT_AT + 8 * KIB * (2 * a + u)))
-            wx_plane = sb([P, PASSES, N], U8, "wx_plane")
-            for q in range(QUADRANTS):
-                nc.sync.dma_start(
-                    out=wx_plane[32 * q : 32 * q + 4, :, :].bitcast(I32),
-                    in_=wx_scales[:, 4 * q : 4 * q + 4, :].rearrange("a r n -> r a n").bitcast(I32),
-                )
+            for a in range(PASSES):
+                load_wt(a, 0, early_at(WT_AT + 4 * KIB * a))
             word_window = early_at(WINDOW_AT)([P, T], I32, "word_window")
             nc.sync.dma_start(out=word_window[:], in_=tab_words[0].rearrange("p t b -> p (t b)").bitcast(I32))
 
@@ -164,50 +159,57 @@ def tile_list_tiert_gelu_kernel(
 
         x_rows = {}
 
-        def load_x(h, a, u, make_tile):
-            x_rows[(h, a, u)] = make_tile([P, PACK, PIECE], F32, "x_rows%d%d%d" % (h, a, u))
+        def x_rows_at(h, a, u):
+            index = 4 * h + 2 * a + u
+            return X_ROWS_AT + 4 * KIB * index + 2 * KIB * min(2, max(0, index - 4))
+
+        def load_x(h, a, u):
+            x_rows[(h, a, u)] = late_at(x_rows_at(h, a, u))([P, PACK, PIECE], F32, "x_rows%d%d%d" % (h, a, u))
             j0 = HALF * h + PIECE * u
             nc.sync.dma_start(
                 out=x_rows[(h, a, u)][:],
                 in_=x[K_PASS * a : K_PASS * (a + 1), j0 : j0 + PIECE].rearrange("(p t) j -> p t j", t=PACK),
             )
 
-        def x_rows_at(h, a, u):
-            index = 4 * h + 2 * a + u
-            return X_ROWS_AT + 4 * KIB * index + 2 * KIB * min(2, max(0, index - 4))
-
         whole = slice(0, HALF)
         spread_scales(0)
-        load_wt(1, 1, late_at(LAST_WT_AT))
-        for u in range(2):
-            load_x(0, 0, u, late_at(x_rows_at(0, 0, u)))
+        for a in range(PASSES):
+            load_wt(a, 1, late_at(LATE_WT_AT + 4 * KIB * a))
         spread_scales(1)
         wx_codes = late_at(WX_AT)([P, PASSES, 2 * N], U8, "wx_codes")
         nc.sync.dma_start(out=wx_codes[:].bitcast(I32), in_=wx_words.rearrange("a p b -> p a b").bitcast(I32))
         for u in range(2):
-            load_x(0, 1, u, late_at(x_rows_at(0, 1, u)))
+            load_x(0, 0, u)
+        wx_plane = late_at(WX_PLANE_AT)([P, PASSES, N], U8, "wx_plane")
+        for q in range(QUADRANTS):
+            nc.sync.dma_start(
+                out=wx_plane[32 * q : 32 * q + 4, :, :].bitcast(I32),
+                in_=wx_scales[:, 4 * q : 4 * q + 4, :].rearrange("a r n -> r a n").bitcast(I32),
+            )
+        for u in range(2):
+            load_x(0, 1, u)
         bias_runs = late_at(BIAS_RUNS_AT)([P, BLOCK], F32, "bias_runs")
         nc.vector.memset(bias_runs[:], 0.0)
         nc.sync.dma_start(out=bias_runs[0:P:8, :], in_=b.rearrange("(m g c) -> g m c", m=TILES, g=QUADRANTS))
         for a in range(PASSES):
             for u in range(2):
-                load_x(1, a, u, late_at(x_rows_at(1, a, u)))
+                load_x(1, a, u)
 
         codes = {}
         planes = {}
         woven = {}
 
         def q_woven_at(a, u):
-            return Q_WOVEN_AT + 4 * KIB * (2 * a + u)
+            return Q_WOVEN_AT + 4 * KIB * (2 * u + a)
 
         def r_woven_at(a, u):
-            return R_WOVEN_AT + 4 * KIB * (2 * a + u)
+            return R_WOVEN_AT + 2 * KIB * (2 * u + a)
 
         def round_wt(a, u):
             woven[("q", a, u)] = early_at(q_woven_at(a, u))([P, PIECE, PACK], BF16, "q_woven%d%d" % (a, u))
             weave_on_scalar(woven[("q", a, u)][:], wt_rows[(a, u)][:])
 
-        def quantize_tier(tier, a, u, make_tile):
+        def quantize_tier(tier, a, u, make_tile=sb):
             codes[(tier, a, u)] = make_tile([P, PIECE], U32, "%s_codes%d%d" % (tier, a, u))
             planes[(tier, a, u)] = sb([P, PIECE], U8, "%s_plane%d%d" % (tier, a, u))
             quantize(codes[(tier, a, u)][:], planes[(tier, a, u)][:], woven[(tier, a, u)][:])
@@ -218,10 +220,13 @@ def tile_list_tiert_gelu_kernel(
                 planes[(tier, a, m // 2)][:, within_piece(m)],
             )
 
+        def back_bank(a, m):
+            return TILES * (m // 2) + 2 * a + m % 2
+
         back = {}
 
-        def bring_back(a, m, index):
-            back[(a, m)] = bank(index, [P, PACK, P], "back%d%d" % (a, m))
+        def bring_back(a, m):
+            back[(a, m)] = bank(back_bank(a, m), [P, PACK, P], "back%d%d" % (a, m))
             q_codes, q_plane = tier_tile("q", a, m)
             for t in range(PACK):
                 nc.tensor.matmul_mx(
@@ -282,21 +287,22 @@ def tile_list_tiert_gelu_kernel(
         x_codes = {}
         x_plane = {}
 
-        def round_x(h, a, u, weave, offset):
+        def round_x(h, a, u, weave, make_tile=None):
             if (h, a) not in x_woven:
-                x_woven[(h, a)] = late_at(offset)([P, HALF, PACK], BF16, "x_woven%d%d" % (h, a))
+                make_tile = make_tile or late_at(X_WOVEN_AT + 4 * KIB * (PASSES * h + a))
+                x_woven[(h, a)] = make_tile([P, HALF, PACK], BF16, "x_woven%d%d" % (h, a))
             weave(x_woven[(h, a)][:, piece(u), :], x_rows[(h, a, u)][:])
 
-        def quantize_x(h, a, make_tile):
+        def quantize_x(h, a, make_tile=sb):
             x_codes[(h, a)] = make_tile([P, HALF], U32, "x_codes%d%d" % (h, a))
-            x_plane[(h, a)] = moving_plane(HALF, "x_plane%d%d" % (h, a), PASSES * (1 + h) + a)
+            x_plane[(h, a)] = moving_plane(HALF, "x_plane%d%d" % (h, a), PASSES * h + a)
             quantize(x_codes[(h, a)][:], x_plane[(h, a)][:], x_woven[(h, a)][:])
 
         acc = {}
         first_pass = {}
         last_pass = {}
 
-        def open_sum(h, m, index, columns, first=("q", 0), last=("x", 1)):
+        def open_sum(h, m, index, columns=whole, first=("q", 0), last=("x", 1)):
             acc[(h, m)] = (bank(index, [P, columns.stop - columns.start], "acc%d%d_%d" % (h, m, columns.start)), columns)
             first_pass[(h, m)] = first
             last_pass[(h, m)] = last
@@ -343,89 +349,84 @@ def tile_list_tiert_gelu_kernel(
                 out=out[P * m : P * (m + 1), HALF * h + columns.start : HALF * h + columns.stop], in_=result
             )
 
-        for a in range(PASSES):
-            for u in range(2):
+        for u in range(2):
+            for a in range(PASSES):
                 round_wt(a, u)
         for h, a in ((0, 0), (0, 1), (1, 0)):
             for u in range(2):
-                round_x(h, a, u, weave_on_scalar, X_WOVEN_AT + 4 * KIB * (PASSES * h + a))
+                round_x(h, a, u, weave_on_scalar)
 
-        for u in range(2):
-            quantize_tier("q", 0, u, early_at(EYE_AT + KIB * u))
-        for m in range(TILES):
-            bring_back(0, m, m)
+        for a in range(PASSES):
+            quantize_tier("q", a, 0, early_at(EYE_AT + KIB * a))
+            for m in range(2):
+                bring_back(a, m)
+        for a in range(PASSES):
+            for m in range(2):
+                left_over(a, m)
+                if a == 1:
+                    keep_warm(back_bank(a, m), *tier_tile("q", a, m))
+        quantize_tier("r", 0, 0)
         for m in range(2):
-            left_over(0, m)
-        quantize_tier("q", 1, 0, early_at(q_woven_at(0, 1)))
-        for m in range(2):
-            bring_back(1, m, TILES + m)
-        for m in range(2, TILES):
-            left_over(0, m)
-            keep_warm(m, *tier_tile("q", 0, m))
-        quantize_tier("r", 0, 0, early_at(WT_AT))
-        keep_warm(6, *tier_tile("r", 0, 0))
-        left_over(1, 0, early_at(WT_AT + 8 * KIB))
-        for m in range(2):
-            keep_warm(4, *tier_tile("q", 1, m))
+            keep_warm(TILES + m, *tier_tile("r", 0, m))
 
-        for m in range(TILES):
-            open_sum(0, m, m, whole)
-
-        def first_passes(u):
+        def pair_passes(h, u, a, columns=None):
             for tier in ("q", "r"):
-                for m in range(TILES):
-                    table_pass(0, m, tier, 0, piece(u))
+                for m in range(2 * u, 2 * u + 2):
+                    table_pass(h, m, tier, a, columns)
+
+        for h in range(2):
+            for m in range(2):
+                open_sum(h, m, 2 * h + m)
+        for quarter in range(2):
+            pick_words(piece(quarter), r_woven_at(0, 0) + KIB * quarter)
+        for a in range(PASSES):
+            part_words(piece(0), a)
+        pair_passes(0, 0, 0, piece(0))
+        part_words(piece(1), 0)
+        pair_passes(0, 0, 0, piece(1))
+        quantize_tier("r", 1, 0, early_at(r_woven_at(0, 0) - KIB // 2))
+        part_words(piece(1), 1)
+        pair_passes(0, 0, 1)
 
         second_half = slice(HALF, J)
-        pick_words(piece(0), r_woven_at(0, 0))
-        quantize_tier("r", 0, 1, early_at(r_woven_at(0, 0) + KIB))
-        part_words(piece(0), 0)
-        first_passes(0)
-        pick_words(piece(1), r_woven_at(0, 1))
-        part_words(piece(0), 1)
-        part_words(piece(1), 0)
-        first_passes(1)
-
-        quantize_tier("q", 1, 1, early_at(r_woven_at(0, 0)))
-        for m in range(2, TILES):
-            bring_back(1, m, TILES + m)
-        part_words(piece(1), 1)
-        left_over(1, 1)
-        for m in range(TILES):
-            table_pass(0, m, "q", 1)
-        pick_words(second_half, q_woven_at(1, 1) + KIB // 2)
-        quantize_tier("r", 1, 0, early_at(q_woven_at(1, 1) - KIB // 2))
-        for m in range(2):
-            table_pass(0, m, "r", 1)
-        quantize_x(0, 0, sb)
         for a in range(PASSES):
-            part_words(second_half, a, late_at(X_WOVEN_AT + (2 + a) * KIB))
+            quantize_tier("q", a, 1, early_at(EYE_AT + 2 * KIB if a == 0 else q_woven_at(0, 1) - 768))
+            for m in range(2, TILES):
+                bring_back(a, m)
+            if a == 0:
+                pick_words(second_half, q_woven_at(0, 1) + 256)
+        for a in range(PASSES):
+            part_words(second_half, a, early_at(q_woven_at(1, 1) - 768 + KIB * a))
+            pair_passes(1, 0, a)
+
         for m in range(2, TILES):
-            left_over(1, m, late_at(X_WOVEN_AT))
-        bias = late_at(LAST_WT_AT)([P, BLOCK], F32, "bias")
+            left_over(0, m, early_at(q_woven_at(1, 1) + 1536))
+            open_sum(0, m, back_bank(0, m))
+        left_over(1, 2)
+        quantize_tier("r", 0, 1)
+        left_over(1, 3)
+        for tier, a in (("q", 0), ("q", 1), ("r", 0)):
+            for m in range(2, TILES):
+                table_pass(0, m, tier, a)
+        quantize_x(0, 0, early_at(q_woven_at(1, 1) + 1536))
+        bias = late_at(LATE_WT_AT + 4 * KIB)([P, BLOCK], F32, "bias")
         nc.vector.transpose(out=bias[:], in_=bias_runs[:])
-        quantize_x(0, 1, sb)
+        quantize_x(0, 1, late_at(LATE_WT_AT + 5 * KIB))
         quantize_tier("r", 1, 1, late_at(X_WOVEN_AT + 4 * KIB))
-        round_x(1, 1, 0, weave_on_vector, X_WOVEN_AT + 12 * KIB)
-        quantize_x(1, 0, sb)
-        round_x(1, 1, 1, weave_on_vector, X_WOVEN_AT + 12 * KIB)
+        round_x(1, 1, 0, weave_on_vector, early_at(r_woven_at(1, 1)))
+        quantize_x(1, 0)
+        round_x(1, 1, 1, weave_on_vector)
         quantize_x(1, 1, late_at(X_WOVEN_AT + 8 * KIB))
 
         for m in range(TILES):
             token_pass(0, m, 0)
-        for m in range(2):
-            open_sum(1, m, TILES + m, whole)
-        for a in range(PASSES):
-            for m in range(2):
-                for tier in ("q", "r"):
-                    table_pass(1, m, tier, a)
         for m in range(TILES):
             if m >= 2:
                 table_pass(0, m, "r", 1)
             token_pass(0, m, 1)
             finish(0, m)
 
-        open_sum(1, 2, 6, whole, ("r", 1))
+        open_sum(1, 2, back_bank(1, 2), whole, ("r", 1))
         for tier, a in (("r", 1), ("q", 1), ("r", 0), ("q", 0)):
             table_pass(1, 2, tier, a)
         for m in range(3):
@@ -433,7 +434,7 @@ def tile_list_tiert_gelu_kernel(
         for m in range(3):
             token_pass(1, m, 1)
             finish(1, m)
-        for columns, index in ((slice(0, 256), 7), (slice(256, 384), 0), (slice(384, 512), 1)):
+        for columns, index in ((slice(0, 256), back_bank(1, 3)), (slice(256, 384), 0), (slice(384, 512), 1)):
             open_sum(1, 3, index, columns, ("x", 1), ("r", 1))
             for a in reversed(range(PASSES)):
                 token_pass(1, 3, a)

@@ -33,8 +33,9 @@ WINDOW_AT = 0
 WT_AT = WINDOW_AT + 16 * KIB
 Q_WOVEN_AT = WT_AT + 8 * KIB
 R_WOVEN_AT = Q_WOVEN_AT + 17 * KIB
-EYE_AT = R_WOVEN_AT + 10 * KIB
-PLANES_AT = EYE_AT + 5 * KIB + 128
+EYE_AT = R_WOVEN_AT + 12 * KIB
+PICKED_SCALES_AT = EYE_AT + 3 * KIB + 256
+PLANES_AT = EYE_AT + 7 * KIB + 128
 LATE_WT_AT = 0
 BIAS_RUNS_AT = LATE_WT_AT + 8 * KIB
 WX_AT = BIAS_RUNS_AT + KIB
@@ -137,7 +138,7 @@ def tile_list_tiert_gelu_kernel(
             eye_codes = sb([P, K_PASS], U32, "eye_codes")
             eye_plane = sb([P, K_PASS], U8, "eye_plane")
             nc.vector.quantize_mx(out=eye_codes[:].bitcast(FP8X4), scales=eye_plane[:], in_=eye_woven[:, : PACK * K_PASS])
-            picked_scales = early_at(EYE_AT + 2 * KIB)([P, J], U8, "picked_scales")
+            picked_scales = early_at(PICKED_SCALES_AT)([P, J], U8, "picked_scales")
             nc.vector.tensor_copy(out=picked_scales[:], in_=scale_window[:].indirect(offsets[:]))
 
         late = ctx.enter_context(tc.tile_pool(name="late", bufs=1, side="right"))
@@ -357,7 +358,7 @@ def tile_list_tiert_gelu_kernel(
                 round_x(h, a, u, weave_on_scalar)
 
         for a in range(PASSES):
-            quantize_tier("q", a, 0, early_at(EYE_AT + KIB * a))
+            quantize_tier("q", a, 0, early_at(EYE_AT - 768 + KIB * a))
             for m in range(2):
                 bring_back(a, m)
         for a in range(PASSES):
@@ -366,8 +367,10 @@ def tile_list_tiert_gelu_kernel(
                 if a == 1:
                     keep_warm(back_bank(a, m), *tier_tile("q", a, m))
         quantize_tier("r", 0, 0)
+        keep_warm(TILES, *tier_tile("r", 0, 0))
+        quantize_tier("r", 1, 0)
         for m in range(2):
-            keep_warm(TILES + m, *tier_tile("r", 0, m))
+            keep_warm(TILES + 1 + m, *tier_tile("r", 1, m))
 
         def pair_passes(h, u, a, columns=None):
             for tier in ("q", "r"):
@@ -378,29 +381,26 @@ def tile_list_tiert_gelu_kernel(
             for m in range(2):
                 open_sum(h, m, 2 * h + m)
         for quarter in range(2):
-            pick_words(piece(quarter), r_woven_at(0, 0) + KIB * quarter)
-        for a in range(PASSES):
-            part_words(piece(0), a)
-        pair_passes(0, 0, 0, piece(0))
-        part_words(piece(1), 0)
-        pair_passes(0, 0, 0, piece(1))
-        quantize_tier("r", 1, 0, early_at(r_woven_at(0, 0) - KIB // 2))
-        part_words(piece(1), 1)
+            pick_words(piece(quarter), r_woven_at(quarter, 0))
+        for quarter in range(2):
+            for a in range(PASSES):
+                part_words(piece(quarter), a)
+            pair_passes(0, 0, 0, piece(quarter))
         pair_passes(0, 0, 1)
 
         second_half = slice(HALF, J)
+        pick_words(second_half, r_woven_at(0, 0))
+        codes_at = (PICKED_SCALES_AT - 768, q_woven_at(0, 1))
+        parted_at = (PICKED_SCALES_AT + 256, q_woven_at(0, 1) + KIB)
         for a in range(PASSES):
-            quantize_tier("q", a, 1, early_at(EYE_AT + 2 * KIB if a == 0 else q_woven_at(0, 1) - 768))
+            quantize_tier("q", a, 1, early_at(codes_at[a]))
             for m in range(2, TILES):
                 bring_back(a, m)
-            if a == 0:
-                pick_words(second_half, q_woven_at(0, 1) + 256)
-        for a in range(PASSES):
-            part_words(second_half, a, early_at(q_woven_at(1, 1) - 768 + KIB * a))
+            part_words(second_half, a, early_at(parted_at[a]))
             pair_passes(1, 0, a)
 
         for m in range(2, TILES):
-            left_over(0, m, early_at(q_woven_at(1, 1) + 1536))
+            left_over(0, m, early_at(q_woven_at(1, 1)))
             open_sum(0, m, back_bank(0, m))
         left_over(1, 2)
         quantize_tier("r", 0, 1)
@@ -408,7 +408,7 @@ def tile_list_tiert_gelu_kernel(
         for tier, a in (("q", 0), ("q", 1), ("r", 0)):
             for m in range(2, TILES):
                 table_pass(0, m, tier, a)
-        quantize_x(0, 0, early_at(q_woven_at(1, 1) + 1536))
+        quantize_x(0, 0, early_at(q_woven_at(1, 1)))
         bias = late_at(LATE_WT_AT + 4 * KIB)([P, BLOCK], F32, "bias")
         nc.vector.transpose(out=bias[:], in_=bias_runs[:])
         quantize_x(0, 1, late_at(LATE_WT_AT + 5 * KIB))

@@ -162,7 +162,7 @@ def tile_list_tiert_gelu_kernel(
 
         def x_rows_at(h, a, u):
             index = 4 * h + 2 * a + u
-            return X_ROWS_AT + 4 * KIB * index + 2 * KIB * min(2, max(0, index - 4))
+            return X_ROWS_AT + 4 * KIB * index + 2 * KIB * min(2, max(0, index - 3))
 
         def load_x(h, a, u):
             x_rows[(h, a, u)] = late_at(x_rows_at(h, a, u))([P, PACK, PIECE], F32, "x_rows%d%d%d" % (h, a, u))
@@ -340,7 +340,7 @@ def tile_list_tiert_gelu_kernel(
             total, columns = acc[(h, m)]
             if h == 0:
                 if m // 2 not in first_results:
-                    make_tile = late_at(x_rows_at(1, 0, 1) - 2 * KIB + 4 * KIB * (m // 2))
+                    make_tile = late_at(x_rows_at(1, 0, 0) - 2 * KIB + 4 * KIB * (m // 2))
                     first_results[m // 2] = make_tile([P, 2 * HALF], F32, "first_results%d" % (m // 2))
                 result = first_results[m // 2][:, HALF * (m % 2) : HALF * (m % 2 + 1)]
             else:
@@ -353,9 +353,8 @@ def tile_list_tiert_gelu_kernel(
         for u in range(2):
             for a in range(PASSES):
                 round_wt(a, u)
-        for h, a in ((0, 0), (0, 1), (1, 0)):
-            for u in range(2):
-                round_x(h, a, u, weave_on_scalar)
+        for h, a, u in ((0, 0, 0), (0, 0, 1), (0, 1, 0), (0, 1, 1), (1, 0, 0)):
+            round_x(h, a, u, weave_on_scalar)
 
         for a in range(PASSES):
             quantize_tier("q", a, 0, early_at(EYE_AT - 768 + KIB * a))
@@ -413,6 +412,7 @@ def tile_list_tiert_gelu_kernel(
         nc.vector.transpose(out=bias[:], in_=bias_runs[:])
         quantize_x(0, 1, late_at(LATE_WT_AT + 5 * KIB))
         quantize_tier("r", 1, 1, late_at(X_WOVEN_AT + 4 * KIB))
+        round_x(1, 0, 1, weave_on_vector)
         round_x(1, 1, 0, weave_on_vector, early_at(r_woven_at(1, 1)))
         quantize_x(1, 0)
         round_x(1, 1, 1, weave_on_vector)

@@ -161,7 +161,7 @@ def tile_list_tiert_gelu_kernel(
         x_rows = {}
 
         def x_rows_at(h, a, u):
-            index = 4 * h + 2 * a + u
+            index = 2 * a + u if h == 0 else 4 + 2 * u + a
             return X_ROWS_AT + 4 * KIB * index + 2 * KIB * min(2, max(0, index - 3))
 
         def load_x(h, a, u):
@@ -192,8 +192,8 @@ def tile_list_tiert_gelu_kernel(
         bias_runs = late_at(BIAS_RUNS_AT)([P, BLOCK], F32, "bias_runs")
         nc.vector.memset(bias_runs[:], 0.0)
         nc.sync.dma_start(out=bias_runs[0:P:8, :], in_=b.rearrange("(m g c) -> g m c", m=TILES, g=QUADRANTS))
-        for a in range(PASSES):
-            for u in range(2):
+        for u in range(2):
+            for a in range(PASSES):
                 load_x(1, a, u)
 
         codes = {}
@@ -289,27 +289,39 @@ def tile_list_tiert_gelu_kernel(
         x_plane = {}
 
         def round_x(h, a, u, weave, make_tile=None):
-            if (h, a) not in x_woven:
-                make_tile = make_tile or late_at(X_WOVEN_AT + 4 * KIB * (PASSES * h + a))
-                x_woven[(h, a)] = make_tile([P, HALF, PACK], BF16, "x_woven%d%d" % (h, a))
-            weave(x_woven[(h, a)][:, piece(u), :], x_rows[(h, a, u)][:])
+            if make_tile:
+                x_woven[(h, a, u)] = make_tile([P, PIECE, PACK], BF16, "x_woven%d%d%d" % (h, a, u))[:]
+            else:
+                if (h, a) not in x_woven:
+                    offset = X_WOVEN_AT + 4 * KIB * (PASSES * h + a)
+                    x_woven[(h, a)] = late_at(offset)([P, HALF, PACK], BF16, "x_woven%d%d" % (h, a))
+                x_woven[(h, a, u)] = x_woven[(h, a)][:, piece(u), :]
+            weave(x_woven[(h, a, u)], x_rows[(h, a, u)][:])
 
-        def quantize_x(h, a, make_tile=sb):
-            x_codes[(h, a)] = make_tile([P, HALF], U32, "x_codes%d%d" % (h, a))
-            x_plane[(h, a)] = moving_plane(HALF, "x_plane%d%d" % (h, a), PASSES * h + a)
-            quantize(x_codes[(h, a)][:], x_plane[(h, a)][:], x_woven[(h, a)][:])
+        def quantize_x(h, a, make_tile=sb, u=None):
+            if (h, a) not in x_codes:
+                x_codes[(h, a)] = make_tile([P, HALF], U32, "x_codes%d%d" % (h, a))
+                x_plane[(h, a)] = moving_plane(HALF, "x_plane%d%d" % (h, a), PASSES * h + a)
+            if u is None:
+                quantize(x_codes[(h, a)][:], x_plane[(h, a)][:], x_woven[(h, a)][:])
+            else:
+                quantize(x_codes[(h, a)][:, piece(u)], x_plane[(h, a)][:, piece(u)], x_woven[(h, a, u)])
 
         acc = {}
-        first_pass = {}
-        last_pass = {}
+        opens = set()
+        closes = set()
 
-        def open_sum(h, m, index, columns=whole, first=("q", 0), last=("x", 1)):
-            acc[(h, m)] = (bank(index, [P, columns.stop - columns.start], "acc%d%d_%d" % (h, m, columns.start)), columns)
-            first_pass[(h, m)] = first
-            last_pass[(h, m)] = last
+        def open_group(index, h, tiles, u=None, first=("q", 0), last=("x", 1)):
+            columns = whole if u is None else piece(u)
+            width = columns.stop - columns.start
+            total = bank(index, [P, len(tiles), width], "acc%d%d_%d" % (h, tiles[0], columns.start))
+            for place, m in enumerate(tiles):
+                acc[(h, m, u)] = (total[:, place, :], columns)
+            opens.add((h, tiles[0], u) + first)
+            closes.add((h, tiles[-1], u) + last)
 
-        def table_pass(h, m, tier, a, columns=None):
-            total, span = acc[(h, m)]
+        def table_pass(h, m, u, tier, a, columns=None):
+            total, span = acc[(h, m, u)]
             columns = columns or span
             weights, weights_plane = tier_tile(tier, a, m)
             nc.tensor.matmul_mx(
@@ -318,26 +330,26 @@ def tile_list_tiert_gelu_kernel(
                 lhsT_scale=weights_plane,
                 rhs=tab_codes[(h, a)][:, 2 * columns.start : 2 * columns.stop].bitcast(FP4X4),
                 rhs_scale=tab_plane[a][:, HALF * h + columns.start : HALF * h + columns.stop],
-                start=(tier, a) == first_pass[(h, m)] and columns.start == span.start,
-                stop=(tier, a) == last_pass[(h, m)],
+                start=(h, m, u, tier, a) in opens and columns.start == span.start,
+                stop=(h, m, u, tier, a) in closes,
             )
 
-        def token_pass(h, m, a):
-            total, columns = acc[(h, m)]
+        def token_pass(h, m, u, a):
+            total, columns = acc[(h, m, u)]
             nc.tensor.matmul_mx(
-                out=total[:],
+                out=total,
                 lhsT=wx_codes[:, a, 2 * P * m : 2 * P * (m + 1)].bitcast(FP4X4),
                 lhsT_scale=wx_plane[:, a, P * m : P * (m + 1)],
                 rhs=x_codes[(h, a)][:, columns].bitcast(FP8X4),
                 rhs_scale=x_plane[(h, a)][:, columns],
-                start=("x", a) == first_pass[(h, m)],
-                stop=("x", a) == last_pass[(h, m)],
+                start=(h, m, u, "x", a) in opens,
+                stop=(h, m, u, "x", a) in closes,
             )
 
         first_results = {}
 
-        def finish(h, m):
-            total, columns = acc[(h, m)]
+        def finish(h, m, u=None):
+            total, columns = acc[(h, m, u)]
             if h == 0:
                 if m // 2 not in first_results:
                     make_tile = late_at(x_rows_at(1, 0, 0) - 2 * KIB + 4 * KIB * (m // 2))
@@ -345,7 +357,7 @@ def tile_list_tiert_gelu_kernel(
                 result = first_results[m // 2][:, HALF * (m % 2) : HALF * (m % 2 + 1)]
             else:
                 result = sb([P, columns.stop - columns.start], F32, "result%d_%d" % (m, columns.start))[:]
-            nc.scalar.activation(out=result, in_=total[:], func=ACT.Gelu_apprx_tanh, bias=bias[:, 8 * m : 8 * m + 1])
+            nc.scalar.activation(out=result, in_=total, func=ACT.Gelu_apprx_tanh, bias=bias[:, 8 * m : 8 * m + 1])
             nc.sync.dma_start(
                 out=out[P * m : P * (m + 1), HALF * h + columns.start : HALF * h + columns.stop], in_=result
             )
@@ -371,21 +383,22 @@ def tile_list_tiert_gelu_kernel(
         for m in range(2):
             keep_warm(TILES + 1 + m, *tier_tile("r", 1, m))
 
-        def pair_passes(h, u, a, columns=None):
+        def first_pair_passes(h, u, a, columns=None):
             for tier in ("q", "r"):
-                for m in range(2 * u, 2 * u + 2):
-                    table_pass(h, m, tier, a, columns)
+                for m in range(2):
+                    table_pass(h, m, u, tier, a, columns)
 
-        for h in range(2):
-            for m in range(2):
-                open_sum(h, m, 2 * h + m)
+        for m in range(2):
+            open_group(m, 0, (m,))
+        for u in range(2):
+            open_group(2 + u, 1, (0, 1), u)
         for quarter in range(2):
             pick_words(piece(quarter), r_woven_at(quarter, 0))
         for quarter in range(2):
             for a in range(PASSES):
                 part_words(piece(quarter), a)
-            pair_passes(0, 0, 0, piece(quarter))
-        pair_passes(0, 0, 1)
+            first_pair_passes(0, None, 0, piece(quarter))
+        first_pair_passes(0, None, 1)
 
         second_half = slice(HALF, J)
         pick_words(second_half, r_woven_at(0, 0))
@@ -396,49 +409,68 @@ def tile_list_tiert_gelu_kernel(
             for m in range(2, TILES):
                 bring_back(a, m)
             part_words(second_half, a, early_at(parted_at[a]))
-            pair_passes(1, 0, a)
+            for u in range(2):
+                first_pair_passes(1, u, a)
 
         for m in range(2, TILES):
             left_over(0, m, early_at(q_woven_at(1, 1)))
-            open_sum(0, m, back_bank(0, m))
+            open_group(back_bank(0, m), 0, (m,))
         left_over(1, 2)
         quantize_tier("r", 0, 1)
         left_over(1, 3)
         for tier, a in (("q", 0), ("q", 1), ("r", 0)):
             for m in range(2, TILES):
-                table_pass(0, m, tier, a)
+                table_pass(0, m, None, tier, a)
         quantize_x(0, 0, early_at(q_woven_at(1, 1)))
         bias = late_at(LATE_WT_AT + 4 * KIB)([P, BLOCK], F32, "bias")
         nc.vector.transpose(out=bias[:], in_=bias_runs[:])
         quantize_x(0, 1, late_at(LATE_WT_AT + 5 * KIB))
         quantize_tier("r", 1, 1, late_at(X_WOVEN_AT + 4 * KIB))
-        round_x(1, 0, 1, weave_on_vector)
-        round_x(1, 1, 0, weave_on_vector, early_at(r_woven_at(1, 1)))
-        quantize_x(1, 0)
-        round_x(1, 1, 1, weave_on_vector)
-        quantize_x(1, 1, late_at(X_WOVEN_AT + 8 * KIB))
+        behind_r11 = r_woven_at(1, 1)
+        round_x(1, 1, 0, weave_on_vector, early_at(behind_r11 + 256))
+        quantize_x(1, 0, early_at(behind_r11 - 1792), 0)
+        quantize_x(1, 1, sb, 0)
+        round_x(1, 0, 1, weave_on_vector, late_at(X_WOVEN_AT + 9 * KIB))
+        quantize_x(1, 0, u=1)
+        round_x(1, 1, 1, weave_on_vector, early_at(behind_r11 + 256))
+        quantize_x(1, 1, u=1)
 
         for m in range(TILES):
-            token_pass(0, m, 0)
+            token_pass(0, m, None, 0)
         for m in range(TILES):
             if m >= 2:
-                table_pass(0, m, "r", 1)
-            token_pass(0, m, 1)
+                table_pass(0, m, None, "r", 1)
+            token_pass(0, m, None, 1)
             finish(0, m)
 
-        open_sum(1, 2, back_bank(1, 2), whole, ("r", 1))
-        for tier, a in (("r", 1), ("q", 1), ("r", 0), ("q", 0)):
-            table_pass(1, 2, tier, a)
+        def four_table_passes(m, u):
+            for tier, a in (("r", 1), ("q", 1), ("r", 0), ("q", 0)):
+                table_pass(1, m, u, tier, a)
+
+        for a in range(PASSES):
+            for m in range(2):
+                token_pass(1, m, 0, a)
+        for m in range(2):
+            finish(1, m, 0)
+        open_group(back_bank(1, 2), 1, (2, 3), 0, ("x", 0))
+        for m in range(2, TILES):
+            token_pass(1, m, 0, 0)
+        for m in range(2, TILES):
+            four_table_passes(m, 0)
+        for m in range(2, TILES):
+            token_pass(1, m, 0, 1)
+        for m in range(2, TILES):
+            finish(1, m, 0)
+
+        open_group(back_bank(1, 3), 1, (2,), 1, ("r", 1))
+        four_table_passes(2, 1)
+        for a in range(PASSES):
+            for m in range(3):
+                token_pass(1, m, 1, a)
         for m in range(3):
-            token_pass(1, m, 0)
-        for m in range(3):
-            token_pass(1, m, 1)
-            finish(1, m)
-        for columns, index in ((slice(0, 256), back_bank(1, 3)), (slice(256, 384), 0), (slice(384, 512), 1)):
-            open_sum(1, 3, index, columns, ("x", 1), ("r", 1))
-            for a in reversed(range(PASSES)):
-                token_pass(1, 3, a)
-            for tier in ("q", "r"):
-                for a in range(PASSES):
-                    table_pass(1, 3, tier, a)
-            finish(1, 3)
+            finish(1, m, 1)
+        open_group(0, 1, (3,), 1, ("x", 1), ("q", 0))
+        for a in reversed(range(PASSES)):
+            token_pass(1, 3, 1, a)
+        four_table_passes(3, 1)
+        finish(1, 3, 1)

@@ -27,6 +27,7 @@ GROUP = 16
 SCALE_ROW0 = P - PASSES * GROUP
 BLOCK = 32
 EYE_RUN = K_PASS + 1
+EYE_PAD = 64
 KIB = 1024
 
 WINDOW_AT = 0
@@ -34,7 +35,7 @@ WT_AT = WINDOW_AT + 16 * KIB
 Q_WOVEN_AT = WT_AT + 8 * KIB
 R_WOVEN_AT = Q_WOVEN_AT + 17 * KIB
 EYE_AT = R_WOVEN_AT + 12 * KIB
-PICKED_SCALES_AT = EYE_AT + 3 * KIB + 256
+PICKED_SCALES_AT = EYE_AT + 1792
 PLANES_AT = EYE_AT + 7 * KIB + 128
 LATE_WT_AT = 0
 BIAS_RUNS_AT = LATE_WT_AT + 8 * KIB
@@ -127,19 +128,28 @@ def tile_list_tiert_gelu_kernel(
                 channel_multiplier=PACK // 2,
             )
             nc.vector.memset(scale_window[0:SCALE_ROW0, :].bitcast(I32), 0)
-            eye_woven = early_at(EYE_AT)([P, PACK * EYE_RUN], BF16, "eye_woven")
+            eye_words = sb([P, EYE_PAD + K_PASS], U32, "eye_words")
+            eye_codes = eye_words[:, EYE_PAD:]
+            eye_plane = sb([P, PIECE], U8, "eye_plane")
+            nc.vector.memset(eye_words[:, :EYE_PAD].bitcast(I32), 0)
+            eye_woven = early_at(EYE_AT)([P, 2 * EYE_RUN], BF16, "eye_woven")
             nc.vector.tensor_copy(
-                out=eye_woven[:].rearrange("p (t c) -> p t c", t=PACK),
+                out=eye_woven[:].rearrange("p (t c) -> p t c", t=2),
                 in_=eye_run[:]
                 .bitcast(BF16)[:, 1 : EYE_RUN + 1]
                 .rearrange("p (o c) -> p o c", o=1)
-                .to_broadcast([P, PACK, EYE_RUN]),
+                .to_broadcast([P, 2, EYE_RUN]),
             )
-            eye_codes = sb([P, K_PASS], U32, "eye_codes")
-            eye_plane = sb([P, K_PASS], U8, "eye_plane")
-            nc.vector.quantize_mx(out=eye_codes[:].bitcast(FP8X4), scales=eye_plane[:], in_=eye_woven[:, : PACK * K_PASS])
+            nc.vector.quantize_mx(
+                out=eye_codes[:, :PIECE].bitcast(FP8X4), scales=eye_plane[:], in_=eye_woven[:, : 2 * K_PASS]
+            )
             picked_scales = early_at(PICKED_SCALES_AT)([P, J], U8, "picked_scales")
             nc.vector.tensor_copy(out=picked_scales[:], in_=scale_window[:].indirect(offsets[:]))
+            eye_halves = eye_words[:].bitcast(U16)
+            first_half = 2 * EYE_PAD
+            nc.vector.tensor_copy(
+                out=eye_halves[:, first_half + K_PASS :], in_=eye_halves[:, first_half - 1 : first_half - 1 + K_PASS]
+            )
 
         late = ctx.enter_context(tc.tile_pool(name="late", bufs=1, side="right"))
 
@@ -211,9 +221,10 @@ def tile_list_tiert_gelu_kernel(
             weave_on_scalar(woven[("q", a, u)][:], wt_rows[(a, u)][:])
 
         def quantize_tier(tier, a, u, make_tile=sb):
-            codes[(tier, a, u)] = make_tile([P, PIECE], U32, "%s_codes%d%d" % (tier, a, u))
-            planes[(tier, a, u)] = sb([P, PIECE], U8, "%s_plane%d%d" % (tier, a, u))
-            quantize(codes[(tier, a, u)][:], planes[(tier, a, u)][:], woven[(tier, a, u)][:])
+            if (tier, a, u) not in codes:
+                codes[(tier, a, u)] = make_tile([P, PIECE], U32, "%s_codes%d%d" % (tier, a, u))[:]
+                planes[(tier, a, u)] = sb([P, PIECE], U8, "%s_plane%d%d" % (tier, a, u))[:]
+            quantize(codes[(tier, a, u)], planes[(tier, a, u)], woven[(tier, a, u)][:])
 
         def tier_tile(tier, a, m):
             return (
@@ -233,7 +244,7 @@ def tile_list_tiert_gelu_kernel(
                 nc.tensor.matmul_mx(
                     out=back[(a, m)][:, t, :],
                     lhsT=eye_codes[:, P * t : P * (t + 1)].bitcast(FP8X4),
-                    lhsT_scale=eye_plane[:, P * t : P * (t + 1)],
+                    lhsT_scale=eye_plane[:, within_piece(t)],
                     rhs=q_codes,
                     rhs_scale=q_plane,
                     start=True,
@@ -245,8 +256,8 @@ def tile_list_tiert_gelu_kernel(
                 out=bank(index, [P, HALF], "warm")[:],
                 lhsT=weights,
                 lhsT_scale=weights_plane,
-                rhs=eye_codes[:].bitcast(FP8X4),
-                rhs_scale=eye_plane[:],
+                rhs=first_codes[:].bitcast(FP8X4),
+                rhs_scale=first_plane[:],
                 start=True,
                 stop=True,
             )
@@ -311,8 +322,8 @@ def tile_list_tiert_gelu_kernel(
         opens = set()
         closes = set()
 
-        def open_group(index, h, tiles, u=None, first=("q", 0), last=("x", 1)):
-            columns = whole if u is None else piece(u)
+        def open_group(index, h, tiles, u=None, first=("q", 0), last=("x", 1), columns=None):
+            columns = columns or (whole if u is None else piece(u))
             width = columns.stop - columns.start
             total = bank(index, [P, len(tiles), width], "acc%d%d_%d" % (h, tiles[0], columns.start))
             for place, m in enumerate(tiles):
@@ -368,8 +379,12 @@ def tile_list_tiert_gelu_kernel(
         for h, a, u in ((0, 0, 0), (0, 0, 1), (0, 1, 0), (0, 1, 1), (1, 0, 0)):
             round_x(h, a, u, weave_on_scalar)
 
+        first_codes = early_at(EYE_AT - 768)([P, PASSES * PIECE], U32, "first_codes")
+        first_plane = sb([P, PASSES * PIECE], U8, "first_plane")
         for a in range(PASSES):
-            quantize_tier("q", a, 0, early_at(EYE_AT - 768 + KIB * a))
+            codes[("q", a, 0)] = first_codes[:, piece(a)]
+            planes[("q", a, 0)] = first_plane[:, piece(a)]
+            quantize_tier("q", a, 0)
             for m in range(2):
                 bring_back(a, m)
         for a in range(PASSES):
@@ -378,32 +393,36 @@ def tile_list_tiert_gelu_kernel(
                 if a == 1:
                     keep_warm(back_bank(a, m), *tier_tile("q", a, m))
         quantize_tier("r", 0, 0)
-        keep_warm(TILES, *tier_tile("r", 0, 0))
-        quantize_tier("r", 1, 0)
-        for m in range(2):
-            keep_warm(TILES + 1 + m, *tier_tile("r", 1, m))
+        for index in range(3):
+            keep_warm(TILES + index, *tier_tile("r", 0, 0))
 
-        def first_pair_passes(h, u, a, columns=None):
+        def first_pair_passes(h, u, a):
             for tier in ("q", "r"):
                 for m in range(2):
-                    table_pass(h, m, u, tier, a, columns)
+                    table_pass(h, m, u, tier, a)
 
         for m in range(2):
             open_group(m, 0, (m,))
         for u in range(2):
             open_group(2 + u, 1, (0, 1), u)
         for quarter in range(2):
-            pick_words(piece(quarter), r_woven_at(quarter, 0))
+            pick_words(piece(quarter), r_woven_at(0, 0) + KIB * quarter)
+        for a in range(PASSES):
+            part_words(piece(0), a)
+        part_words(piece(1), 0)
         for quarter in range(2):
-            for a in range(PASSES):
-                part_words(piece(quarter), a)
-            first_pair_passes(0, None, 0, piece(quarter))
+            for m in range(2):
+                table_pass(0, m, None, "q", 0, piece(quarter))
+        for m in range(2):
+            table_pass(0, m, None, "r", 0)
+        quantize_tier("r", 1, 0, early_at(r_woven_at(0, 0) - KIB // 2))
+        part_words(piece(1), 1)
         first_pair_passes(0, None, 1)
 
         second_half = slice(HALF, J)
-        pick_words(second_half, r_woven_at(0, 0))
-        codes_at = (PICKED_SCALES_AT - 768, q_woven_at(0, 1))
-        parted_at = (PICKED_SCALES_AT + 256, q_woven_at(0, 1) + KIB)
+        pick_words(second_half, r_woven_at(1, 0))
+        codes_at = (PICKED_SCALES_AT - 512, q_woven_at(0, 1))
+        parted_at = (PICKED_SCALES_AT + 512, q_woven_at(0, 1) + KIB)
         for a in range(PASSES):
             quantize_tier("q", a, 1, early_at(codes_at[a]))
             for m in range(2, TILES):
@@ -469,8 +488,10 @@ def tile_list_tiert_gelu_kernel(
                 token_pass(1, m, 1, a)
         for m in range(3):
             finish(1, m, 1)
-        open_group(0, 1, (3,), 1, ("x", 1), ("q", 0))
-        for a in reversed(range(PASSES)):
-            token_pass(1, 3, 1, a)
-        four_table_passes(3, 1)
-        finish(1, 3, 1)
+        for index in range(2):
+            first = PIECE + P * index
+            open_group(index, 1, (3,), 1, ("x", 1), ("q", 0), slice(first, first + P))
+            for a in reversed(range(PASSES)):
+                token_pass(1, 3, 1, a)
+            four_table_passes(3, 1)
+            finish(1, 3, 1)

@@ -187,18 +187,18 @@ def tile_list_tiert_gelu_kernel(
         for a in range(PASSES):
             load_wt(a, 1, late_at(LATE_WT_AT + 4 * KIB * a))
         spread_scales(1)
+        for u in range(2):
+            load_x(0, 0, u)
         wx_codes = late_at(WX_AT)([P, PASSES, 2 * N], U8, "wx_codes")
         nc.sync.dma_start(out=wx_codes[:].bitcast(I32), in_=wx_words.rearrange("a p b -> p a b").bitcast(I32))
         for u in range(2):
-            load_x(0, 0, u)
+            load_x(0, 1, u)
         wx_plane = late_at(WX_PLANE_AT)([P, PASSES, N], U8, "wx_plane")
         for q in range(QUADRANTS):
             nc.sync.dma_start(
                 out=wx_plane[32 * q : 32 * q + 4, :, :].bitcast(I32),
                 in_=wx_scales[:, 4 * q : 4 * q + 4, :].rearrange("a r n -> r a n").bitcast(I32),
             )
-        for u in range(2):
-            load_x(0, 1, u)
         bias_runs = late_at(BIAS_RUNS_AT)([P, BLOCK], F32, "bias_runs")
         nc.vector.memset(bias_runs[:], 0.0)
         nc.sync.dma_start(out=bias_runs[0:P:8, :], in_=b.rearrange("(m g c) -> g m c", m=TILES, g=QUADRANTS))
@@ -393,8 +393,10 @@ def tile_list_tiert_gelu_kernel(
                 if a == 1:
                     keep_warm(back_bank(a, m), *tier_tile("q", a, m))
         quantize_tier("r", 0, 0)
-        for index in range(3):
-            keep_warm(TILES + index, *tier_tile("r", 0, 0))
+        keep_warm(TILES, *tier_tile("r", 0, 0))
+        quantize_tier("r", 1, 0)
+        for m in range(2):
+            keep_warm(TILES + 1 + m, *tier_tile("r", 1, m))
 
         def first_pair_passes(h, u, a):
             for tier in ("q", "r"):
@@ -406,7 +408,7 @@ def tile_list_tiert_gelu_kernel(
         for u in range(2):
             open_group(2 + u, 1, (0, 1), u)
         for quarter in range(2):
-            pick_words(piece(quarter), r_woven_at(0, 0) + KIB * quarter)
+            pick_words(piece(quarter), r_woven_at(quarter, 0))
         for a in range(PASSES):
             part_words(piece(0), a)
         part_words(piece(1), 0)
@@ -415,12 +417,11 @@ def tile_list_tiert_gelu_kernel(
                 table_pass(0, m, None, "q", 0, piece(quarter))
         for m in range(2):
             table_pass(0, m, None, "r", 0)
-        quantize_tier("r", 1, 0, early_at(r_woven_at(0, 0) - KIB // 2))
         part_words(piece(1), 1)
         first_pair_passes(0, None, 1)
 
         second_half = slice(HALF, J)
-        pick_words(second_half, r_woven_at(1, 0))
+        pick_words(second_half, r_woven_at(0, 0))
         codes_at = (PICKED_SCALES_AT - 512, q_woven_at(0, 1))
         parted_at = (PICKED_SCALES_AT + 512, q_woven_at(0, 1) + KIB)
         for a in range(PASSES):

from contextlib import ExitStack

import concourse.mybir as mybir

K, L, N, T, J = 1024, 1024, 512, 4096, 1024

F32 = mybir.dt.float32
BF16 = mybir.dt.bfloat16
I32 = mybir.dt.int32
U32 = mybir.dt.uint32
U16 = mybir.dt.uint16
U8 = mybir.dt.uint8
FP8X4 = mybir.dt.float8_e4m3fn_x4
FP4X4 = mybir.dt.float4_e2m1fn_x4
ACT = mybir.ActivationFunctionType
ALU = mybir.AluOpType

P = 128
PACK = 4
K_PASS = P * PACK
PASSES = K // K_PASS
TILES = N // P
HALF = 512
PIECE = 256
QUADRANTS = 4
GROUP = 16
SCALE_ROW0 = P - PASSES * GROUP
BLOCK = 32
EYE_RUN = K_PASS + 1
EYE_PAD = 64
KIB = 1024

WINDOW_AT = 0
WT_AT = WINDOW_AT + 16 * KIB
Q_WOVEN_AT = WT_AT + 8 * KIB
R_WOVEN_AT = Q_WOVEN_AT + 17 * KIB
EYE_AT = R_WOVEN_AT + 12 * KIB
PICKED_SCALES_AT = EYE_AT + 1792
PLANES_AT = EYE_AT + 7 * KIB + 128
LATE_WT_AT = 0
BIAS_RUNS_AT = LATE_WT_AT + 8 * KIB
WX_AT = BIAS_RUNS_AT + KIB
WX_PLANE_AT = WX_AT + 2 * KIB
X_ROWS_AT = WX_PLANE_AT + KIB
X_WOVEN_AT = X_ROWS_AT + 36 * KIB
TAB_PLANES_AT = X_WOVEN_AT + 16 * KIB + 128

FLOPS = 2 * N * J * (2 * K + L) + 2 * K_PASS * K * N


def tile_list_tiert_gelu_kernel(
    tc, tab_words, tab_scales, wt, x, wx_words, wx_scales, b, offs, out
):
    nc = tc.nc
    with ExitStack() as ctx:
        lists = ctx.enter_context(tc.tile_pool(name="lists", bufs=1))
        keep = ctx.enter_context(tc.tile_pool(name="keep", bufs=1))
        early = ctx.enter_context(tc.tile_pool(name="early", bufs=1))
        psum = ctx.enter_context(tc.psum_pool(name="psum", bufs=1))

        def sb(shape, dtype, name):
            return keep.tile(shape, dtype, name=name, align_bytes=256)

        def early_at(offset):
            return lambda shape, dtype, name: early.tile(shape, dtype, name=name, align_bytes=256, offset=offset)

        def moving_plane(width, name, index):
            return early.tile([P, width], U8, name=name, align_bytes=128, offset=PLANES_AT + KIB * index)

        def bank(index, shape, name):
            return psum.tile(shape, F32, name=name, tag="bank%d" % index)

        def walk_woven(ap):
            return ap.rearrange("p (c i) t -> p c t i", i=2)

        def walk_rows(ap):
            return ap.rearrange("p t (c i) -> p c t i", i=2)

        def weave_on_scalar(woven_ap, rows):
            nc.scalar.activation(out=walk_woven(woven_ap), in_=walk_rows(rows), func=ACT.Copy)

        def weave_on_vector(woven_ap, rows):
            nc.vector.tensor_copy(out=walk_woven(woven_ap), in_=walk_rows(rows))

        def quantize(codes_ap, plane_ap, woven_ap):
            nc.vector.quantize_mx(out=codes_ap.bitcast(FP8X4), scales=plane_ap, in_=woven_ap.rearrange("p c t -> p (c t)"))

        def piece(u):
            return slice(PIECE * u, PIECE * (u + 1))

        def within_piece(m):
            return slice(P * (m % 2), P * (m % 2 + 1))

        offsets = lists.tile([P, J // GROUP], U16, name="offsets")
        wt_by_pass = wt.rearrange("(a p t) n -> a p t n", p=P, t=PACK)

        warm_in = sb([P, 1], F32, "warm_in")
        warm_out = sb([P, 1], F32, "warm_out")
        nc.vector.memset(warm_in[:], 0.0)
        nc.scalar.activation(out=warm_out[:], in_=warm_in[:], func=ACT.Gelu_apprx_tanh)

        with tc.tile_pool(name="scales", bufs=1, side="right") as scales:
            scale_window = scales.tile([P, T], U8, name="scale_window", align_bytes=256)
            nc.sync.dma_start(offsets[:], offs)
            nc.sync.dma_start(
                out=scale_window[SCALE_ROW0:P, :].bitcast(I32), in_=tab_scales.rearrange("a q t -> (a q) t").bitcast(I32)
            )
            wt_rows = {}

            def load_wt(a, u, make_tile):
                wt_rows[(a, u)] = make_tile([P, PACK, PIECE], F32, "wt_rows%d%d" % (a, u))
                nc.sync.dma_start(out=wt_rows[(a, u)][:], in_=wt_by_pass[a][:, :, piece(u)])

            for a in range(PASSES):
                load_wt(a, 0, early_at(WT_AT + 4 * KIB * a))
            word_window = early_at(WINDOW_AT)([P, T], I32, "word_window")
            nc.sync.dma_start(out=word_window[:], in_=tab_words[0].rearrange("p t b -> p (t b)").bitcast(I32))

            eye_run = sb([P, EYE_RUN // 2 + 2], F32, "eye_run")
            nc.gpsimd.memset(eye_run[:], 0.0)
            nc.gpsimd.affine_select(
                out=eye_run[:],
                in_=eye_run[:],
                compare_op=ALU.not_equal,
                fill=1.0,
                base=0,
                pattern=[[-1, EYE_RUN // 2 + 2]],
                channel_multiplier=PACK // 2,
            )
            nc.vector.memset(scale_window[0:SCALE_ROW0, :].bitcast(I32), 0)
            eye_words = sb([P, EYE_PAD + K_PASS], U32, "eye_words")
            eye_codes = eye_words[:, EYE_PAD:]
            eye_plane = sb([P, PIECE], U8, "eye_plane")
            nc.vector.memset(eye_words[:, :EYE_PAD].bitcast(I32), 0)
            eye_woven = early_at(EYE_AT)([P, 2 * EYE_RUN], BF16, "eye_woven")
            nc.vector.tensor_copy(
                out=eye_woven[:].rearrange("p (t c) -> p t c", t=2),
                in_=eye_run[:]
                .bitcast(BF16)[:, 1 : EYE_RUN + 1]
                .rearrange("p (o c) -> p o c", o=1)
                .to_broadcast([P, 2, EYE_RUN]),
            )
            nc.vector.quantize_mx(
                out=eye_codes[:, :PIECE].bitcast(FP8X4), scales=eye_plane[:], in_=eye_woven[:, : 2 * K_PASS]
            )
            picked_scales = early_at(PICKED_SCALES_AT)([P, J], U8, "picked_scales")
            nc.vector.tensor_copy(out=picked_scales[:], in_=scale_window[:].indirect(offsets[:]))
            eye_halves = eye_words[:].bitcast(U16)
            first_half = 2 * EYE_PAD
            nc.vector.tensor_copy(
                out=eye_halves[:, first_half + K_PASS :], in_=eye_halves[:, first_half - 1 : first_half - 1 + K_PASS]
            )

        late = ctx.enter_context(tc.tile_pool(name="late", bufs=1, side="right"))

        def late_at(offset):
            return lambda shape, dtype, name: late.tile(shape, dtype, name=name, align_bytes=256, offset=offset)

        tab_plane = [
            late.tile([P, J], U8, name="tab_plane%d" % a, align_bytes=128, offset=TAB_PLANES_AT + KIB * a)
            for a in range(PASSES)
        ]

        def spread_scales(a):
            for q in range(QUADRANTS):
                row = SCALE_ROW0 + GROUP * a + 4 * q
                nc.sync.dma_start(
                    out=tab_plane[a][32 * q : 32 * q + 4, :].bitcast(I32), in_=picked_scales[row : row + 4, :].bitcast(I32)
                )

        x_rows = {}

        def x_rows_at(h, a, u):
            index = 2 * a + u if h == 0 else 4 + 2 * u + a
            return X_ROWS_AT + 4 * KIB * index + 2 * KIB * min(2, max(0, index - 3))

        def load_x(h, a, u):
            x_rows[(h, a, u)] = late_at(x_rows_at(h, a, u))([P, PACK, PIECE], F32, "x_rows%d%d%d" % (h, a, u))
            j0 = HALF * h + PIECE * u
            nc.sync.dma_start(
                out=x_rows[(h, a, u)][:],
                in_=x[K_PASS * a : K_PASS * (a + 1), j0 : j0 + PIECE].rearrange("(p t) j -> p t j", t=PACK),
            )

        whole = slice(0, HALF)
        spread_scales(0)
        for a in range(PASSES):
            load_wt(a, 1, late_at(LATE_WT_AT + 4 * KIB * a))
        spread_scales(1)
        for u in range(2):
            load_x(0, 0, u)
        wx_codes = late_at(WX_AT)([P, PASSES, 2 * N], U8, "wx_codes")
        nc.sync.dma_start(out=wx_codes[:].bitcast(I32), in_=wx_words.rearrange("a p b -> p a b").bitcast(I32))
        for u in range(2):
            load_x(0, 1, u)
        wx_plane = late_at(WX_PLANE_AT)([P, PASSES, N], U8, "wx_plane")
        for q in range(QUADRANTS):
            nc.sync.dma_start(
                out=wx_plane[32 * q : 32 * q + 4, :, :].bitcast(I32),
                in_=wx_scales[:, 4 * q : 4 * q + 4, :].rearrange("a r n -> r a n").bitcast(I32),
            )
        bias_runs = late_at(BIAS_RUNS_AT)([P, BLOCK], F32, "bias_runs")
        nc.vector.memset(bias_runs[:], 0.0)
        nc.sync.dma_start(out=bias_runs[0:P:8, :], in_=b.rearrange("(m g c) -> g m c", m=TILES, g=QUADRANTS))
        for u in range(2):
            for a in range(PASSES):
                load_x(1, a, u)

        codes = {}
        planes = {}
        woven = {}

        def q_woven_at(a, u):
            return Q_WOVEN_AT + 4 * KIB * (2 * u + a)

        def r_woven_at(a, u):
            return R_WOVEN_AT + 2 * KIB * (2 * u + a)

        def round_wt(a, u):
            woven[("q", a, u)] = early_at(q_woven_at(a, u))([P, PIECE, PACK], BF16, "q_woven%d%d" % (a, u))
            weave_on_scalar(woven[("q", a, u)][:], wt_rows[(a, u)][:])

        def quantize_tier(tier, a, u, make_tile=sb):
            if (tier, a, u) not in codes:
                codes[(tier, a, u)] = make_tile([P, PIECE], U32, "%s_codes%d%d" % (tier, a, u))[:]
                planes[(tier, a, u)] = sb([P, PIECE], U8, "%s_plane%d%d" % (tier, a, u))[:]
            quantize(codes[(tier, a, u)], planes[(tier, a, u)], woven[(tier, a, u)][:])

        def tier_tile(tier, a, m):
            return (
                codes[(tier, a, m // 2)][:, within_piece(m)].bitcast(FP8X4),
                planes[(tier, a, m // 2)][:, within_piece(m)],
            )

        def back_bank(a, m):
            return TILES * (m // 2) + 2 * a + m % 2

        back = {}

        def bring_back(a, m):
            back[(a, m)] = bank(back_bank(a, m), [P, PACK, P], "back%d%d" % (a, m))
            q_codes, q_plane = tier_tile("q", a, m)
            for t in range(PACK):
                nc.tensor.matmul_mx(
                    out=back[(a, m)][:, t, :],
                    lhsT=eye_codes[:, P * t : P * (t + 1)].bitcast(FP8X4),
                    lhsT_scale=eye_plane[:, within_piece(t)],
                    rhs=q_codes,
                    rhs_scale=q_plane,
                    start=True,
                    stop=True,
                )

        def keep_warm(index, weights, weights_plane):
            nc.tensor.matmul_mx(
                out=bank(index, [P, HALF], "warm")[:],
                lhsT=weights,
                lhsT_scale=weights_plane,
                rhs=first_codes[:].bitcast(FP8X4),
                rhs_scale=first_plane[:],
                start=True,
                stop=True,
            )

        def left_over(a, m, make_tile=None):
            u = m // 2
            if ("r", a, u) not in woven:
                make_tile = make_tile or early_at(r_woven_at(a, u))
                woven[("r", a, u)] = make_tile([P, PIECE, PACK], BF16, "r_woven%d%d" % (a, u))
            nc.vector.tensor_tensor(
                out=walk_woven(woven[("r", a, u)][:, within_piece(m), :]),
                in0=walk_rows(wt_rows[(a, u)][:, :, within_piece(m)]),
                in1=walk_rows(back[(a, m)][:]),
                op=ALU.subtract,
            )

        picked_words = {}

        def pick_words(tokens, offset):
            tile = early_at(offset)([P, tokens.stop - tokens.start], U32, "picked_words%d" % tokens.start)
            picked_words[tokens.start] = tile
            nc.vector.tensor_copy(
                out=tile[:],
                in_=word_window[:].bitcast(U32).indirect(offsets[:, tokens.start // GROUP : tokens.stop // GROUP]),
            )

        tab_codes = {}

        def part_words(tokens, a, make_tile=sb):
            h, first = divmod(tokens.start, HALF)
            if (h, a) not in tab_codes:
                tab_codes[(h, a)] = make_tile([P, 2 * HALF], U8, "tab_codes%d%d" % (h, a))
            nc.vector.tensor_copy(
                out=tab_codes[(h, a)][:].bitcast(U16)[:, first : first + tokens.stop - tokens.start],
                in_=picked_words[tokens.start][:].bitcast(U16).rearrange("p (j a) -> p a j", a=PASSES)[:, a, :],
            )

        x_woven = {}
        x_codes = {}
        x_plane = {}

        def round_x(h, a, u, weave, make_tile=None):
            if make_tile:
                x_woven[(h, a, u)] = make_tile([P, PIECE, PACK], BF16, "x_woven%d%d%d" % (h, a, u))[:]
            else:
                if (h, a) not in x_woven:
                    offset = X_WOVEN_AT + 4 * KIB * (PASSES * h + a)
                    x_woven[(h, a)] = late_at(offset)([P, HALF, PACK], BF16, "x_woven%d%d" % (h, a))
                x_woven[(h, a, u)] = x_woven[(h, a)][:, piece(u), :]
            weave(x_woven[(h, a, u)], x_rows[(h, a, u)][:])

        def quantize_x(h, a, make_tile=sb, u=None):
            if (h, a) not in x_codes:
                x_codes[(h, a)] = make_tile([P, HALF], U32, "x_codes%d%d" % (h, a))
                x_plane[(h, a)] = moving_plane(HALF, "x_plane%d%d" % (h, a), PASSES * h + a)
            if u is None:
                quantize(x_codes[(h, a)][:], x_plane[(h, a)][:], x_woven[(h, a)][:])
            else:
                quantize(x_codes[(h, a)][:, piece(u)], x_plane[(h, a)][:, piece(u)], x_woven[(h, a, u)])

        acc = {}
        opens = set()
        closes = set()

        def open_group(index, h, tiles, u=None, first=("q", 0), last=("x", 1), columns=None):
            columns = columns or (whole if u is None else piece(u))
            width = columns.stop - columns.start
            total = bank(index, [P, len(tiles), width], "acc%d%d_%d" % (h, tiles[0], columns.start))
            for place, m in enumerate(tiles):
                acc[(h, m, u)] = (total[:, place, :], columns)
            opens.add((h, tiles[0], u) + first)
            closes.add((h, tiles[-1], u) + last)

        def table_pass(h, m, u, tier, a, columns=None):
            total, span = acc[(h, m, u)]
            columns = columns or span
            weights, weights_plane = tier_tile(tier, a, m)
            nc.tensor.matmul_mx(
                out=total[:, columns.start - span.start : columns.stop - span.start],
                lhsT=weights,
                lhsT_scale=weights_plane,
                rhs=tab_codes[(h, a)][:, 2 * columns.start : 2 * columns.stop].bitcast(FP4X4),
                rhs_scale=tab_plane[a][:, HALF * h + columns.start : HALF * h + columns.stop],
                start=(h, m, u, tier, a) in opens and columns.start == span.start,
                stop=(h, m, u, tier, a) in closes,
            )

        def token_pass(h, m, u, a):
            total, columns = acc[(h, m, u)]
            nc.tensor.matmul_mx(
                out=total,
                lhsT=wx_codes[:, a, 2 * P * m : 2 * P * (m + 1)].bitcast(FP4X4),
                lhsT_scale=wx_plane[:, a, P * m : P * (m + 1)],
                rhs=x_codes[(h, a)][:, columns].bitcast(FP8X4),
                rhs_scale=x_plane[(h, a)][:, columns],
                start=(h, m, u, "x", a) in opens,
                stop=(h, m, u, "x", a) in closes,
            )

        first_results = {}

        def finish(h, m, u=None):
            total, columns = acc[(h, m, u)]
            if h == 0:
                if m // 2 not in first_results:
                    make_tile = late_at(x_rows_at(1, 0, 0) - 2 * KIB + 4 * KIB * (m // 2))
                    first_results[m // 2] = make_tile([P, 2 * HALF], F32, "first_results%d" % (m // 2))
                result = first_results[m // 2][:, HALF * (m % 2) : HALF * (m % 2 + 1)]
            else:
                result = sb([P, columns.stop - columns.start], F32, "result%d_%d" % (m, columns.start))[:]
            nc.scalar.activation(out=result, in_=total, func=ACT.Gelu_apprx_tanh, bias=bias[:, 8 * m : 8 * m + 1])
            nc.sync.dma_start(
                out=out[P * m : P * (m + 1), HALF * h + columns.start : HALF * h + columns.stop], in_=result
            )

        for u in range(2):
            for a in range(PASSES):
                round_wt(a, u)
        for h, a, u in ((0, 0, 0), (0, 0, 1), (0, 1, 0), (0, 1, 1), (1, 0, 0)):
            round_x(h, a, u, weave_on_scalar)

        first_codes = early_at(EYE_AT - 768)([P, PASSES * PIECE], U32, "first_codes")
        first_plane = sb([P, PASSES * PIECE], U8, "first_plane")
        for a in range(PASSES):
            codes[("q", a, 0)] = first_codes[:, piece(a)]
            planes[("q", a, 0)] = first_plane[:, piece(a)]
            quantize_tier("q", a, 0)
            for m in range(2):
                bring_back(a, m)
        for a in range(PASSES):
            for m in range(2):
                left_over(a, m)
                if a == 1:
                    keep_warm(back_bank(a, m), *tier_tile("q", a, m))
        quantize_tier("r", 0, 0)
        keep_warm(TILES, *tier_tile("r", 0, 0))
        quantize_tier("r", 1, 0)
        for m in range(2):
            keep_warm(TILES + 1 + m, *tier_tile("r", 1, m))

        def first_pair_passes(h, u, a):
            for tier in ("q", "r"):
                for m in range(2):
                    table_pass(h, m, u, tier, a)

        for m in range(2):
            open_group(m, 0, (m,))
        for u in range(2):
            open_group(2 + u, 1, (0, 1), u)
        for quarter in range(2):
            pick_words(piece(quarter), r_woven_at(quarter, 0))
        for a in range(PASSES):
            part_words(piece(0), a)
        part_words(piece(1), 0)
        for quarter in range(2):
            for m in range(2):
                table_pass(0, m, None, "q", 0, piece(quarter))
        for m in range(2):
            table_pass(0, m, None, "r", 0)
        part_words(piece(1), 1)
        first_pair_passes(0, None, 1)

        second_half = slice(HALF, J)
        pick_words(second_half, r_woven_at(0, 0))
        codes_at = (PICKED_SCALES_AT - 512, q_woven_at(0, 1))
        parted_at = (PICKED_SCALES_AT + 512, q_woven_at(0, 1) + KIB)
        for a in range(PASSES):
            quantize_tier("q", a, 1, early_at(codes_at[a]))
            for m in range(2, TILES):
                bring_back(a, m)
            part_words(second_half, a, early_at(parted_at[a]))
            for u in range(2):
                first_pair_passes(1, u, a)

        for m in range(2, TILES):
            left_over(0, m, early_at(q_woven_at(1, 1)))
            open_group(back_bank(0, m), 0, (m,))
        left_over(1, 2)
        quantize_tier("r", 0, 1)
        left_over(1, 3)
        for tier, a in (("q", 0), ("q", 1), ("r", 0)):
            for m in range(2, TILES):
                table_pass(0, m, None, tier, a)
        quantize_x(0, 0, early_at(q_woven_at(1, 1)))
        bias = late_at(LATE_WT_AT + 4 * KIB)([P, BLOCK], F32, "bias")
        nc.vector.transpose(out=bias[:], in_=bias_runs[:])
        quantize_x(0, 1, late_at(LATE_WT_AT + 5 * KIB))
        quantize_tier("r", 1, 1, late_at(X_WOVEN_AT + 4 * KIB))
        behind_r11 = r_woven_at(1, 1)
        round_x(1, 1, 0, weave_on_vector, early_at(behind_r11 + 256))
        quantize_x(1, 0, early_at(behind_r11 - 1792), 0)
        quantize_x(1, 1, sb, 0)
        round_x(1, 0, 1, weave_on_vector, late_at(X_WOVEN_AT + 9 * KIB))
        quantize_x(1, 0, u=1)
        round_x(1, 1, 1, weave_on_vector, early_at(behind_r11 + 256))
        quantize_x(1, 1, u=1)

        for m in range(TILES):
            token_pass(0, m, None, 0)
        for m in range(TILES):
            if m >= 2:
                table_pass(0, m, None, "r", 1)
            token_pass(0, m, None, 1)
            finish(0, m)

        def four_table_passes(m, u):
            for tier, a in (("r", 1), ("q", 1), ("r", 0), ("q", 0)):
                table_pass(1, m, u, tier, a)

        for a in range(PASSES):
            for m in range(2):
                token_pass(1, m, 0, a)
        for m in range(2):
            finish(1, m, 0)
        open_group(back_bank(1, 2), 1, (2, 3), 0, ("x", 0))
        for m in range(2, TILES):
            token_pass(1, m, 0, 0)
        for m in range(2, TILES):
            four_table_passes(m, 0)
        for m in range(2, TILES):
            token_pass(1, m, 0, 1)
        for m in range(2, TILES):
            finish(1, m, 0)

        open_group(back_bank(1, 3), 1, (2,), 1, ("r", 1))
        four_table_passes(2, 1)
        for a in range(PASSES):
            for m in range(3):
                token_pass(1, m, 1, a)
        for m in range(3):
            finish(1, m, 1)
        for index in range(2):
            first = PIECE + P * index
            open_group(index, 1, (3,), 1, ("x", 1), ("q", 0), slice(first, first + P))
            for a in reversed(range(PASSES)):
                token_pass(1, 3, 1, a)
            four_table_passes(3, 1)
            finish(1, 3, 1)
